import numpy as np
import ml_dtypes


def mxq(x, axis, fmt="e4m3"):
    dtype, down = {"e4m3": (ml_dtypes.float8_e4m3fn, 7), "e5m2": (ml_dtypes.float8_e5m2, 14)}[fmt]
    v = np.moveaxis(np.asarray(x, np.float32).astype(ml_dtypes.bfloat16).astype(np.float64), axis, -1)
    blocks = v.reshape(v.shape[:-1] + (-1, 32))
    amax = np.abs(blocks).max(-1, keepdims=True)
    byte = np.maximum(np.where(amax > 0, np.frexp(amax)[1] - 1 + 127, 0) - down, 1)
    scale = np.exp2(byte - 127.0)
    codes = (blocks / scale).astype(np.float32).astype(dtype).astype(np.float64)
    return np.moveaxis((codes * scale).reshape(v.shape), -1, axis)


WIDE = False


def mx_kscale(k):
    if not WIDE:
        return np.ones(k)
    levels = np.array([10, -10, 5, -5, 0])
    if k % 512:
        return np.exp2(np.random.permutation(np.resize(levels, k // 32))).repeat(32)
    a = np.empty((k // 512, 16))
    for p in range(k // 512):
        a[p, :8] = np.random.permutation(np.resize(levels, 8))
        for g in range(8):
            far = levels[np.abs(levels - a[p, g]) >= 10]
            a[p, g + 8] = far[np.random.randint(len(far))]
    return np.exp2(a.ravel()).repeat(32)


def f64(x):
    return np.asarray(x).astype(np.float64)


def striped(idx):
    return np.tile(idx.reshape(-1, 16).T, (8, 1)).astype(np.uint16)


def unstriped(offs):
    return offs[:16].T.reshape(-1).astype(np.int64)


def pack_weight(w):
    k, n = w.shape
    w = f64(np.asarray(w, np.float32).astype(ml_dtypes.bfloat16)).reshape(k // 32, 32, n)
    amax = np.abs(w).max(1)
    byte = np.clip(np.where(amax > 0, np.frexp(amax)[1] - 1 + 127 - 7, 1), 1, 254)
    scaled = (w * np.exp2(127.0 - byte)[:, None, :]).reshape(k, n).astype(np.float32)
    words = np.ascontiguousarray(scaled.reshape(k // 512, 128, 4, n).transpose(0, 1, 3, 2)).astype(ml_dtypes.float8_e4m3fn).view(np.uint8)
    return words, np.ascontiguousarray(byte.astype(np.uint8).reshape(k // 512, 16, n))


def unpack_weight(words, scales):
    g, p, n, _ = words.shape
    vals = np.ascontiguousarray(words).view(ml_dtypes.float8_e4m3fn).astype(np.float64) * np.repeat(np.exp2(scales.astype(np.float64) - 127.0), 8, axis=1)[..., None]
    return vals.transpose(0, 1, 3, 2).reshape(g * 512, n)


def sigmoid(v):
    return 1.0 / (1.0 + np.exp(-np.maximum(v, -700.0)))


K, T, S, V, U, R = 1024, 2048, 1024, 512, 512, 256
P = 2 ** 7


def setup_inputs():
    n = np.random.standard_normal
    s = mx_kscale(K)[:, None]
    packed_xT = pack_weight(n((K, T)) * s)
    return {
        "x_words": packed_xT[0],
        "x_scales": packed_xT[1],
        "hT": (n((K, V)) / np.sqrt(K) / s).astype(np.float32),
        "norm": (np.tile(np.random.uniform(0.5, 2.0, U), (P, 1))).astype(np.float32),
        "offs": striped(np.random.permutation(T)[:S]),
        "code1": striped(np.random.permutation(np.concatenate([np.arange(R), np.random.randint(0, R, U - R)]))),
        "code2": striped(np.random.permutation(np.concatenate([np.arange(R), np.random.randint(0, R, U - R)]))),
        "code3": striped(np.random.permutation(np.concatenate([np.arange(R), np.random.randint(0, R, U - R)]))),
        "code4": striped(np.random.permutation(np.concatenate([np.arange(R), np.random.randint(0, R, U - R)]))),
    }


def reference(x_words, x_scales, hT, norm, offs, code1, code2, code3, code4):
    hTq = mxq(f64(hT), 0, "e4m3")
    xq = unpack_weight(x_words, x_scales)[:, unstriped(offs)]
    y = hTq.T @ xq
    l0 = y[:, :R]
    l1 = y[:, R:2 * R]
    l2 = y[:, 2 * R:3 * R]
    l3 = y[:, 3 * R:4 * R]
    return sigmoid(0.5 * (l0[:, unstriped(code1)] + l1[:, unstriped(code2)] + l2[:, unstriped(code3)] + l3[:, unstriped(code4)]) - f64(norm)[:1])

@@ -1,0 +1,161 @@
+from contextlib import ExitStack
+
+import concourse.mybir as mybir
+
+K, T, S, V, U, R = 1024, 2048, 1024, 512, 512, 256
+P = 128
+PACK = 4
+PASSES = K // (P * PACK)
+BOOKS = S // R
+BLOCKS = V // P
+WINDOW = U + 16
+FLOPS = 2 * K * V * S
+
+F32 = mybir.dt.float32
+BF16 = mybir.dt.bfloat16
+I32 = mybir.dt.int32
+U32 = mybir.dt.uint32
+U16 = mybir.dt.uint16
+U8 = mybir.dt.uint8
+FP8X4 = mybir.dt.float8_e4m3fn_x4
+ACT = mybir.ActivationFunctionType
+ADD = mybir.AluOpType.add
+
+
+def tile_picked_yadc_prob_p_kernel(
+    tc, x_words, x_scales, hT, norm, offs, code1, code2, code3, code4, out
+):
+    nc = tc.nc
+    with ExitStack() as ctx:
+        keep = ctx.enter_context(tc.tile_pool(name="keep", bufs=1))
+        psum = ctx.enter_context(tc.psum_pool(name="psum", bufs=8))
+
+        warm = keep.tile([P, 8], F32, name="warm")
+        warm_out = keep.tile([P, 8], F32, name="warm_out")
+        store_scales = keep.tile([P, T], U8, name="store_scales", align_bytes=64)
+        nc.vector.memset(store_scales[:].bitcast(I32), 0)
+        nc.vector.memset(warm[:], 0.0)
+        nc.scalar.activation(warm_out[:], warm[:], ACT.Sigmoid)
+
+        def load_words(o):
+            t = keep.tile([P, T], I32, name="store_words%d" % o, align_bytes=64)
+            nc.sync.dma_start(out=t[:], in_=x_words[o].rearrange("p n t -> p (n t)").bitcast(I32))
+            return t
+
+        def load_queries(o, b0, b1):
+            t = keep.tile([P, PACK, (b1 - b0) * P], F32, name="raw%d_%d" % (o, b0), align_bytes=64)
+            rows = hT[o * P * PACK : (o + 1) * P * PACK, b0 * P : b1 * P]
+            nc.sync.dma_start(out=t[:], in_=rows.rearrange("(p j) w -> p j w", j=PACK))
+            return [t[:, :, (b - b0) * P : (b - b0 + 1) * P] for b in range(b0, b1)]
+
+        def load_list(name, src, n):
+            t = keep.tile([P, n // 16], U16, name=name)
+            nc.sync.dma_start(t[:], src)
+            return t
+
+        offs_sb = load_list("offs_sb", offs, S)
+        words = [load_words(0)]
+        for q in range(4):
+            nc.sync.dma_start(
+                out=store_scales[32 * q : 32 * q + 4 * PASSES, :].bitcast(I32),
+                in_=x_scales[:, 4 * q : 4 * q + 4, :].bitcast(I32),
+            )
+        raw = [[], []]
+        raw[0].extend(load_queries(0, 0, 1))
+        raw[1].extend(load_queries(1, 0, 1))
+        words.append(load_words(1))
+        codes = [load_list("code1_sb", code1, U)]
+        norm_sb = keep.tile([P, U], F32, name="norm_sb")
+        nc.sync.dma_start(out=norm_sb[:], in_=norm)
+        raw[0].extend(load_queries(0, 1, 3))
+        raw[1].extend(load_queries(1, 1, 3))
+        codes.append(load_list("code2_sb", code2, U))
+        codes.append(load_list("code3_sb", code3, U))
+        codes.append(load_list("code4_sb", code4, U))
+        raw[0].extend(load_queries(0, 3, 4))
+        raw[1].extend(load_queries(1, 3, 4))
+
+        picked0 = keep.tile([P, S], U32, name="picked0", align_bytes=64)
+        nc.vector.tensor_copy(picked0[:], words[0][:].bitcast(U32).indirect(offs_sb[:]))
+        picked_scales = keep.tile([P, S], U8, name="picked_scales", align_bytes=64)
+        nc.vector.tensor_copy(picked_scales[:], store_scales[:].indirect(offs_sb[:]))
+        picked = [[picked0[:, d * R : (d + 1) * R] for d in range(BOOKS)], []]
+
+        def pick_book(d):
+            t = keep.tile([P, R], U32, name="picked1_%d" % d, align_bytes=64)
+            piece = offs_sb[:, d * R // 16 : (d + 1) * R // 16]
+            nc.vector.tensor_copy(t[:], words[1][:].bitcast(U32).indirect(piece))
+            picked[1].append(t[:])
+
+        quantized = {}
+
+        def quantize(b0, b1):
+            n = b1 - b0
+            grouped = keep.tile([P, n, PASSES, P, PACK], BF16, name="grouped%d" % b0, tag="grouped%d" % b0, align_bytes=64)
+            for o in range(PASSES):
+                for b in range(b0, b1):
+                    nc.scalar.copy(out=grouped[:, b - b0, o, :, :], in_=raw[o][b].rearrange("p j w -> p w j"))
+            q_codes = keep.tile([P, n, PASSES, P], U32, name="q_codes%d" % b0, align_bytes=64)
+            q_scales = keep.tile([P, n, PASSES, P], U8, name="q_scales%d" % b0, align_bytes=64)
+            nc.vector.quantize_mx(
+                out=q_codes[:].rearrange("p b o w -> p (b o w)").bitcast(FP8X4),
+                scales=q_scales[:].rearrange("p b o w -> p (b o w)"),
+                in_=grouped[:].rearrange("p b o w j -> p (b o w j)"),
+            )
+            for b in range(b0, b1):
+                quantized[b] = (q_codes[:, b - b0, :, :], q_scales[:, b - b0, :, :])
+
+        tabs = {}
+        sums = {}
+
+        def table(b, d):
+            q_codes, q_scales = quantized[b]
+            acc = psum.tile([P, R], F32, name="acc")
+            for o in range(PASSES):
+                nc.tensor.matmul_mx(
+                    out=acc[:],
+                    lhsT=q_codes[:, o, :].bitcast(FP8X4),
+                    lhsT_scale=q_scales[:, o, :],
+                    rhs=picked[o][d].bitcast(FP8X4),
+                    rhs_scale=picked_scales[4 * o : P, d * R : (d + 1) * R],
+                    start=(o == 0),
+                    stop=(o == PASSES - 1),
+                )
+            tab = keep.tile([P, WINDOW], F32, name="tab%d_%d" % (b, d))
+            nc.scalar.activation(tab[:, :R], acc[:], ACT.Copy, scale=-0.5)
+            tabs[(b, d)] = tab
+
+        def look_up(b, d, c0, c1, tag=None):
+            prev = norm_sb[:, c0:c1] if d == 0 else sums[(b, d - 1, c0)][:]
+            name = "sum%d_%d_%d" % (b, d, c0)
+            s = keep.tile([P, c1 - c0], F32, name=name, tag=tag or name, align_bytes=64)
+            piece = codes[d][:, c0 // 16 : c1 // 16]
+            nc.vector.tensor_tensor(s[:], tabs[(b, d)][:].indirect(piece), prev, ADD)
+            sums[(b, d, c0)] = s
+            if d == BOOKS - 1:
+                res = keep.tile([P, c1 - c0], F32, name="res%d_%d" % (b, c0))
+                nc.scalar.activation(res[:], s[:], ACT.Sigmoid, scale=-1.0)
+                nc.sync.dma_start(out=out[b * P : (b + 1) * P, c0:c1], in_=res[:])
+
+        H = U // 2
+        quantize(0, 1)
+        for d in range(BOOKS):
+            pick_book(d)
+        for d in range(BOOKS):
+            table(0, d)
+        quantize(1, 3)
+        for d in range(BOOKS):
+            look_up(0, d, 0, H)
+            look_up(0, d, H, U, "grouped1" if d == 2 else None)
+        for d in range(BOOKS):
+            table(1, d)
+            table(2, d)
+        quantize(3, 4)
+        for d in range(BOOKS):
+            look_up(1, d, 0, U)
+            look_up(2, d, 0, U)
+        for d in range(BOOKS):
+            table(3, d)
+        for d in range(BOOKS):
+            look_up(3, d, 0, H)
+            look_up(3, d, H, U)

@@ -9,6 +9,7 @@ PASSES = K // (P * PACK)
 BOOKS = S // R
 BLOCKS = V // P
 WINDOW = U + 16
+LAST = 64
 FLOPS = 2 * K * V * S
 
 F32 = mybir.dt.float32
@@ -54,17 +55,17 @@ def tile_picked_yadc_prob_p_kernel(
             return t
 
         offs_sb = load_list("offs_sb", offs, S)
-        words = [load_words(0)]
+        codes = [load_list("code1_sb", code1, U)]
         for q in range(4):
             nc.sync.dma_start(
                 out=store_scales[32 * q : 32 * q + 4 * PASSES, :].bitcast(I32),
                 in_=x_scales[:, 4 * q : 4 * q + 4, :].bitcast(I32),
             )
+        words = [load_words(0)]
         raw = [[], []]
         raw[0].extend(load_queries(0, 0, 1))
         raw[1].extend(load_queries(1, 0, 1))
         words.append(load_words(1))
-        codes = [load_list("code1_sb", code1, U)]
         norm_sb = keep.tile([P, U], F32, name="norm_sb")
         nc.sync.dma_start(out=norm_sb[:], in_=norm)
         raw[0].extend(load_queries(0, 1, 3))
@@ -75,10 +76,10 @@ def tile_picked_yadc_prob_p_kernel(
         raw[0].extend(load_queries(0, 3, 4))
         raw[1].extend(load_queries(1, 3, 4))
 
-        picked0 = keep.tile([P, S], U32, name="picked0", align_bytes=64)
-        nc.vector.tensor_copy(picked0[:], words[0][:].bitcast(U32).indirect(offs_sb[:]))
         picked_scales = keep.tile([P, S], U8, name="picked_scales", align_bytes=64)
         nc.vector.tensor_copy(picked_scales[:], store_scales[:].indirect(offs_sb[:]))
+        picked0 = keep.tile([P, S], U32, name="picked0", align_bytes=64)
+        nc.vector.tensor_copy(picked0[:], words[0][:].bitcast(U32).indirect(offs_sb[:]))
         picked = [[picked0[:, d * R : (d + 1) * R] for d in range(BOOKS)], []]
 
         def pick_book(d):
@@ -125,8 +126,9 @@ def tile_picked_yadc_prob_p_kernel(
             nc.scalar.activation(tab[:, :R], acc[:], ACT.Copy, scale=-0.5)
             tabs[(b, d)] = tab
 
-        def look_up(b, d, c0, c1, tag=None):
-            prev = norm_sb[:, c0:c1] if d == 0 else sums[(b, d - 1, c0)][:]
+        def look_up(b, d, c0, c1, tag=None, base=None, queue=None):
+            base = c0 if base is None else base
+            prev = norm_sb[:, c0:c1] if d == 0 else sums[(b, d - 1, base)][:, c0 - base : c1 - base]
             name = "sum%d_%d_%d" % (b, d, c0)
             s = keep.tile([P, c1 - c0], F32, name=name, tag=tag or name, align_bytes=64)
             piece = codes[d][:, c0 // 16 : c1 // 16]
@@ -135,7 +137,7 @@ def tile_picked_yadc_prob_p_kernel(
             if d == BOOKS - 1:
                 res = keep.tile([P, c1 - c0], F32, name="res%d_%d" % (b, c0))
                 nc.scalar.activation(res[:], s[:], ACT.Sigmoid, scale=-1.0)
-                nc.sync.dma_start(out=out[b * P : (b + 1) * P, c0:c1], in_=res[:])
+                (queue or nc.sync).dma_start(out=out[b * P : (b + 1) * P, c0:c1], in_=res[:])
 
         H = U // 2
         quantize(0, 1)
@@ -156,6 +158,9 @@ def tile_picked_yadc_prob_p_kernel(
             look_up(2, d, 0, U)
         for d in range(BOOKS):
             table(3, d)
-        for d in range(BOOKS):
+        for d in range(BOOKS - 1):
             look_up(3, d, 0, H)
             look_up(3, d, H, U)
+        look_up(3, BOOKS - 1, 0, H)
+        look_up(3, BOOKS - 1, H, U - LAST)
+        look_up(3, BOOKS - 1, U - LAST, U, base=H, queue=nc.scalar)

@@ -10,6 +10,7 @@ BOOKS = S // R
 BLOCKS = V // P
 WINDOW = U + 16
 LAST = 64
+FIRST = 384
 FLOPS = 2 * K * V * S
 
 F32 = mybir.dt.float32
@@ -31,85 +32,92 @@ def tile_picked_yadc_prob_p_kernel(
         keep = ctx.enter_context(tc.tile_pool(name="keep", bufs=1))
         psum = ctx.enter_context(tc.psum_pool(name="psum", bufs=8))
 
-        warm = keep.tile([P, 8], F32, name="warm")
-        warm_out = keep.tile([P, 8], F32, name="warm_out")
         store_scales = keep.tile([P, T], U8, name="store_scales", align_bytes=64)
         nc.vector.memset(store_scales[:].bitcast(I32), 0)
+        warm = keep.tile([P, 8], F32, name="warm")
+        warm_out = keep.tile([P, 8], F32, name="warm_out")
         nc.vector.memset(warm[:], 0.0)
         nc.scalar.activation(warm_out[:], warm[:], ACT.Sigmoid)
 
-        def load_words(o):
-            t = keep.tile([P, T], I32, name="store_words%d" % o, align_bytes=64)
-            nc.sync.dma_start(out=t[:], in_=x_words[o].rearrange("p n t -> p (n t)").bitcast(I32))
-            return t
+        words = [keep.tile([P, T], I32, name="store_words%d" % o, align_bytes=64) for o in range(PASSES)]
 
-        def load_queries(o, b0, b1):
-            t = keep.tile([P, PACK, (b1 - b0) * P], F32, name="raw%d_%d" % (o, b0), align_bytes=64)
-            rows = hT[o * P * PACK : (o + 1) * P * PACK, b0 * P : b1 * P]
+        def load_words(o, c0, c1):
+            src = x_words[o].rearrange("p n t -> p (n t)").bitcast(I32)
+            nc.sync.dma_start(out=words[o][:, c0:c1], in_=src[:, c0:c1])
+
+        raw = {}
+
+        def load_queries(b, o):
+            name = "raw%d_%d" % (b, o)
+            t = keep.tile([P, PACK, P], F32, name=name, tag=name, align_bytes=64)
+            rows = hT[o * P * PACK : (o + 1) * P * PACK, b * P : (b + 1) * P]
             nc.sync.dma_start(out=t[:], in_=rows.rearrange("(p j) w -> p j w", j=PACK))
-            return [t[:, :, (b - b0) * P : (b - b0 + 1) * P] for b in range(b0, b1)]
+            raw[(b, o)] = t
 
         def load_list(name, src, n):
             t = keep.tile([P, n // 16], U16, name=name)
             nc.sync.dma_start(t[:], src)
             return t
 
+        load_words(0, 0, FIRST)
         offs_sb = load_list("offs_sb", offs, S)
-        codes = [load_list("code1_sb", code1, U)]
         for q in range(4):
             nc.sync.dma_start(
                 out=store_scales[32 * q : 32 * q + 4 * PASSES, :].bitcast(I32),
                 in_=x_scales[:, 4 * q : 4 * q + 4, :].bitcast(I32),
             )
-        words = [load_words(0)]
-        raw = [[], []]
-        raw[0].extend(load_queries(0, 0, 1))
-        raw[1].extend(load_queries(1, 0, 1))
-        words.append(load_words(1))
+        load_words(0, FIRST, T)
+        load_queries(0, 0)
+        load_queries(0, 1)
+        load_words(1, 0, T)
+        load_queries(1, 0)
+        codes = [load_list("code1_sb", code1, U)]
         norm_sb = keep.tile([P, U], F32, name="norm_sb")
         nc.sync.dma_start(out=norm_sb[:], in_=norm)
-        raw[0].extend(load_queries(0, 1, 3))
-        raw[1].extend(load_queries(1, 1, 3))
+        load_queries(1, 1)
         codes.append(load_list("code2_sb", code2, U))
+        load_queries(2, 0)
+        load_queries(2, 1)
         codes.append(load_list("code3_sb", code3, U))
         codes.append(load_list("code4_sb", code4, U))
-        raw[0].extend(load_queries(0, 3, 4))
-        raw[1].extend(load_queries(1, 3, 4))
+        load_queries(3, 0)
+        load_queries(3, 1)
 
         picked_scales = keep.tile([P, S], U8, name="picked_scales", align_bytes=64)
         nc.vector.tensor_copy(picked_scales[:], store_scales[:].indirect(offs_sb[:]))
-        picked0 = keep.tile([P, S], U32, name="picked0", align_bytes=64)
-        nc.vector.tensor_copy(picked0[:], words[0][:].bitcast(U32).indirect(offs_sb[:]))
-        picked = [[picked0[:, d * R : (d + 1) * R] for d in range(BOOKS)], []]
+        picked = {}
 
-        def pick_book(d):
-            t = keep.tile([P, R], U32, name="picked1_%d" % d, align_bytes=64)
-            piece = offs_sb[:, d * R // 16 : (d + 1) * R // 16]
-            nc.vector.tensor_copy(t[:], words[1][:].bitcast(U32).indirect(piece))
-            picked[1].append(t[:])
+        def pick(o, d0, d1, tag=None):
+            name = "picked%d_%d" % (o, d0)
+            t = keep.tile([P, (d1 - d0) * R], U32, name=name, tag=tag or name, align_bytes=64)
+            piece = offs_sb[:, d0 * R // 16 : d1 * R // 16]
+            nc.vector.tensor_copy(t[:], words[o][:].bitcast(U32).indirect(piece))
+            for d in range(d0, d1):
+                picked[(o, d)] = t[:, (d - d0) * R : (d - d0 + 1) * R]
 
+        grouped = {}
         quantized = {}
 
-        def quantize(b0, b1):
-            n = b1 - b0
-            grouped = keep.tile([P, n, PASSES, P, PACK], BF16, name="grouped%d" % b0, tag="grouped%d" % b0, align_bytes=64)
+        def interleave(b):
+            t = keep.tile([P, PASSES, P, PACK], BF16, name="grouped%d" % b, align_bytes=64)
             for o in range(PASSES):
-                for b in range(b0, b1):
-                    nc.scalar.copy(out=grouped[:, b - b0, o, :, :], in_=raw[o][b].rearrange("p j w -> p w j"))
-            q_codes = keep.tile([P, n, PASSES, P], U32, name="q_codes%d" % b0, align_bytes=64)
-            q_scales = keep.tile([P, n, PASSES, P], U8, name="q_scales%d" % b0, align_bytes=64)
+                nc.scalar.copy(out=t[:, o, :, :], in_=raw[(b, o)][:].rearrange("p j w -> p w j"))
+            grouped[b] = t
+
+        def quantize(b):
+            q_codes = keep.tile([P, PASSES, P], U32, name="q_codes%d" % b, align_bytes=64)
+            q_scales = keep.tile([P, PASSES, P], U8, name="q_scales%d" % b, align_bytes=64)
             nc.vector.quantize_mx(
-                out=q_codes[:].rearrange("p b o w -> p (b o w)").bitcast(FP8X4),
-                scales=q_scales[:].rearrange("p b o w -> p (b o w)"),
-                in_=grouped[:].rearrange("p b o w j -> p (b o w j)"),
+                out=q_codes[:].rearrange("p o w -> p (o w)").bitcast(FP8X4),
+                scales=q_scales[:].rearrange("p o w -> p (o w)"),
+                in_=grouped[b][:].rearrange("p o w j -> p (o w j)"),
             )
-            for b in range(b0, b1):
-                quantized[b] = (q_codes[:, b - b0, :, :], q_scales[:, b - b0, :, :])
+            quantized[b] = (q_codes, q_scales)
 
         tabs = {}
         sums = {}
 
-        def table(b, d):
+        def table(b, d, tag=None):
             q_codes, q_scales = quantized[b]
             acc = psum.tile([P, R], F32, name="acc")
             for o in range(PASSES):
@@ -117,50 +125,71 @@ def tile_picked_yadc_prob_p_kernel(
                     out=acc[:],
                     lhsT=q_codes[:, o, :].bitcast(FP8X4),
                     lhsT_scale=q_scales[:, o, :],
-                    rhs=picked[o][d].bitcast(FP8X4),
+                    rhs=picked[(o, d)].bitcast(FP8X4),
                     rhs_scale=picked_scales[4 * o : P, d * R : (d + 1) * R],
                     start=(o == 0),
                     stop=(o == PASSES - 1),
                 )
-            tab = keep.tile([P, WINDOW], F32, name="tab%d_%d" % (b, d))
+            name = "tab%d_%d" % (b, d)
+            tab = keep.tile([P, WINDOW], F32, name=name, tag=tag or name, align_bytes=64)
             nc.scalar.activation(tab[:, :R], acc[:], ACT.Copy, scale=-0.5)
             tabs[(b, d)] = tab
 
-        def look_up(b, d, c0, c1, tag=None, base=None, queue=None):
-            base = c0 if base is None else base
-            prev = norm_sb[:, c0:c1] if d == 0 else sums[(b, d - 1, base)][:, c0 - base : c1 - base]
+        def look_up(b, d, c0=0, c1=U, tag=None):
+            prev = norm_sb if d == 0 else sums[(b, d - 1, 0)]
             name = "sum%d_%d_%d" % (b, d, c0)
             s = keep.tile([P, c1 - c0], F32, name=name, tag=tag or name, align_bytes=64)
             piece = codes[d][:, c0 // 16 : c1 // 16]
-            nc.vector.tensor_tensor(s[:], tabs[(b, d)][:].indirect(piece), prev, ADD)
+            nc.vector.tensor_tensor(s[:], tabs[(b, d)][:].indirect(piece), prev[:, c0:c1], ADD)
             sums[(b, d, c0)] = s
-            if d == BOOKS - 1:
-                res = keep.tile([P, c1 - c0], F32, name="res%d_%d" % (b, c0))
-                nc.scalar.activation(res[:], s[:], ACT.Sigmoid, scale=-1.0)
-                (queue or nc.sync).dma_start(out=out[b * P : (b + 1) * P, c0:c1], in_=res[:])
 
-        H = U // 2
-        quantize(0, 1)
-        for d in range(BOOKS):
-            pick_book(d)
-        for d in range(BOOKS):
-            table(0, d)
-        quantize(1, 3)
-        for d in range(BOOKS):
-            look_up(0, d, 0, H)
-            look_up(0, d, H, U, "grouped1" if d == 2 else None)
-        for d in range(BOOKS):
-            table(1, d)
+        def finish(b, c0=0, c1=U, queue=nc.sync):
+            res = keep.tile([P, c1 - c0], F32, name="res%d_%d" % (b, c0))
+            nc.scalar.activation(res[:], sums[(b, BOOKS - 1, c0)][:], ACT.Sigmoid, scale=-1.0)
+            queue.dma_start(out=out[b * P : (b + 1) * P, c0:c1], in_=res[:])
+
+        pick(0, 0, BOOKS)
+        interleave(0)
+        quantize(0)
+        pick(1, 0, 1)
+        pick(1, 1, BOOKS)
+        table(0, 0)
+        interleave(1)
+        table(0, 1, "raw1_1")
+        look_up(0, 0)
+        quantize(1)
+        look_up(0, 1)
+        interleave(2)
+        table(0, 2, "raw2_1")
+        quantize(2)
+        look_up(0, 2)
+        table(1, 0)
+        table(0, 3)
+        table(1, 1)
+        look_up(1, 0)
+        look_up(0, 3)
+        look_up(1, 1)
+        interleave(3)
+        table(1, 2, "raw3_1")
+        quantize(3)
+        table(2, 0)
+        table(1, 3)
+        table(3, 0)
+        for d in range(1, BOOKS):
             table(2, d)
-        quantize(3, 4)
-        for d in range(BOOKS):
-            look_up(1, d, 0, U)
-            look_up(2, d, 0, U)
-        for d in range(BOOKS):
             table(3, d)
-        for d in range(BOOKS - 1):
-            look_up(3, d, 0, H)
-            look_up(3, d, H, U)
-        look_up(3, BOOKS - 1, 0, H)
-        look_up(3, BOOKS - 1, H, U - LAST)
-        look_up(3, BOOKS - 1, U - LAST, U, base=H, queue=nc.scalar)
+        look_up(1, 2)
+        look_up(2, 0)
+        look_up(1, 3)
+        look_up(3, 0)
+        finish(0)
+        finish(1)
+        for d in range(1, BOOKS - 1):
+            look_up(2, d)
+            look_up(3, d)
+        look_up(2, BOOKS - 1)
+        finish(2)
+        cuts = (0, U // 2, U - LAST, U)
+        for c0, c1 in zip(cuts, cuts[1:]):
+            look_up(3, BOOKS - 1, c0, c1)
+            finish(3, c0, c1, nc.scalar if c1 == U else nc.sync)

@@ -61,7 +61,7 @@ def tile_picked_yadc_prob_p_kernel(
 
         load_words(0, 0, FIRST)
         offs_sb = load_list("offs_sb", offs, S)
-        for q in range(4):
+        for q in (2, 3, 0, 1):
             nc.sync.dma_start(
                 out=store_scales[32 * q : 32 * q + 4 * PASSES, :].bitcast(I32),
                 in_=x_scales[:, 4 * q : 4 * q + 4, :].bitcast(I32),

@@ -10,7 +10,7 @@ BOOKS = S // R
 BLOCKS = V // P
 WINDOW = U + 16
 LAST = 64
-FIRST = 384
+FIRST = 512
 FLOPS = 2 * K * V * S
 
 F32 = mybir.dt.float32
@@ -30,14 +30,11 @@ def tile_picked_yadc_prob_p_kernel(
     nc = tc.nc
     with ExitStack() as ctx:
         keep = ctx.enter_context(tc.tile_pool(name="keep", bufs=1))
-        psum = ctx.enter_context(tc.psum_pool(name="psum", bufs=8))
+        psum = ctx.enter_context(tc.psum_pool(name="psum", bufs=7))
+        shared = ctx.enter_context(tc.psum_pool(name="shared", bufs=1))
 
         store_scales = keep.tile([P, T], U8, name="store_scales", align_bytes=64)
         nc.vector.memset(store_scales[:].bitcast(I32), 0)
-        warm = keep.tile([P, 8], F32, name="warm")
-        warm_out = keep.tile([P, 8], F32, name="warm_out")
-        nc.vector.memset(warm[:], 0.0)
-        nc.scalar.activation(warm_out[:], warm[:], ACT.Sigmoid)
 
         words = [keep.tile([P, T], I32, name="store_words%d" % o, align_bytes=64) for o in range(PASSES)]
 
@@ -105,7 +102,7 @@ def tile_picked_yadc_prob_p_kernel(
             grouped[b] = t
 
         def quantize(b):
-            q_codes = keep.tile([P, PASSES, P], U32, name="q_codes%d" % b, align_bytes=64)
+            q_codes = keep.tile([P, PASSES, P], U32, name="q_codes%d" % b, tag="q_codes%d" % b, align_bytes=64)
             q_scales = keep.tile([P, PASSES, P], U8, name="q_scales%d" % b, align_bytes=64)
             nc.vector.quantize_mx(
                 out=q_codes[:].rearrange("p o w -> p (o w)").bitcast(FP8X4),
@@ -117,9 +114,9 @@ def tile_picked_yadc_prob_p_kernel(
         tabs = {}
         sums = {}
 
-        def table(b, d, tag=None):
+        def table(b, d, tag=None, bank=psum):
             q_codes, q_scales = quantized[b]
-            acc = psum.tile([P, R], F32, name="acc")
+            acc = bank.tile([P, R], F32, name="acc")
             for o in range(PASSES):
                 nc.tensor.matmul_mx(
                     out=acc[:],
@@ -143,8 +140,9 @@ def tile_picked_yadc_prob_p_kernel(
             nc.vector.tensor_tensor(s[:], tabs[(b, d)][:].indirect(piece), prev[:, c0:c1], ADD)
             sums[(b, d, c0)] = s
 
-        def finish(b, c0=0, c1=U, queue=nc.sync):
-            res = keep.tile([P, c1 - c0], F32, name="res%d_%d" % (b, c0))
+        def finish(b, c0=0, c1=U, queue=nc.sync, tag=None):
+            name = "res%d_%d" % (b, c0)
+            res = keep.tile([P, c1 - c0], F32, name=name, tag=tag or name, align_bytes=64)
             nc.scalar.activation(res[:], sums[(b, BOOKS - 1, c0)][:], ACT.Sigmoid, scale=-1.0)
             queue.dma_start(out=out[b * P : (b + 1) * P, c0:c1], in_=res[:])
 
@@ -155,7 +153,7 @@ def tile_picked_yadc_prob_p_kernel(
         pick(1, 1, BOOKS)
         table(0, 0)
         interleave(1)
-        table(0, 1, "raw1_1")
+        table(0, 1, "raw1_1", shared)
         look_up(0, 0)
         quantize(1)
         look_up(0, 1)
@@ -163,8 +161,8 @@ def tile_picked_yadc_prob_p_kernel(
         table(0, 2, "raw2_1")
         quantize(2)
         look_up(0, 2)
-        table(1, 0)
-        table(0, 3)
+        table(1, 0, "raw2_0")
+        table(0, 3, bank=shared)
         table(1, 1)
         look_up(1, 0)
         look_up(0, 3)
@@ -182,7 +180,7 @@ def tile_picked_yadc_prob_p_kernel(
         look_up(2, 0)
         look_up(1, 3)
         look_up(3, 0)
-        finish(0)
+        finish(0, tag="q_codes3")
         finish(1)
         for d in range(1, BOOKS - 1):
             look_up(2, d)

@@ -1,16 +1,20 @@
 from contextlib import ExitStack
 
 import concourse.mybir as mybir
+from concourse.masks import make_identity
 
 K, T, S, V, U, R = 1024, 2048, 1024, 512, 512, 256
 P = 128
 PACK = 4
 PASSES = K // (P * PACK)
 BOOKS = S // R
-BLOCKS = V // P
 WINDOW = U + 16
+LOG_WINDOW = 4 * U
 LAST = 64
 FIRST = 512
+MARGIN = 33.0 / 64.0
+FLOOR = 1.0 / 16.0
+ROOT_BITS = float(127 << 22)
 FLOPS = 2 * K * V * S
 
 F32 = mybir.dt.float32
@@ -30,11 +34,20 @@ def tile_picked_yadc_prob_p_kernel(
     nc = tc.nc
     with ExitStack() as ctx:
         keep = ctx.enter_context(tc.tile_pool(name="keep", bufs=1))
-        psum = ctx.enter_context(tc.psum_pool(name="psum", bufs=7))
-        shared = ctx.enter_context(tc.psum_pool(name="shared", bufs=1))
+        psum = ctx.enter_context(tc.psum_pool(name="psum", bufs=4))
+        single = ctx.enter_context(tc.psum_pool(name="single", bufs=1))
 
         store_scales = keep.tile([P, T], U8, name="store_scales", align_bytes=64)
         nc.vector.memset(store_scales[:].bitcast(I32), 0)
+        floor = keep.tile([P, 1], F32, name="floor")
+        nc.vector.memset(floor[:], FLOOR)
+        factor = keep.tile([P, 1], F32, name="factor", tag="factor", align_bytes=64)
+        nc.vector.memset(factor[:], -0.5)
+        warm = keep.tile([P, 1], F32, name="warm")
+        nc.scalar.activation(warm[:], floor[:], ACT.Ln)
+        ident = keep.tile([P, P], F32, name="ident", align_bytes=64)
+        nc.vector.memset(ident[:], 0.0)
+        make_identity(nc, ident[:], nomemset=True)
 
         words = [keep.tile([P, T], I32, name="store_words%d" % o, align_bytes=64) for o in range(PASSES)]
 
@@ -44,12 +57,17 @@ def tile_picked_yadc_prob_p_kernel(
 
         raw = {}
 
-        def load_queries(b, o):
-            name = "raw%d_%d" % (b, o)
-            t = keep.tile([P, PACK, P], F32, name=name, tag=name, align_bytes=64)
-            rows = hT[o * P * PACK : (o + 1) * P * PACK, b * P : (b + 1) * P]
-            nc.sync.dma_start(out=t[:], in_=rows.rearrange("(p j) w -> p j w", j=PACK))
-            raw[(b, o)] = t
+        def load_queries(b, n, o):
+            if b == 0:
+                t = keep.tile([P, PACK, P], F32, name="raw0_%d" % o, align_bytes=64)
+                raw[(b, o)] = t
+                dst = t[:]
+            else:
+                if o == 0:
+                    raw[b] = keep.tile([P, PASSES, PACK, n * P], F32, name="raw%d" % b, align_bytes=64)
+                dst = raw[b][:, o, :, :]
+            rows = hT[o * P * PACK : (o + 1) * P * PACK, b * P : (b + n) * P]
+            nc.sync.dma_start(out=dst, in_=rows.rearrange("(p j) w -> p j w", j=PACK))
 
         def load_list(name, src, n):
             t = keep.tile([P, n // 16], U16, name=name)
@@ -64,73 +82,98 @@ def tile_picked_yadc_prob_p_kernel(
                 in_=x_scales[:, 4 * q : 4 * q + 4, :].bitcast(I32),
             )
         load_words(0, FIRST, T)
-        load_queries(0, 0)
-        load_queries(0, 1)
+        load_queries(0, 1, 0)
+        load_queries(0, 1, 1)
         load_words(1, 0, T)
-        load_queries(1, 0)
+        load_queries(1, 2, 0)
+        load_queries(1, 2, 1)
+        load_queries(3, 1, 0)
+        load_queries(3, 1, 1)
         codes = [load_list("code1_sb", code1, U)]
-        norm_sb = keep.tile([P, U], F32, name="norm_sb")
+        norm_sb = keep.tile([P, U], F32, name="norm_sb", align_bytes=64)
         nc.sync.dma_start(out=norm_sb[:], in_=norm)
-        load_queries(1, 1)
         codes.append(load_list("code2_sb", code2, U))
-        load_queries(2, 0)
-        load_queries(2, 1)
         codes.append(load_list("code3_sb", code3, U))
         codes.append(load_list("code4_sb", code4, U))
-        load_queries(3, 0)
-        load_queries(3, 1)
 
         picked_scales = keep.tile([P, S], U8, name="picked_scales", align_bytes=64)
         nc.vector.tensor_copy(picked_scales[:], store_scales[:].indirect(offs_sb[:]))
         picked = {}
 
-        def pick(o, d0, d1, tag=None):
+        def pick(o, d0, d1):
             name = "picked%d_%d" % (o, d0)
-            t = keep.tile([P, (d1 - d0) * R], U32, name=name, tag=tag or name, align_bytes=64)
+            t = keep.tile([P, (d1 - d0) * R], U32, name=name, align_bytes=64)
             piece = offs_sb[:, d0 * R // 16 : d1 * R // 16]
             nc.vector.tensor_copy(t[:], words[o][:].bitcast(U32).indirect(piece))
             for d in range(d0, d1):
-                picked[(o, d)] = t[:, (d - d0) * R : (d - d0 + 1) * R]
+                picked[(o, d)] = (t, d0)
 
         grouped = {}
         quantized = {}
 
-        def interleave(b):
-            t = keep.tile([P, PASSES, P, PACK], BF16, name="grouped%d" % b, align_bytes=64)
-            for o in range(PASSES):
-                nc.scalar.copy(out=t[:, o, :, :], in_=raw[(b, o)][:].rearrange("p j w -> p w j"))
+        def interleave(b, n):
+            t = keep.tile([P, PASSES, n * P, PACK], BF16, name="grouped%d" % b, align_bytes=64)
+            if b == 0:
+                for o in range(PASSES):
+                    nc.scalar.copy(out=t[:, o, :, :], in_=raw[(b, o)][:].rearrange("p j w -> p w j"))
+            else:
+                nc.vector.tensor_copy(out=t[:], in_=raw[b][:].rearrange("p o j w -> p o w j"))
             grouped[b] = t
 
-        def quantize(b):
-            q_codes = keep.tile([P, PASSES, P], U32, name="q_codes%d" % b, tag="q_codes%d" % b, align_bytes=64)
-            q_scales = keep.tile([P, PASSES, P], U8, name="q_scales%d" % b, align_bytes=64)
+        def quantize(b, n):
+            q_codes = keep.tile([P, PASSES, n * P], U32, name="q_codes%d" % b, align_bytes=64)
+            q_scales = keep.tile([P, PASSES, n * P], U8, name="q_scales%d" % b, align_bytes=64)
             nc.vector.quantize_mx(
                 out=q_codes[:].rearrange("p o w -> p (o w)").bitcast(FP8X4),
                 scales=q_scales[:].rearrange("p o w -> p (o w)"),
                 in_=grouped[b][:].rearrange("p o w j -> p (o w j)"),
             )
-            quantized[b] = (q_codes, q_scales)
+            for i in range(n):
+                quantized[b + i] = (q_codes, q_scales, slice(i * P, (i + 1) * P))
+
+        def product(acc, b, d0, d1):
+            q_codes, q_scales, cols = quantized[b]
+            for o in range(PASSES):
+                t, first = picked[(o, d0)]
+                nc.tensor.matmul_mx(
+                    out=acc[:],
+                    lhsT=q_codes[:, o, cols].bitcast(FP8X4),
+                    lhsT_scale=q_scales[:, o, cols],
+                    rhs=t[:, (d0 - first) * R : (d1 - first) * R].bitcast(FP8X4),
+                    rhs_scale=picked_scales[4 * o : P, d0 * R : d1 * R],
+                    start=(o == 0),
+                    stop=(o == PASSES - 1),
+                )
 
         tabs = {}
         sums = {}
 
-        def table(b, d, tag=None, bank=psum):
-            q_codes, q_scales = quantized[b]
-            acc = bank.tile([P, R], F32, name="acc")
-            for o in range(PASSES):
-                nc.tensor.matmul_mx(
-                    out=acc[:],
-                    lhsT=q_codes[:, o, :].bitcast(FP8X4),
-                    lhsT_scale=q_scales[:, o, :],
-                    rhs=picked[(o, d)].bitcast(FP8X4),
-                    rhs_scale=picked_scales[4 * o : P, d * R : (d + 1) * R],
-                    start=(o == 0),
-                    stop=(o == PASSES - 1),
-                )
+        def leave(b, d, acc, tag=None, scale=-0.5):
             name = "tab%d_%d" % (b, d)
             tab = keep.tile([P, WINDOW], F32, name=name, tag=tag or name, align_bytes=64)
-            nc.scalar.activation(tab[:, :R], acc[:], ACT.Copy, scale=-0.5)
+            nc.scalar.activation(tab[:, :R], acc, ACT.Copy, scale=scale)
             tabs[(b, d)] = tab
+
+        def table(b, d, scale=-0.5):
+            acc = psum.tile([P, R], F32, name="acc")
+            product(acc, b, d, d + 1)
+            leave(b, d, acc[:], scale=scale)
+
+        logs = {}
+        totals = keep.tile([P, BOOKS], F32, name="totals", align_bytes=64)
+        shifts = keep.tile([P, BOOKS], F32, name="shifts", align_bytes=64)
+
+        def log_table(d):
+            acc = single.tile([P, R], F32, name="log_acc", tag="bank%d" % d)
+            product(acc, 0, d, d + 1)
+            squares = keep.tile([P, R], BF16, name="squares%d" % d, align_bytes=64)
+            total = totals[:, d : d + 1]
+            shift = shifts[:, d : d + 1]
+            nc.scalar.activation(squares[:], acc[:], ACT.Square, bias=floor[:], scale=MARGIN, accum_out=total)
+            nc.scalar.activation(shift.bitcast(U32), total.bitcast(U32), ACT.Copy, bias=ROOT_BITS, scale=0.5)
+            tab = keep.tile([P, LOG_WINDOW], F32, name="log%d" % d, align_bytes=64)
+            nc.scalar.activation(tab[:, :R], acc[:], ACT.Ln, bias=shift, scale=factor[:])
+            logs[d] = tab
 
         def look_up(b, d, c0=0, c1=U, tag=None):
             prev = norm_sb if d == 0 else sums[(b, d - 1, 0)]
@@ -147,47 +190,59 @@ def tile_picked_yadc_prob_p_kernel(
             queue.dma_start(out=out[b * P : (b + 1) * P, c0:c1], in_=res[:])
 
         pick(0, 0, BOOKS)
-        interleave(0)
-        quantize(0)
-        pick(1, 0, 1)
-        pick(1, 1, BOOKS)
-        table(0, 0)
-        interleave(1)
-        table(0, 1, "raw1_1", shared)
-        look_up(0, 0)
-        quantize(1)
-        look_up(0, 1)
-        interleave(2)
-        table(0, 2, "raw2_1")
-        quantize(2)
-        look_up(0, 2)
-        table(1, 0, "raw2_0")
-        table(0, 3, bank=shared)
-        table(1, 1)
-        look_up(1, 0)
-        look_up(0, 3)
-        look_up(1, 1)
-        interleave(3)
-        table(1, 2, "raw3_1")
-        quantize(3)
-        table(2, 0)
-        table(1, 3)
-        table(3, 0)
-        for d in range(1, BOOKS):
-            table(2, d)
-            table(3, d)
-        look_up(1, 2)
-        look_up(2, 0)
-        look_up(1, 3)
-        look_up(3, 0)
-        finish(0, tag="q_codes3")
-        finish(1)
-        for d in range(1, BOOKS - 1):
-            look_up(2, d)
-            look_up(3, d)
+        interleave(0, 1)
+        quantize(0, 1)
+        for d in range(BOOKS):
+            pick(1, d, d + 1)
+        for d in range(BOOKS):
+            log_table(d)
+        shifts_again = keep.tile([P, BOOKS], F32, name="shifts_again")
+        unshift = keep.tile([P, 1], F32, name="unshift", tag="unshift", align_bytes=64)
+        nc.scalar.activation(shifts_again[:], shifts[:], ACT.Copy, accum_out=unshift[:])
+
+        interleave(1, 2)
+        interleave(3, 1)
+        quantize(1, 2)
+        quantize(3, 1)
+        for d in range(BOOKS):
+            for b in (1, 2, 3):
+                table(b, d, factor[:])
+        for d in range(BOOKS - 1):
+            for b in (1, 2, 3):
+                look_up(b, d)
+        look_up(1, BOOKS - 1)
         look_up(2, BOOKS - 1)
-        finish(2)
+
+        fetched = keep.tile([P, BOOKS, U], F32, name="fetched", tag="factor", align_bytes=64)
+        for d in range(BOOKS):
+            nc.scalar.activation(fetched[:, d, :], logs[d][:].indirect(codes[d][:]), ACT.Exp)
+
+        turned = [single.tile([P, P], F32, name="turned%d" % c, tag="bank%d" % c) for c in range(U // P)]
+        terms = [fetched[:, 0, :], norm_sb[:]] + [fetched[:, d, :] for d in range(1, BOOKS)]
+        for i, term in enumerate(terms):
+            for c in range(U // P):
+                nc.tensor.matmul(
+                    turned[c][:],
+                    term[:, c * P : (c + 1) * P],
+                    ident[:],
+                    start=(i == 0),
+                    stop=(i == len(terms) - 1),
+                    is_transpose=True,
+                )
+        turned_sb = keep.tile([P, U // P, P], F32, name="turned_sb", align_bytes=64)
+        back = psum.tile([P, U], F32, name="acc")
+        for c in range(U // P):
+            nc.scalar.copy(out=turned_sb[:, c, :], in_=turned[c][:])
+            nc.tensor.transpose(back[:, c * P : (c + 1) * P], turned_sb[:, c, :], ident[:])
+        res0 = keep.tile([P, U], F32, name="res0", align_bytes=64)
+        nc.scalar.activation(res0[:], back[:], ACT.Sigmoid, bias=unshift[:], scale=-1.0)
+        nc.sync.dma_start(out=out[0:P, :], in_=res0[:])
+        finish(1, tag="unshift")
+        finish(2, tag="sum1_3_0")
+        res3 = keep.tile([P, U], F32, name="res3", tag="sum2_3_0", align_bytes=64)
         cuts = (0, U // 2, U - LAST, U)
         for c0, c1 in zip(cuts, cuts[1:]):
             look_up(3, BOOKS - 1, c0, c1)
-            finish(3, c0, c1, nc.scalar if c1 == U else nc.sync)
+            nc.scalar.activation(res3[:, c0:c1], sums[(3, BOOKS - 1, c0)][:], ACT.Sigmoid, scale=-1.0)
+            queue = nc.scalar if c1 == U else nc.sync
+            queue.dma_start(out=out[3 * P : 4 * P, c0:c1], in_=res3[:, c0:c1])

@@ -12,6 +12,7 @@ WINDOW = U + 16
 LOG_WINDOW = 4 * U
 LAST = 64
 FIRST = 512
+HELD = 4 * WINDOW * 4 + LOG_WINDOW * 4
 MARGIN = 33.0 / 64.0
 FLOOR = 1.0 / 16.0
 ROOT_BITS = float(127 << 22)
@@ -34,6 +35,7 @@ def tile_picked_yadc_prob_p_kernel(
     nc = tc.nc
     with ExitStack() as ctx:
         keep = ctx.enter_context(tc.tile_pool(name="keep", bufs=1))
+        shared = ctx.enter_context(tc.tile_pool(name="shared", bufs=1))
         psum = ctx.enter_context(tc.psum_pool(name="psum", bufs=4))
         single = ctx.enter_context(tc.psum_pool(name="single", bufs=1))
 
@@ -43,6 +45,10 @@ def tile_picked_yadc_prob_p_kernel(
         nc.vector.memset(floor[:], FLOOR)
         factor = keep.tile([P, 1], F32, name="factor", tag="factor", align_bytes=64)
         nc.vector.memset(factor[:], -0.5)
+        late_factor = keep.tile([P, 1], F32, name="late_factor", tag="late_factor", align_bytes=64)
+        nc.vector.memset(late_factor[:], -0.5)
+        first_factor = shared.tile([P, 16], F32, name="first_factor", offset=HELD - 32)
+        nc.vector.memset(first_factor[:], -0.5)
         warm = keep.tile([P, 1], F32, name="warm")
         nc.scalar.activation(warm[:], floor[:], ACT.Ln)
         ident = keep.tile([P, P], F32, name="ident", align_bytes=64)
@@ -85,13 +91,15 @@ def tile_picked_yadc_prob_p_kernel(
         load_queries(0, 1, 0)
         load_queries(0, 1, 1)
         load_words(1, 0, T)
-        load_queries(1, 2, 0)
-        load_queries(1, 2, 1)
-        load_queries(3, 1, 0)
-        load_queries(3, 1, 1)
+        load_queries(1, 1, 0)
+        load_queries(1, 1, 1)
         codes = [load_list("code1_sb", code1, U)]
+        load_queries(2, 1, 0)
+        load_queries(2, 1, 1)
         norm_sb = keep.tile([P, U], F32, name="norm_sb", align_bytes=64)
         nc.sync.dma_start(out=norm_sb[:], in_=norm)
+        load_queries(3, 1, 0)
+        load_queries(3, 1, 1)
         codes.append(load_list("code2_sb", code2, U))
         codes.append(load_list("code3_sb", code3, U))
         codes.append(load_list("code4_sb", code4, U))
@@ -148,31 +156,48 @@ def tile_picked_yadc_prob_p_kernel(
         tabs = {}
         sums = {}
 
-        def leave(b, d, acc, tag=None, scale=-0.5):
+        def leave(b, d, acc, scale, place):
             name = "tab%d_%d" % (b, d)
-            tab = keep.tile([P, WINDOW], F32, name=name, tag=tag or name, align_bytes=64)
+            if place is None:
+                tab = keep.tile([P, WINDOW], F32, name=name, align_bytes=64)
+            else:
+                tab = shared.tile([P, WINDOW], F32, name=name, offset=place * WINDOW * 4)
             nc.scalar.activation(tab[:, :R], acc, ACT.Copy, scale=scale)
             tabs[(b, d)] = tab
 
-        def table(b, d, scale=-0.5):
-            acc = psum.tile([P, R], F32, name="acc")
+        def table(b, d, scale, place=None):
+            if b == 3:
+                acc = single.tile([P, R], F32, name="acc3", tag="bank%d" % d)
+            else:
+                acc = psum.tile([P, R], F32, name="acc")
             product(acc, b, d, d + 1)
-            leave(b, d, acc[:], scale=scale)
+            leave(b, d, acc[:], scale, place)
 
         logs = {}
         totals = keep.tile([P, BOOKS], F32, name="totals", align_bytes=64)
         shifts = keep.tile([P, BOOKS], F32, name="shifts", align_bytes=64)
 
-        def log_table(d):
+        log_accs = {}
+
+        def shift_of(d):
             acc = single.tile([P, R], F32, name="log_acc", tag="bank%d" % d)
             product(acc, 0, d, d + 1)
             squares = keep.tile([P, R], BF16, name="squares%d" % d, align_bytes=64)
             total = totals[:, d : d + 1]
-            shift = shifts[:, d : d + 1]
             nc.scalar.activation(squares[:], acc[:], ACT.Square, bias=floor[:], scale=MARGIN, accum_out=total)
+            shift = shifts[:, d : d + 1]
             nc.scalar.activation(shift.bitcast(U32), total.bitcast(U32), ACT.Copy, bias=ROOT_BITS, scale=0.5)
-            tab = keep.tile([P, LOG_WINDOW], F32, name="log%d" % d, align_bytes=64)
-            nc.scalar.activation(tab[:, :R], acc[:], ACT.Ln, bias=shift, scale=factor[:])
+            log_accs[d] = acc
+
+        def log_table(d):
+            name = "log%d" % d
+            if d == 0:
+                tab = shared.tile([P, LOG_WINDOW], F32, name=name, offset=0)
+            elif d == BOOKS - 1:
+                tab = shared.tile([P, LOG_WINDOW], F32, name=name, offset=HELD - LOG_WINDOW * 4)
+            else:
+                tab = keep.tile([P, LOG_WINDOW], F32, name=name, align_bytes=64)
+            nc.scalar.activation(tab[:, :R], log_accs[d][:], ACT.Ln, bias=shifts[:, d : d + 1], scale=factor[:])
             logs[d] = tab
 
         def look_up(b, d, c0=0, c1=U, tag=None):
@@ -192,33 +217,53 @@ def tile_picked_yadc_prob_p_kernel(
         pick(0, 0, BOOKS)
         interleave(0, 1)
         quantize(0, 1)
+        pick(1, 0, 1)
+        pick(1, 1, 2)
+        pick(1, 2, BOOKS)
         for d in range(BOOKS):
-            pick(1, d, d + 1)
-        for d in range(BOOKS):
-            log_table(d)
+            shift_of(d)
+            if d < BOOKS - 1:
+                log_table(d)
         shifts_again = keep.tile([P, BOOKS], F32, name="shifts_again")
         unshift = keep.tile([P, 1], F32, name="unshift", tag="unshift", align_bytes=64)
         nc.scalar.activation(shifts_again[:], shifts[:], ACT.Copy, accum_out=unshift[:])
 
-        interleave(1, 2)
-        interleave(3, 1)
-        quantize(1, 2)
-        quantize(3, 1)
-        for d in range(BOOKS):
-            for b in (1, 2, 3):
-                table(b, d, factor[:])
-        for d in range(BOOKS - 1):
-            for b in (1, 2, 3):
-                look_up(b, d)
-        look_up(1, BOOKS - 1)
-        look_up(2, BOOKS - 1)
+        fetched = {}
 
-        fetched = keep.tile([P, BOOKS, U], F32, name="fetched", tag="factor", align_bytes=64)
+        def fetch(d0, d1, tag):
+            t = keep.tile([P, d1 - d0, U], F32, name="fetched%d" % d0, tag=tag, align_bytes=64)
+            for d in range(d0, d1):
+                nc.scalar.activation(t[:, d - d0, :], logs[d][:].indirect(codes[d][:]), ACT.Exp)
+                fetched[d] = t[:, d - d0, :]
+
+        interleave(1, 1)
+        quantize(1, 1)
+        table(1, 0, first_factor[:, 0:1])
+        table(1, 1, factor[:])
+        log_table(BOOKS - 1)
+        table(1, 2, factor[:])
+        table(1, 3, factor[:])
+        interleave(2, 1)
+        quantize(2, 1)
+        look_up(1, 0)
+        interleave(3, 1)
+        look_up(1, 1)
+        quantize(3, 1)
+        look_up(1, 2)
+        fetch(0, 1, "factor")
         for d in range(BOOKS):
-            nc.scalar.activation(fetched[:, d, :], logs[d][:].indirect(codes[d][:]), ACT.Exp)
+            table(2, d, late_factor[:], d)
+        for d in range(BOOKS):
+            table(3, d, late_factor[:])
+        fetch(1, BOOKS, "late_factor")
+        look_up(2, 0)
+        look_up(1, 3)
+        for d in range(BOOKS - 1):
+            look_up(3, d)
+            look_up(2, d + 1)
 
         turned = [single.tile([P, P], F32, name="turned%d" % c, tag="bank%d" % c) for c in range(U // P)]
-        terms = [fetched[:, 0, :], norm_sb[:]] + [fetched[:, d, :] for d in range(1, BOOKS)]
+        terms = [fetched[1], fetched[0], norm_sb[:]] + [fetched[d] for d in range(2, BOOKS)]
         for i, term in enumerate(terms):
             for c in range(U // P):
                 nc.tensor.matmul(

@@ -12,7 +12,7 @@ WINDOW = U + 16
 LOG_WINDOW = 4 * U
 LAST = 64
 FIRST = 512
-HELD = 4 * WINDOW * 4 + LOG_WINDOW * 4
+LOGS = BOOKS - 1
 MARGIN = 33.0 / 64.0
 FLOOR = 1.0 / 16.0
 ROOT_BITS = float(127 << 22)
@@ -47,8 +47,6 @@ def tile_picked_yadc_prob_p_kernel(
         nc.vector.memset(factor[:], -0.5)
         late_factor = keep.tile([P, 1], F32, name="late_factor", tag="late_factor", align_bytes=64)
         nc.vector.memset(late_factor[:], -0.5)
-        first_factor = shared.tile([P, 16], F32, name="first_factor", offset=HELD - 32)
-        nc.vector.memset(first_factor[:], -0.5)
         warm = keep.tile([P, 1], F32, name="warm")
         nc.scalar.activation(warm[:], floor[:], ACT.Ln)
         ident = keep.tile([P, P], F32, name="ident", align_bytes=64)
@@ -93,16 +91,16 @@ def tile_picked_yadc_prob_p_kernel(
         load_words(1, 0, T)
         load_queries(1, 1, 0)
         load_queries(1, 1, 1)
-        codes = [load_list("code1_sb", code1, U)]
-        load_queries(2, 1, 0)
-        load_queries(2, 1, 1)
+        codes = {3: load_list("code4_sb", code4, U)}
         norm_sb = keep.tile([P, U], F32, name="norm_sb", align_bytes=64)
         nc.sync.dma_start(out=norm_sb[:], in_=norm)
+        load_queries(2, 1, 0)
+        load_queries(2, 1, 1)
+        codes[0] = load_list("code1_sb", code1, U)
         load_queries(3, 1, 0)
         load_queries(3, 1, 1)
-        codes.append(load_list("code2_sb", code2, U))
-        codes.append(load_list("code3_sb", code3, U))
-        codes.append(load_list("code4_sb", code4, U))
+        codes[1] = load_list("code2_sb", code2, U)
+        codes[2] = load_list("code3_sb", code3, U)
 
         picked_scales = keep.tile([P, S], U8, name="picked_scales", align_bytes=64)
         nc.vector.tensor_copy(picked_scales[:], store_scales[:].indirect(offs_sb[:]))
@@ -120,7 +118,7 @@ def tile_picked_yadc_prob_p_kernel(
         quantized = {}
 
         def interleave(b, n):
-            t = keep.tile([P, PASSES, n * P, PACK], BF16, name="grouped%d" % b, align_bytes=64)
+            t = keep.tile([P, PASSES, n * P, PACK], BF16, name="grouped%d" % b, tag="grouped%d" % b, align_bytes=64)
             if b == 0:
                 for o in range(PASSES):
                     nc.scalar.copy(out=t[:, o, :, :], in_=raw[(b, o)][:].rearrange("p j w -> p w j"))
@@ -166,7 +164,7 @@ def tile_picked_yadc_prob_p_kernel(
             tabs[(b, d)] = tab
 
         def table(b, d, scale, place=None):
-            if b == 3:
+            if b in (0, 3):
                 acc = single.tile([P, R], F32, name="acc3", tag="bank%d" % d)
             else:
                 acc = psum.tile([P, R], F32, name="acc")
@@ -174,8 +172,8 @@ def tile_picked_yadc_prob_p_kernel(
             leave(b, d, acc[:], scale, place)
 
         logs = {}
-        totals = keep.tile([P, BOOKS], F32, name="totals", align_bytes=64)
-        shifts = keep.tile([P, BOOKS], F32, name="shifts", align_bytes=64)
+        totals = keep.tile([P, LOGS], F32, name="totals", align_bytes=64)
+        shifts = keep.tile([P, LOGS], F32, name="shifts", align_bytes=64)
 
         log_accs = {}
 
@@ -191,17 +189,15 @@ def tile_picked_yadc_prob_p_kernel(
 
         def log_table(d):
             name = "log%d" % d
-            if d == 0:
-                tab = shared.tile([P, LOG_WINDOW], F32, name=name, offset=0)
-            elif d == BOOKS - 1:
-                tab = shared.tile([P, LOG_WINDOW], F32, name=name, offset=HELD - LOG_WINDOW * 4)
+            if d == 1:
+                tab = shared.tile([P, LOG_WINDOW], F32, name=name, offset=4 * WINDOW - 32)
             else:
                 tab = keep.tile([P, LOG_WINDOW], F32, name=name, align_bytes=64)
             nc.scalar.activation(tab[:, :R], log_accs[d][:], ACT.Ln, bias=shifts[:, d : d + 1], scale=factor[:])
             logs[d] = tab
 
         def look_up(b, d, c0=0, c1=U, tag=None):
-            prev = norm_sb if d == 0 else sums[(b, d - 1, 0)]
+            prev = norm_sb if d == 0 or b == 0 else sums[(b, d - 1, 0)]
             name = "sum%d_%d_%d" % (b, d, c0)
             s = keep.tile([P, c1 - c0], F32, name=name, tag=tag or name, align_bytes=64)
             piece = codes[d][:, c0 // 16 : c1 // 16]
@@ -220,11 +216,11 @@ def tile_picked_yadc_prob_p_kernel(
         pick(1, 0, 1)
         pick(1, 1, 2)
         pick(1, 2, BOOKS)
-        for d in range(BOOKS):
+        for d in range(LOGS):
             shift_of(d)
-            if d < BOOKS - 1:
-                log_table(d)
-        shifts_again = keep.tile([P, BOOKS], F32, name="shifts_again")
+            log_table(d)
+        table(0, LOGS, factor[:])
+        shifts_again = keep.tile([P, LOGS], F32, name="shifts_again")
         unshift = keep.tile([P, 1], F32, name="unshift", tag="unshift", align_bytes=64)
         nc.scalar.activation(shifts_again[:], shifts[:], ACT.Copy, accum_out=unshift[:])
 
@@ -238,24 +234,21 @@ def tile_picked_yadc_prob_p_kernel(
 
         interleave(1, 1)
         quantize(1, 1)
-        table(1, 0, first_factor[:, 0:1])
-        table(1, 1, factor[:])
-        log_table(BOOKS - 1)
-        table(1, 2, factor[:])
-        table(1, 3, factor[:])
+        look_up(0, LOGS)
+        for d in range(BOOKS):
+            table(1, d, factor[:])
         interleave(2, 1)
-        quantize(2, 1)
         look_up(1, 0)
+        quantize(2, 1)
         interleave(3, 1)
         look_up(1, 1)
         quantize(3, 1)
         look_up(1, 2)
-        fetch(0, 1, "factor")
+        fetch(0, 2, "factor")
         for d in range(BOOKS):
             table(2, d, late_factor[:], d)
-        for d in range(BOOKS):
             table(3, d, late_factor[:])
-        fetch(1, BOOKS, "late_factor")
+        fetch(2, LOGS, "late_factor")
         look_up(2, 0)
         look_up(1, 3)
         for d in range(BOOKS - 1):
@@ -263,7 +256,7 @@ def tile_picked_yadc_prob_p_kernel(
             look_up(2, d + 1)
 
         turned = [single.tile([P, P], F32, name="turned%d" % c, tag="bank%d" % c) for c in range(U // P)]
-        terms = [fetched[1], fetched[0], norm_sb[:]] + [fetched[d] for d in range(2, BOOKS)]
+        terms = [sums[(0, LOGS, 0)][:]] + [fetched[d] for d in range(LOGS)]
         for i, term in enumerate(terms):
             for c in range(U // P):
                 nc.tensor.matmul(

@@ -45,8 +45,11 @@ def tile_picked_yadc_prob_p_kernel(
         nc.vector.memset(floor[:], FLOOR)
         factor = keep.tile([P, 1], F32, name="factor", tag="factor", align_bytes=64)
         nc.vector.memset(factor[:], -0.5)
-        late_factor = keep.tile([P, 1], F32, name="late_factor", tag="late_factor", align_bytes=64)
-        nc.vector.memset(late_factor[:], -0.5)
+        late_factor = []
+        for i in range(2):
+            name = "late_factor%d" % i
+            late_factor.append(keep.tile([P, 1], F32, name=name, tag=name, align_bytes=64))
+            nc.vector.memset(late_factor[i][:], -0.5)
         warm = keep.tile([P, 1], F32, name="warm")
         nc.scalar.activation(warm[:], floor[:], ACT.Ln)
         ident = keep.tile([P, P], F32, name="ident", align_bytes=64)
@@ -189,10 +192,7 @@ def tile_picked_yadc_prob_p_kernel(
 
         def log_table(d):
             name = "log%d" % d
-            if d == 1:
-                tab = shared.tile([P, LOG_WINDOW], F32, name=name, offset=4 * WINDOW - 32)
-            else:
-                tab = keep.tile([P, LOG_WINDOW], F32, name=name, align_bytes=64)
+            tab = shared.tile([P, LOG_WINDOW], F32, name=name, offset=(5 * d + 1) * 4 * WINDOW - 32)
             nc.scalar.activation(tab[:, :R], log_accs[d][:], ACT.Ln, bias=shifts[:, d : d + 1], scale=factor[:])
             logs[d] = tab
 
@@ -219,7 +219,7 @@ def tile_picked_yadc_prob_p_kernel(
         for d in range(LOGS):
             shift_of(d)
             log_table(d)
-        table(0, LOGS, factor[:])
+        table(0, LOGS, -0.5)
         shifts_again = keep.tile([P, LOGS], F32, name="shifts_again")
         unshift = keep.tile([P, 1], F32, name="unshift", tag="unshift", align_bytes=64)
         nc.scalar.activation(shifts_again[:], shifts[:], ACT.Copy, accum_out=unshift[:])
@@ -235,20 +235,27 @@ def tile_picked_yadc_prob_p_kernel(
         interleave(1, 1)
         quantize(1, 1)
         look_up(0, LOGS)
-        for d in range(BOOKS):
-            table(1, d, factor[:])
+        table(1, 0, -0.5)
+        table(1, 1, factor[:])
         interleave(2, 1)
         look_up(1, 0)
         quantize(2, 1)
         interleave(3, 1)
         look_up(1, 1)
         quantize(3, 1)
+        fetch(0, 1, "factor")
+        table(1, 2, -0.5, 0)
+        table(2, 0, late_factor[0][:], 1)
+        fetch(1, 2, "late_factor0")
+        table(1, 3, -0.5, 2)
+        for place, (b, d) in enumerate(((3, 0), (2, 1), (3, 1))):
+            table(b, d, -0.5, 5 + place)
+        table(3, 2, -0.5)
+        table(3, 3, late_factor[1][:])
+        fetch(2, LOGS, "late_factor1")
+        table(2, 2, -0.5, 8)
+        table(2, 3, -0.5, 11)
         look_up(1, 2)
-        fetch(0, 2, "factor")
-        for d in range(BOOKS):
-            table(2, d, late_factor[:], d)
-            table(3, d, late_factor[:])
-        fetch(2, LOGS, "late_factor")
         look_up(2, 0)
         look_up(1, 3)
         for d in range(BOOKS - 1):

@@ -10,6 +10,7 @@ PASSES = K // (P * PACK)
 BOOKS = S // R
 WINDOW = U + 16
 LOG_WINDOW = 4 * U
+COPY_WINDOW = 2 * U
 LAST = 64
 FIRST = 512
 LOGS = BOOKS - 1
@@ -65,14 +66,14 @@ def tile_picked_yadc_prob_p_kernel(
         raw = {}
 
         def load_queries(b, n, o):
-            if b == 0:
-                t = keep.tile([P, PACK, P], F32, name="raw0_%d" % o, align_bytes=64)
+            if b < 2:
+                t = keep.tile([P, PACK, n * P], F32, name="raw", tag="raw%d_%d" % (b, o), align_bytes=64)
                 raw[(b, o)] = t
                 dst = t[:]
             else:
                 if o == 0:
-                    raw[b] = keep.tile([P, PASSES, PACK, n * P], F32, name="raw%d" % b, align_bytes=64)
-                dst = raw[b][:, o, :, :]
+                    raw[(b, 0)] = keep.tile([P, PASSES, PACK, P], F32, name="raw%d" % b, align_bytes=64)
+                dst = raw[(b, 0)][:, o, :, :]
             rows = hT[o * P * PACK : (o + 1) * P * PACK, b * P : (b + n) * P]
             nc.sync.dma_start(out=dst, in_=rows.rearrange("(p j) w -> p j w", j=PACK))
 
@@ -89,17 +90,16 @@ def tile_picked_yadc_prob_p_kernel(
                 in_=x_scales[:, 4 * q : 4 * q + 4, :].bitcast(I32),
             )
         load_words(0, FIRST, T)
-        load_queries(0, 1, 0)
-        load_queries(0, 1, 1)
+        load_queries(0, 2, 0)
         load_words(1, 0, T)
-        load_queries(1, 1, 0)
+        load_queries(0, 1, 1)
         load_queries(1, 1, 1)
         codes = {3: load_list("code4_sb", code4, U)}
-        norm_sb = keep.tile([P, U], F32, name="norm_sb", align_bytes=64)
-        nc.sync.dma_start(out=norm_sb[:], in_=norm)
+        codes[0] = load_list("code1_sb", code1, U)
         load_queries(2, 1, 0)
         load_queries(2, 1, 1)
-        codes[0] = load_list("code1_sb", code1, U)
+        norm_sb = keep.tile([P, U], F32, name="norm_sb", align_bytes=64)
+        nc.sync.dma_start(out=norm_sb[:], in_=norm)
         load_queries(3, 1, 0)
         load_queries(3, 1, 1)
         codes[1] = load_list("code2_sb", code2, U)
@@ -109,9 +109,9 @@ def tile_picked_yadc_prob_p_kernel(
         nc.vector.tensor_copy(picked_scales[:], store_scales[:].indirect(offs_sb[:]))
         picked = {}
 
-        def pick(o, d0, d1):
+        def pick(o, d0, d1, tag=None):
             name = "picked%d_%d" % (o, d0)
-            t = keep.tile([P, (d1 - d0) * R], U32, name=name, align_bytes=64)
+            t = keep.tile([P, (d1 - d0) * R], U32, name=name, tag=tag or name, align_bytes=64)
             piece = offs_sb[:, d0 * R // 16 : d1 * R // 16]
             nc.vector.tensor_copy(t[:], words[o][:].bitcast(U32).indirect(piece))
             for d in range(d0, d1):
@@ -120,34 +120,34 @@ def tile_picked_yadc_prob_p_kernel(
         grouped = {}
         quantized = {}
 
-        def interleave(b, n):
-            t = keep.tile([P, PASSES, n * P, PACK], BF16, name="grouped%d" % b, tag="grouped%d" % b, align_bytes=64)
-            if b == 0:
-                for o in range(PASSES):
-                    nc.scalar.copy(out=t[:, o, :, :], in_=raw[(b, o)][:].rearrange("p j w -> p w j"))
+        def interleave(b, o):
+            name = "grouped%d_%d" % (b, o)
+            src = raw[(b, o)]
+            if b < 2:
+                t = keep.tile([P, src.shape[2], PACK], BF16, name=name, align_bytes=64)
+                nc.scalar.copy(out=t[:], in_=src[:].rearrange("p j w -> p w j"))
+                grouped[(b, o)] = t[:].rearrange("p w j -> p (w j)")
             else:
-                nc.vector.tensor_copy(out=t[:], in_=raw[b][:].rearrange("p o j w -> p o w j"))
-            grouped[b] = t
+                t = keep.tile([P, PASSES, P, PACK], BF16, name=name, align_bytes=64)
+                nc.vector.tensor_copy(out=t[:], in_=src[:].rearrange("p o j w -> p o w j"))
+                grouped[(b, o)] = t[:].rearrange("p o w j -> p (o w j)")
 
-        def quantize(b, n):
-            q_codes = keep.tile([P, PASSES, n * P], U32, name="q_codes%d" % b, align_bytes=64)
-            q_scales = keep.tile([P, PASSES, n * P], U8, name="q_scales%d" % b, align_bytes=64)
-            nc.vector.quantize_mx(
-                out=q_codes[:].rearrange("p o w -> p (o w)").bitcast(FP8X4),
-                scales=q_scales[:].rearrange("p o w -> p (o w)"),
-                in_=grouped[b][:].rearrange("p o w j -> p (o w j)"),
-            )
-            for i in range(n):
-                quantized[b + i] = (q_codes, q_scales, slice(i * P, (i + 1) * P))
+        def quantize(*parts):
+            name = "%d_%d" % parts[0]
+            q_codes = keep.tile([P, len(parts) * P], U32, name="q_codes" + name, align_bytes=64)
+            q_scales = keep.tile([P, len(parts) * P], U8, name="q_scales" + name, align_bytes=64)
+            nc.vector.quantize_mx(out=q_codes[:].bitcast(FP8X4), scales=q_scales[:], in_=grouped[parts[0]])
+            for i, part in enumerate(parts):
+                quantized[part] = (q_codes[:, i * P : (i + 1) * P], q_scales[:, i * P : (i + 1) * P])
 
         def product(acc, b, d0, d1):
-            q_codes, q_scales, cols = quantized[b]
             for o in range(PASSES):
+                q_codes, q_scales = quantized[(b, o)]
                 t, first = picked[(o, d0)]
                 nc.tensor.matmul_mx(
                     out=acc[:],
-                    lhsT=q_codes[:, o, cols].bitcast(FP8X4),
-                    lhsT_scale=q_scales[:, o, cols],
+                    lhsT=q_codes.bitcast(FP8X4),
+                    lhsT_scale=q_scales,
                     rhs=t[:, (d0 - first) * R : (d1 - first) * R].bitcast(FP8X4),
                     rhs_scale=picked_scales[4 * o : P, d0 * R : d1 * R],
                     start=(o == 0),
@@ -160,7 +160,7 @@ def tile_picked_yadc_prob_p_kernel(
         def leave(b, d, acc, scale, place):
             name = "tab%d_%d" % (b, d)
             if place is None:
-                tab = keep.tile([P, WINDOW], F32, name=name, align_bytes=64)
+                tab = keep.tile([P, COPY_WINDOW if b == 0 else WINDOW], F32, name=name, align_bytes=64)
             else:
                 tab = shared.tile([P, WINDOW], F32, name=name, offset=place * WINDOW * 4)
             nc.scalar.activation(tab[:, :R], acc, ACT.Copy, scale=scale)
@@ -197,7 +197,7 @@ def tile_picked_yadc_prob_p_kernel(
             logs[d] = tab
 
         def look_up(b, d, c0=0, c1=U, tag=None):
-            prev = norm_sb if d == 0 or b == 0 else sums[(b, d - 1, 0)]
+            prev = norm_sb if d == 0 else sums[(b, d - 1, 0)]
             name = "sum%d_%d_%d" % (b, d, c0)
             s = keep.tile([P, c1 - c0], F32, name=name, tag=tag or name, align_bytes=64)
             piece = codes[d][:, c0 // 16 : c1 // 16]
@@ -211,15 +211,20 @@ def tile_picked_yadc_prob_p_kernel(
             queue.dma_start(out=out[b * P : (b + 1) * P, c0:c1], in_=res[:])
 
         pick(0, 0, BOOKS)
-        interleave(0, 1)
-        quantize(0, 1)
-        pick(1, 0, 1)
-        pick(1, 1, 2)
+        interleave(0, 0)
+        quantize((0, 0), (1, 0))
         pick(1, 2, BOOKS)
-        for d in range(LOGS):
+        pick(1, 0, 1)
+        interleave(0, 1)
+        quantize((0, 1))
+        pick(1, 1, 2, "raw0_1")
+        interleave(1, 1)
+        table(0, LOGS, -0.5)
+        shift_of(2)
+        log_table(2)
+        for d in range(2):
             shift_of(d)
             log_table(d)
-        table(0, LOGS, -0.5)
         shifts_again = keep.tile([P, LOGS], F32, name="shifts_again")
         unshift = keep.tile([P, 1], F32, name="unshift", tag="unshift", align_bytes=64)
         nc.scalar.activation(shifts_again[:], shifts[:], ACT.Copy, accum_out=unshift[:])
@@ -232,19 +237,19 @@ def tile_picked_yadc_prob_p_kernel(
                 nc.scalar.activation(t[:, d - d0, :], logs[d][:].indirect(codes[d][:]), ACT.Exp)
                 fetched[d] = t[:, d - d0, :]
 
-        interleave(1, 1)
-        quantize(1, 1)
-        look_up(0, LOGS)
+        quantize((1, 1))
+        copied = keep.tile([P, U], F32, name="copied", align_bytes=64)
+        nc.vector.tensor_copy(copied[:], tabs[(0, LOGS)][:].indirect(codes[LOGS][:]))
         table(1, 0, -0.5)
-        table(1, 1, factor[:])
-        interleave(2, 1)
+        table(1, 1, -0.5)
+        table(1, 2, factor[:])
+        interleave(2, 0)
         look_up(1, 0)
-        quantize(2, 1)
-        interleave(3, 1)
+        quantize((2, 0), (2, 1))
+        interleave(3, 0)
         look_up(1, 1)
-        quantize(3, 1)
+        quantize((3, 0), (3, 1))
         fetch(0, 1, "factor")
-        table(1, 2, -0.5, 0)
         table(2, 0, late_factor[0][:], 1)
         fetch(1, 2, "late_factor0")
         table(1, 3, -0.5, 2)
@@ -263,7 +268,7 @@ def tile_picked_yadc_prob_p_kernel(
             look_up(2, d + 1)
 
         turned = [single.tile([P, P], F32, name="turned%d" % c, tag="bank%d" % c) for c in range(U // P)]
-        terms = [sums[(0, LOGS, 0)][:]] + [fetched[d] for d in range(LOGS)]
+        terms = [copied[:], norm_sb[:]] + [fetched[d] for d in range(LOGS)]
         for i, term in enumerate(terms):
             for c in range(U // P):
                 nc.tensor.matmul(

@@ -8,15 +8,17 @@ P = 128
 PACK = 4
 PASSES = K // (P * PACK)
 BOOKS = S // R
-WINDOW = U + 16
-LOG_WINDOW = 4 * U
+LOG_BOOKS = BOOKS - 1
+ADD_WINDOW = U + 16
 COPY_WINDOW = 2 * U
-LAST = 64
-FIRST = 512
-LOGS = BOOKS - 1
+EXP_WINDOW = 4 * U
+TABLE_BYTES = 4 * ADD_WINDOW
+LOG_STRIDE = 4 * TABLE_BYTES
+FIRST_WORDS = 512
+LAST_PIECE = 64
 MARGIN = 33.0 / 64.0
-FLOOR = 1.0 / 16.0
-ROOT_BITS = float(127 << 22)
+FLOOR_SEED = 17.0 / 16.0
+HALF_BIAS_BITS = float(127 << 22)
 FLOPS = 2 * K * V * S
 
 F32 = mybir.dt.float32
@@ -36,230 +38,211 @@ def tile_picked_yadc_prob_p_kernel(
     nc = tc.nc
     with ExitStack() as ctx:
         keep = ctx.enter_context(tc.tile_pool(name="keep", bufs=1))
-        shared = ctx.enter_context(tc.tile_pool(name="shared", bufs=1))
-        psum = ctx.enter_context(tc.psum_pool(name="psum", bufs=4))
-        single = ctx.enter_context(tc.psum_pool(name="single", bufs=1))
+        placed = ctx.enter_context(tc.tile_pool(name="placed", bufs=1))
+        rotating = ctx.enter_context(tc.psum_pool(name="rotating", bufs=4))
+        named = ctx.enter_context(tc.psum_pool(name="named", bufs=1))
 
         store_scales = keep.tile([P, T], U8, name="store_scales", align_bytes=64)
         nc.vector.memset(store_scales[:].bitcast(I32), 0)
+        seed = keep.tile([P, 1], F32, name="seed")
+        nc.vector.memset(seed[:], FLOOR_SEED)
+        factors = []
+        for d in range(LOG_BOOKS):
+            factors.append(keep.tile([P, 1], F32, name="factor", tag="factor%d" % d, align_bytes=64))
+            nc.vector.memset(factors[d][:], -0.5)
         floor = keep.tile([P, 1], F32, name="floor")
-        nc.vector.memset(floor[:], FLOOR)
-        factor = keep.tile([P, 1], F32, name="factor", tag="factor", align_bytes=64)
-        nc.vector.memset(factor[:], -0.5)
-        late_factor = []
-        for i in range(2):
-            name = "late_factor%d" % i
-            late_factor.append(keep.tile([P, 1], F32, name=name, tag=name, align_bytes=64))
-            nc.vector.memset(late_factor[i][:], -0.5)
-        warm = keep.tile([P, 1], F32, name="warm")
-        nc.scalar.activation(warm[:], floor[:], ACT.Ln)
-        ident = keep.tile([P, P], F32, name="ident", align_bytes=64)
-        nc.vector.memset(ident[:], 0.0)
-        make_identity(nc, ident[:], nomemset=True)
+        nc.scalar.activation(floor[:], seed[:], ACT.Ln)
+        identity = keep.tile([P, P], F32, name="identity", align_bytes=64)
+        nc.vector.memset(identity[:], 0.0)
+        make_identity(nc, identity[:], nomemset=True)
 
-        words = [keep.tile([P, T], I32, name="store_words%d" % o, align_bytes=64) for o in range(PASSES)]
+        store_words = [keep.tile([P, T], I32, name="store_words%d" % o, align_bytes=64) for o in range(PASSES)]
 
         def load_words(o, c0, c1):
             src = x_words[o].rearrange("p n t -> p (n t)").bitcast(I32)
-            nc.sync.dma_start(out=words[o][:, c0:c1], in_=src[:, c0:c1])
+            nc.sync.dma_start(out=store_words[o][:, c0:c1], in_=src[:, c0:c1])
 
-        raw = {}
-
-        def load_queries(b, n, o):
-            if b < 2:
-                t = keep.tile([P, PACK, n * P], F32, name="raw", tag="raw%d_%d" % (b, o), align_bytes=64)
-                raw[(b, o)] = t
-                dst = t[:]
-            else:
-                if o == 0:
-                    raw[(b, 0)] = keep.tile([P, PASSES, PACK, P], F32, name="raw%d" % b, align_bytes=64)
-                dst = raw[(b, 0)][:, o, :, :]
-            rows = hT[o * P * PACK : (o + 1) * P * PACK, b * P : (b + n) * P]
+        def load_rows(dst, o, b0, b1):
+            rows = hT[o * P * PACK : (o + 1) * P * PACK, b0 * P : b1 * P]
             nc.sync.dma_start(out=dst, in_=rows.rearrange("(p j) w -> p j w", j=PACK))
 
-        def load_list(name, src, n):
-            t = keep.tile([P, n // 16], U16, name=name)
-            nc.sync.dma_start(t[:], src)
-            return t
+        def load_pass(name, o, b0, b1):
+            raw = keep.tile([P, PACK, (b1 - b0) * P], F32, name="raw", tag=name, align_bytes=64)
+            load_rows(raw[:], o, b0, b1)
+            return raw
 
-        load_words(0, 0, FIRST)
+        def load_batch(b):
+            raw = keep.tile([P, PASSES, PACK, P], F32, name="raw_batch%d" % b, align_bytes=64)
+            for o in range(PASSES):
+                load_rows(raw[:, o, :, :], o, b, b + 1)
+            return raw
+
+        def load_list(name, src, n):
+            offsets = keep.tile([P, n // 16], U16, name=name)
+            nc.sync.dma_start(offsets[:], src)
+            return offsets
+
+        load_words(0, 0, FIRST_WORDS)
         offs_sb = load_list("offs_sb", offs, S)
         for q in (2, 3, 0, 1):
             nc.sync.dma_start(
                 out=store_scales[32 * q : 32 * q + 4 * PASSES, :].bitcast(I32),
                 in_=x_scales[:, 4 * q : 4 * q + 4, :].bitcast(I32),
             )
-        load_words(0, FIRST, T)
-        load_queries(0, 2, 0)
+        load_words(0, FIRST_WORDS, T)
+        raw_pass0 = load_pass("raw_pass0", 0, 0, 2)
         load_words(1, 0, T)
-        load_queries(0, 1, 1)
-        load_queries(1, 1, 1)
+        raw_pass1 = [load_pass("raw_pass1_%d" % b, 1, b, b + 1) for b in range(2)]
         codes = {3: load_list("code4_sb", code4, U)}
         codes[0] = load_list("code1_sb", code1, U)
-        load_queries(2, 1, 0)
-        load_queries(2, 1, 1)
+        raw_batch2 = load_batch(2)
         norm_sb = keep.tile([P, U], F32, name="norm_sb", align_bytes=64)
         nc.sync.dma_start(out=norm_sb[:], in_=norm)
-        load_queries(3, 1, 0)
-        load_queries(3, 1, 1)
+        raw_batch3 = load_batch(3)
         codes[1] = load_list("code2_sb", code2, U)
         codes[2] = load_list("code3_sb", code3, U)
 
         picked_scales = keep.tile([P, S], U8, name="picked_scales", align_bytes=64)
         nc.vector.tensor_copy(picked_scales[:], store_scales[:].indirect(offs_sb[:]))
-        picked = {}
+        picked_words = {}
 
         def pick(o, d0, d1, tag=None):
             name = "picked%d_%d" % (o, d0)
-            t = keep.tile([P, (d1 - d0) * R], U32, name=name, tag=tag or name, align_bytes=64)
+            words = keep.tile([P, (d1 - d0) * R], U32, name=name, tag=tag or name, align_bytes=64)
             piece = offs_sb[:, d0 * R // 16 : d1 * R // 16]
-            nc.vector.tensor_copy(t[:], words[o][:].bitcast(U32).indirect(piece))
+            nc.vector.tensor_copy(words[:], store_words[o][:].bitcast(U32).indirect(piece))
             for d in range(d0, d1):
-                picked[(o, d)] = (t, d0)
+                picked_words[(o, d)] = words[:, (d - d0) * R : (d - d0 + 1) * R]
 
-        grouped = {}
+        def round_pass(name, raw):
+            grouped = keep.tile([P, raw.shape[2], PACK], BF16, name=name, align_bytes=64)
+            nc.scalar.copy(out=grouped[:], in_=raw[:].rearrange("p j w -> p w j"))
+            return grouped[:].rearrange("p w j -> p (w j)")
+
+        def round_batch(name, raw):
+            grouped = keep.tile([P, PASSES, P, PACK], BF16, name=name, align_bytes=64)
+            nc.vector.tensor_copy(out=grouped[:], in_=raw[:].rearrange("p o j w -> p o w j"))
+            return grouped[:].rearrange("p o w j -> p (o w j)")
+
         quantized = {}
 
-        def interleave(b, o):
-            name = "grouped%d_%d" % (b, o)
-            src = raw[(b, o)]
-            if b < 2:
-                t = keep.tile([P, src.shape[2], PACK], BF16, name=name, align_bytes=64)
-                nc.scalar.copy(out=t[:], in_=src[:].rearrange("p j w -> p w j"))
-                grouped[(b, o)] = t[:].rearrange("p w j -> p (w j)")
-            else:
-                t = keep.tile([P, PASSES, P, PACK], BF16, name=name, align_bytes=64)
-                nc.vector.tensor_copy(out=t[:], in_=src[:].rearrange("p o j w -> p o w j"))
-                grouped[(b, o)] = t[:].rearrange("p o w j -> p (o w j)")
-
-        def quantize(*parts):
+        def quantize(grouped, parts):
             name = "%d_%d" % parts[0]
-            q_codes = keep.tile([P, len(parts) * P], U32, name="q_codes" + name, align_bytes=64)
+            q_words = keep.tile([P, len(parts) * P], U32, name="q_words" + name, align_bytes=64)
             q_scales = keep.tile([P, len(parts) * P], U8, name="q_scales" + name, align_bytes=64)
-            nc.vector.quantize_mx(out=q_codes[:].bitcast(FP8X4), scales=q_scales[:], in_=grouped[parts[0]])
+            nc.vector.quantize_mx(out=q_words[:].bitcast(FP8X4), scales=q_scales[:], in_=grouped)
             for i, part in enumerate(parts):
-                quantized[part] = (q_codes[:, i * P : (i + 1) * P], q_scales[:, i * P : (i + 1) * P])
+                quantized[part] = (q_words[:, i * P : (i + 1) * P], q_scales[:, i * P : (i + 1) * P])
 
-        def product(acc, b, d0, d1):
+        def product(b, d):
+            if b in (0, 3):
+                acc = named.tile([P, R], F32, name="named_acc", tag="bank%d" % d)
+            else:
+                acc = rotating.tile([P, R], F32, name="acc")
             for o in range(PASSES):
-                q_codes, q_scales = quantized[(b, o)]
-                t, first = picked[(o, d0)]
+                q_words, q_scales = quantized[(b, o)]
                 nc.tensor.matmul_mx(
                     out=acc[:],
-                    lhsT=q_codes.bitcast(FP8X4),
+                    lhsT=q_words.bitcast(FP8X4),
                     lhsT_scale=q_scales,
-                    rhs=t[:, (d0 - first) * R : (d1 - first) * R].bitcast(FP8X4),
-                    rhs_scale=picked_scales[4 * o : P, d0 * R : d1 * R],
+                    rhs=picked_words[(o, d)].bitcast(FP8X4),
+                    rhs_scale=picked_scales[4 * o : P, d * R : (d + 1) * R],
                     start=(o == 0),
                     stop=(o == PASSES - 1),
                 )
+            return acc
 
-        tabs = {}
-        sums = {}
+        tables = {}
 
-        def leave(b, d, acc, scale, place):
-            name = "tab%d_%d" % (b, d)
-            if place is None:
-                tab = keep.tile([P, COPY_WINDOW if b == 0 else WINDOW], F32, name=name, align_bytes=64)
+        def table(b, d, scale=-0.5, behind=None):
+            acc = product(b, d)
+            name = "table%d_%d" % (b, d)
+            if behind is None:
+                tab = keep.tile([P, COPY_WINDOW if b == 0 else ADD_WINDOW], F32, name=name, align_bytes=64)
             else:
-                tab = shared.tile([P, WINDOW], F32, name=name, offset=place * WINDOW * 4)
-            nc.scalar.activation(tab[:, :R], acc, ACT.Copy, scale=scale)
-            tabs[(b, d)] = tab
+                offset = behind[0] * LOG_STRIDE + behind[1] * TABLE_BYTES
+                tab = placed.tile([P, ADD_WINDOW], F32, name=name, offset=offset)
+            nc.scalar.activation(tab[:, :R], acc[:], ACT.Copy, scale=scale)
+            tables[(b, d)] = tab
 
-        def table(b, d, scale, place=None):
-            if b in (0, 3):
-                acc = single.tile([P, R], F32, name="acc3", tag="bank%d" % d)
-            else:
-                acc = psum.tile([P, R], F32, name="acc")
-            product(acc, b, d, d + 1)
-            leave(b, d, acc[:], scale, place)
-
-        logs = {}
-        totals = keep.tile([P, LOGS], F32, name="totals", align_bytes=64)
-        shifts = keep.tile([P, LOGS], F32, name="shifts", align_bytes=64)
-
-        log_accs = {}
-
-        def shift_of(d):
-            acc = single.tile([P, R], F32, name="log_acc", tag="bank%d" % d)
-            product(acc, 0, d, d + 1)
-            squares = keep.tile([P, R], BF16, name="squares%d" % d, align_bytes=64)
-            total = totals[:, d : d + 1]
-            nc.scalar.activation(squares[:], acc[:], ACT.Square, bias=floor[:], scale=MARGIN, accum_out=total)
-            shift = shifts[:, d : d + 1]
-            nc.scalar.activation(shift.bitcast(U32), total.bitcast(U32), ACT.Copy, bias=ROOT_BITS, scale=0.5)
-            log_accs[d] = acc
+        log_tables = {}
+        square_sums = keep.tile([P, LOG_BOOKS], F32, name="square_sums", align_bytes=64)
+        shifts = keep.tile([P, LOG_BOOKS], F32, name="shifts", align_bytes=64)
 
         def log_table(d):
-            name = "log%d" % d
-            tab = shared.tile([P, LOG_WINDOW], F32, name=name, offset=(5 * d + 1) * 4 * WINDOW - 32)
-            nc.scalar.activation(tab[:, :R], log_accs[d][:], ACT.Ln, bias=shifts[:, d : d + 1], scale=factor[:])
-            logs[d] = tab
-
-        def look_up(b, d, c0=0, c1=U, tag=None):
-            prev = norm_sb if d == 0 else sums[(b, d - 1, 0)]
-            name = "sum%d_%d_%d" % (b, d, c0)
-            s = keep.tile([P, c1 - c0], F32, name=name, tag=tag or name, align_bytes=64)
-            piece = codes[d][:, c0 // 16 : c1 // 16]
-            nc.vector.tensor_tensor(s[:], tabs[(b, d)][:].indirect(piece), prev[:, c0:c1], ADD)
-            sums[(b, d, c0)] = s
-
-        def finish(b, c0=0, c1=U, queue=nc.sync, tag=None):
-            name = "res%d_%d" % (b, c0)
-            res = keep.tile([P, c1 - c0], F32, name=name, tag=tag or name, align_bytes=64)
-            nc.scalar.activation(res[:], sums[(b, BOOKS - 1, c0)][:], ACT.Sigmoid, scale=-1.0)
-            queue.dma_start(out=out[b * P : (b + 1) * P, c0:c1], in_=res[:])
-
-        pick(0, 0, BOOKS)
-        interleave(0, 0)
-        quantize((0, 0), (1, 0))
-        pick(1, 2, BOOKS)
-        pick(1, 0, 1)
-        interleave(0, 1)
-        quantize((0, 1))
-        pick(1, 1, 2, "raw0_1")
-        interleave(1, 1)
-        table(0, LOGS, -0.5)
-        shift_of(2)
-        log_table(2)
-        for d in range(2):
-            shift_of(d)
-            log_table(d)
-        shifts_again = keep.tile([P, LOGS], F32, name="shifts_again")
-        unshift = keep.tile([P, 1], F32, name="unshift", tag="unshift", align_bytes=64)
-        nc.scalar.activation(shifts_again[:], shifts[:], ACT.Copy, accum_out=unshift[:])
+            acc = product(0, d)
+            squares = keep.tile([P, R], BF16, name="squares%d" % d, align_bytes=64)
+            square_sum = square_sums[:, d : d + 1]
+            nc.scalar.activation(squares[:], acc[:], ACT.Square, bias=floor[:], scale=MARGIN, accum_out=square_sum)
+            shift = shifts[:, d : d + 1]
+            nc.scalar.activation(
+                shift.bitcast(U32), square_sum.bitcast(U32), ACT.Copy, bias=HALF_BIAS_BITS, scale=0.5
+            )
+            tab = placed.tile([P, EXP_WINDOW], F32, name="log_table%d" % d, offset=d * LOG_STRIDE)
+            nc.scalar.activation(tab[:, :R], acc[:], ACT.Ln, bias=shift, scale=factors[0][:])
+            log_tables[d] = tab
 
         fetched = {}
 
-        def fetch(d0, d1, tag):
-            t = keep.tile([P, d1 - d0, U], F32, name="fetched%d" % d0, tag=tag, align_bytes=64)
-            for d in range(d0, d1):
-                nc.scalar.activation(t[:, d - d0, :], logs[d][:].indirect(codes[d][:]), ACT.Exp)
-                fetched[d] = t[:, d - d0, :]
+        def exp_gather(d):
+            fetched[d] = keep.tile([P, U], F32, name="fetched", tag="factor%d" % d, align_bytes=64)
+            nc.scalar.activation(fetched[d][:], log_tables[d][:].indirect(codes[d][:]), ACT.Exp)
 
-        quantize((1, 1))
-        copied = keep.tile([P, U], F32, name="copied", align_bytes=64)
-        nc.vector.tensor_copy(copied[:], tabs[(0, LOGS)][:].indirect(codes[LOGS][:]))
-        table(1, 0, -0.5)
-        table(1, 1, -0.5)
-        table(1, 2, factor[:])
-        interleave(2, 0)
+        sums = {}
+
+        def look_up(b, d, c0=0, c1=U):
+            before = norm_sb if d == 0 else sums[(b, d - 1, 0)]
+            name = "sum%d_%d_%d" % (b, d, c0)
+            total = keep.tile([P, c1 - c0], F32, name=name, tag=name, align_bytes=64)
+            piece = codes[d][:, c0 // 16 : c1 // 16]
+            nc.vector.tensor_tensor(total[:], tables[(b, d)][:].indirect(piece), before[:, c0:c1], ADD)
+            sums[(b, d, c0)] = total
+
+        def finish(b, total, tag, **bias):
+            result = keep.tile([P, U], F32, name="result%d" % b, tag=tag, align_bytes=64)
+            nc.scalar.activation(result[:], total[:], ACT.Sigmoid, scale=-1.0, **bias)
+            nc.sync.dma_start(out=out[b * P : (b + 1) * P, :], in_=result[:])
+
+        pick(0, 0, BOOKS)
+        quantize(round_pass("grouped_pass0", raw_pass0), [(0, 0), (1, 0)])
+        pick(1, 2, BOOKS)
+        pick(1, 0, 1)
+        quantize(round_pass("grouped_pass1_0", raw_pass1[0]), [(0, 1)])
+        pick(1, 1, 2, "raw_pass1_0")
+        grouped_pass1_1 = round_pass("grouped_pass1_1", raw_pass1[1])
+        table(0, LOG_BOOKS)
+        for d in (2, 0, 1):
+            log_table(d)
+        shifts_copy = keep.tile([P, LOG_BOOKS], F32, name="shifts_copy")
+        shift_sum = keep.tile([P, 1], F32, name="shift_sum", tag="shift_sum", align_bytes=64)
+        nc.scalar.activation(shifts_copy[:], shifts[:], ACT.Copy, accum_out=shift_sum[:])
+
+        quantize(grouped_pass1_1, [(1, 1)])
+        fetched[LOG_BOOKS] = keep.tile([P, U], F32, name="copied", align_bytes=64)
+        nc.vector.tensor_copy(fetched[LOG_BOOKS][:], tables[(0, LOG_BOOKS)][:].indirect(codes[LOG_BOOKS][:]))
+        table(1, 0)
+        table(1, 1)
+        table(1, 2, factors[0][:])
+        grouped_batch2 = round_batch("grouped_batch2", raw_batch2)
         look_up(1, 0)
-        quantize((2, 0), (2, 1))
-        interleave(3, 0)
+        quantize(grouped_batch2, [(2, 0), (2, 1)])
+        grouped_batch3 = round_batch("grouped_batch3", raw_batch3)
         look_up(1, 1)
-        quantize((3, 0), (3, 1))
-        fetch(0, 1, "factor")
-        table(2, 0, late_factor[0][:], 1)
-        fetch(1, 2, "late_factor0")
-        table(1, 3, -0.5, 2)
-        for place, (b, d) in enumerate(((3, 0), (2, 1), (3, 1))):
-            table(b, d, -0.5, 5 + place)
-        table(3, 2, -0.5)
-        table(3, 3, late_factor[1][:])
-        fetch(2, LOGS, "late_factor1")
-        table(2, 2, -0.5, 8)
-        table(2, 3, -0.5, 11)
+        quantize(grouped_batch3, [(3, 0), (3, 1)])
+
+        exp_gather(0)
+        table(2, 0, factors[1][:], behind=(0, 0))
+        exp_gather(1)
+        table(1, 3, behind=(0, 1))
+        table(3, 0, behind=(1, 0))
+        table(2, 1, behind=(1, 1))
+        table(3, 1, behind=(1, 2))
+        table(3, 2)
+        table(3, 3, factors[2][:])
+        exp_gather(2)
+        table(2, 2, behind=(1, 3))
+        table(2, 3, behind=(2, 0))
+
         look_up(1, 2)
         look_up(2, 0)
         look_up(1, 3)
@@ -267,32 +250,33 @@ def tile_picked_yadc_prob_p_kernel(
             look_up(3, d)
             look_up(2, d + 1)
 
-        turned = [single.tile([P, P], F32, name="turned%d" % c, tag="bank%d" % c) for c in range(U // P)]
-        terms = [copied[:], norm_sb[:]] + [fetched[d] for d in range(LOGS)]
+        runs = [slice(c * P, (c + 1) * P) for c in range(U // P)]
+        turned = [named.tile([P, P], F32, name="turned", tag="bank%d" % c) for c in range(len(runs))]
+        terms = [fetched[LOG_BOOKS], norm_sb] + [fetched[d] for d in range(LOG_BOOKS)]
         for i, term in enumerate(terms):
-            for c in range(U // P):
+            for c, run in enumerate(runs):
                 nc.tensor.matmul(
                     turned[c][:],
-                    term[:, c * P : (c + 1) * P],
-                    ident[:],
+                    term[:, run],
+                    identity[:],
                     start=(i == 0),
                     stop=(i == len(terms) - 1),
                     is_transpose=True,
                 )
-        turned_sb = keep.tile([P, U // P, P], F32, name="turned_sb", align_bytes=64)
-        back = psum.tile([P, U], F32, name="acc")
-        for c in range(U // P):
-            nc.scalar.copy(out=turned_sb[:, c, :], in_=turned[c][:])
-            nc.tensor.transpose(back[:, c * P : (c + 1) * P], turned_sb[:, c, :], ident[:])
-        res0 = keep.tile([P, U], F32, name="res0", align_bytes=64)
-        nc.scalar.activation(res0[:], back[:], ACT.Sigmoid, bias=unshift[:], scale=-1.0)
-        nc.sync.dma_start(out=out[0:P, :], in_=res0[:])
-        finish(1, tag="unshift")
-        finish(2, tag="sum1_3_0")
-        res3 = keep.tile([P, U], F32, name="res3", tag="sum2_3_0", align_bytes=64)
-        cuts = (0, U // 2, U - LAST, U)
+        turned_sb = keep.tile([P, U], F32, name="turned_sb", align_bytes=64)
+        shifted_total = rotating.tile([P, U], F32, name="acc")
+        for c, run in enumerate(runs):
+            nc.scalar.copy(out=turned_sb[:, run], in_=turned[c][:])
+            nc.tensor.transpose(shifted_total[:, run], turned_sb[:, run], identity[:])
+
+        last = BOOKS - 1
+        finish(0, shifted_total, "result0", bias=shift_sum[:])
+        finish(1, sums[(1, last, 0)], "shift_sum")
+        finish(2, sums[(2, last, 0)], "sum1_%d_0" % last)
+        result3 = keep.tile([P, U], F32, name="result3", tag="sum2_%d_0" % last, align_bytes=64)
+        cuts = (0, U // 2, U - LAST_PIECE, U)
         for c0, c1 in zip(cuts, cuts[1:]):
-            look_up(3, BOOKS - 1, c0, c1)
-            nc.scalar.activation(res3[:, c0:c1], sums[(3, BOOKS - 1, c0)][:], ACT.Sigmoid, scale=-1.0)
+            look_up(3, last, c0, c1)
+            nc.scalar.activation(result3[:, c0:c1], sums[(3, last, c0)][:], ACT.Sigmoid, scale=-1.0)
             queue = nc.scalar if c1 == U else nc.sync
-            queue.dma_start(out=out[3 * P : 4 * P, c0:c1], in_=res3[:, c0:c1])
+            queue.dma_start(out=out[3 * P : 4 * P, c0:c1], in_=result3[:, c0:c1])

@@ -8,17 +8,10 @@ P = 128
 PACK = 4
 PASSES = K // (P * PACK)
 BOOKS = S // R
-LOG_BOOKS = BOOKS - 1
-ADD_WINDOW = U + 16
-COPY_WINDOW = 2 * U
-EXP_WINDOW = 4 * U
-TABLE_BYTES = 4 * ADD_WINDOW
-LOG_STRIDE = 4 * TABLE_BYTES
+SHARE = 128
+WINDOW = U + 16
 FIRST_WORDS = 512
 LAST_PIECE = 64
-MARGIN = 33.0 / 64.0
-FLOOR_SEED = 17.0 / 16.0
-HALF_BIAS_BITS = float(127 << 22)
 FLOPS = 2 * K * V * S
 
 F32 = mybir.dt.float32
@@ -38,20 +31,17 @@ def tile_picked_yadc_prob_p_kernel(
     nc = tc.nc
     with ExitStack() as ctx:
         keep = ctx.enter_context(tc.tile_pool(name="keep", bufs=1))
-        placed = ctx.enter_context(tc.tile_pool(name="placed", bufs=1))
         rotating = ctx.enter_context(tc.psum_pool(name="rotating", bufs=4))
         named = ctx.enter_context(tc.psum_pool(name="named", bufs=1))
 
         store_scales = keep.tile([P, T], U8, name="store_scales", align_bytes=64)
         nc.vector.memset(store_scales[:].bitcast(I32), 0)
-        seed = keep.tile([P, 1], F32, name="seed")
-        nc.vector.memset(seed[:], FLOOR_SEED)
-        factors = []
-        for d in range(LOG_BOOKS):
-            factors.append(keep.tile([P, 1], F32, name="factor", tag="factor%d" % d, align_bytes=64))
-            nc.vector.memset(factors[d][:], -0.5)
-        floor = keep.tile([P, 1], F32, name="floor")
-        nc.scalar.activation(floor[:], seed[:], ACT.Ln)
+        zero = keep.tile([P, 1], F32, name="zero")
+        nc.vector.memset(zero[:], 0.0)
+        half = keep.tile([P, 1], F32, name="half")
+        nc.scalar.activation(half[:], zero[:], ACT.Sigmoid)
+        factor = keep.tile([P, 1], F32, name="factor", align_bytes=64)
+        nc.scalar.activation(factor[:], half[:], ACT.Copy, scale=-1.0)
         identity = keep.tile([P, P], F32, name="identity", align_bytes=64)
         nc.vector.memset(identity[:], 0.0)
         make_identity(nc, identity[:], nomemset=True)
@@ -92,15 +82,15 @@ def tile_picked_yadc_prob_p_kernel(
         load_words(0, FIRST_WORDS, T)
         raw_pass0 = load_pass("raw_pass0", 0, 0, 2)
         load_words(1, 0, T)
-        raw_pass1 = [load_pass("raw_pass1_%d" % b, 1, b, b + 1) for b in range(2)]
-        codes = {3: load_list("code4_sb", code4, U)}
-        codes[0] = load_list("code1_sb", code1, U)
+        raw_pass1 = {b: load_pass("raw_pass1_%d" % b, 1, b, b + 1) for b in (1, 0)}
+        codes = {0: load_list("code1_sb", code1, U)}
+        codes[1] = load_list("code2_sb", code2, U)
         raw_batch2 = load_batch(2)
         norm_sb = keep.tile([P, U], F32, name="norm_sb", align_bytes=64)
         nc.sync.dma_start(out=norm_sb[:], in_=norm)
         raw_batch3 = load_batch(3)
-        codes[1] = load_list("code2_sb", code2, U)
         codes[2] = load_list("code3_sb", code3, U)
+        codes[3] = load_list("code4_sb", code4, U)
 
         picked_scales = keep.tile([P, S], U8, name="picked_scales", align_bytes=64)
         nc.vector.tensor_copy(picked_scales[:], store_scales[:].indirect(offs_sb[:]))
@@ -154,129 +144,108 @@ def tile_picked_yadc_prob_p_kernel(
 
         tables = {}
 
-        def table(b, d, scale=-0.5, behind=None):
+        def table(b, d, scale=-0.5):
             acc = product(b, d)
-            name = "table%d_%d" % (b, d)
-            if behind is None:
-                tab = keep.tile([P, COPY_WINDOW if b == 0 else ADD_WINDOW], F32, name=name, align_bytes=64)
-            else:
-                offset = behind[0] * LOG_STRIDE + behind[1] * TABLE_BYTES
-                tab = placed.tile([P, ADD_WINDOW], F32, name=name, offset=offset)
+            tab = keep.tile([P, WINDOW], F32, name="table%d_%d" % (b, d), align_bytes=64)
             nc.scalar.activation(tab[:, :R], acc[:], ACT.Copy, scale=scale)
             tables[(b, d)] = tab
 
-        log_tables = {}
-        square_sums = keep.tile([P, LOG_BOOKS], F32, name="square_sums", align_bytes=64)
-        shifts = keep.tile([P, LOG_BOOKS], F32, name="shifts", align_bytes=64)
-
-        def log_table(d):
-            acc = product(0, d)
-            squares = keep.tile([P, R], BF16, name="squares%d" % d, align_bytes=64)
-            square_sum = square_sums[:, d : d + 1]
-            nc.scalar.activation(squares[:], acc[:], ACT.Square, bias=floor[:], scale=MARGIN, accum_out=square_sum)
-            shift = shifts[:, d : d + 1]
-            nc.scalar.activation(
-                shift.bitcast(U32), square_sum.bitcast(U32), ACT.Copy, bias=HALF_BIAS_BITS, scale=0.5
-            )
-            tab = placed.tile([P, EXP_WINDOW], F32, name="log_table%d" % d, offset=d * LOG_STRIDE)
-            nc.scalar.activation(tab[:, :R], acc[:], ACT.Ln, bias=shift, scale=factors[0][:])
-            log_tables[d] = tab
-
         fetched = {}
 
-        def exp_gather(d):
-            fetched[d] = keep.tile([P, U], F32, name="fetched", tag="factor%d" % d, align_bytes=64)
-            nc.scalar.activation(fetched[d][:], log_tables[d][:].indirect(codes[d][:]), ACT.Exp)
+        def fetch(b, d, width):
+            fetched[(b, d)] = keep.tile([P, width], F32, name="fetched%d_%d" % (b, d), align_bytes=64)
+            piece = codes[d][:, : width // 16]
+            nc.scalar.activation(fetched[(b, d)][:], tables[(b, d)][:].indirect(piece), ACT.Copy)
 
         sums = {}
 
         def look_up(b, d, c0=0, c1=U):
-            before = norm_sb if d == 0 else sums[(b, d - 1, 0)]
+            start = SHARE if b == 3 else 0
+            before = norm_sb[:, c0:c1] if d == 0 else sums[(b, d - 1, start)][:, c0 - start : c1 - start]
             name = "sum%d_%d_%d" % (b, d, c0)
             total = keep.tile([P, c1 - c0], F32, name=name, tag=name, align_bytes=64)
             piece = codes[d][:, c0 // 16 : c1 // 16]
-            nc.vector.tensor_tensor(total[:], tables[(b, d)][:].indirect(piece), before[:, c0:c1], ADD)
+            nc.vector.tensor_tensor(total[:], tables[(b, d)][:].indirect(piece), before, ADD)
             sums[(b, d, c0)] = total
 
-        def finish(b, total, tag, **bias):
-            result = keep.tile([P, U], F32, name="result%d" % b, tag=tag, align_bytes=64)
-            nc.scalar.activation(result[:], total[:], ACT.Sigmoid, scale=-1.0, **bias)
-            nc.sync.dma_start(out=out[b * P : (b + 1) * P, :], in_=result[:])
+        def finish(b, total, tag, c0=0, c1=U, queue=nc.sync):
+            result = keep.tile([P, c1 - c0], F32, name="result", tag=tag, align_bytes=64)
+            nc.scalar.activation(result[:], total, ACT.Sigmoid, scale=-1.0)
+            queue.dma_start(out=out[b * P : (b + 1) * P, c0:c1], in_=result[:])
+
+        def add_turned(b, width, tag):
+            turned = named.tile([P, width], F32, name="turned", tag=tag)
+            terms = [norm_sb] + [fetched[(b, d)] for d in range(BOOKS)]
+            for i, term in enumerate(terms):
+                for c in range(0, width, P):
+                    nc.tensor.matmul(
+                        turned[:, c : c + P],
+                        term[:, c : c + P],
+                        identity[:],
+                        start=(i == 0 and c == 0),
+                        stop=(i == len(terms) - 1 and c == width - P),
+                        is_transpose=True,
+                    )
+            return turned
+
+        def turn_back(b, turned, width):
+            turned_sb = keep.tile([P, width], F32, name="turned_sb%d" % b, align_bytes=64)
+            nc.scalar.copy(out=turned_sb[:], in_=turned[:])
+            total = rotating.tile([P, width], F32, name="acc")
+            for c in range(0, width, P):
+                nc.tensor.transpose(total[:, c : c + P], turned_sb[:, c : c + P], identity[:])
+            return total
 
         pick(0, 0, BOOKS)
         quantize(round_pass("grouped_pass0", raw_pass0), [(0, 0), (1, 0)])
-        pick(1, 2, BOOKS)
-        pick(1, 0, 1)
+        pick(1, 0, 2)
+        quantize(round_pass("grouped_pass1_1", raw_pass1[1]), [(1, 1)])
+        pick(1, 2, 3, "raw_pass1_1")
         quantize(round_pass("grouped_pass1_0", raw_pass1[0]), [(0, 1)])
-        pick(1, 1, 2, "raw_pass1_0")
-        grouped_pass1_1 = round_pass("grouped_pass1_1", raw_pass1[1])
-        table(0, LOG_BOOKS)
-        for d in (2, 0, 1):
-            log_table(d)
-        shifts_copy = keep.tile([P, LOG_BOOKS], F32, name="shifts_copy")
-        shift_sum = keep.tile([P, 1], F32, name="shift_sum", tag="shift_sum", align_bytes=64)
-        nc.scalar.activation(shifts_copy[:], shifts[:], ACT.Copy, accum_out=shift_sum[:])
+        pick(1, 3, 4, "raw_pass1_0")
 
-        quantize(grouped_pass1_1, [(1, 1)])
-        fetched[LOG_BOOKS] = keep.tile([P, U], F32, name="copied", align_bytes=64)
-        nc.vector.tensor_copy(fetched[LOG_BOOKS][:], tables[(0, LOG_BOOKS)][:].indirect(codes[LOG_BOOKS][:]))
-        table(1, 0)
+        table(1, 0, factor[:])
         table(1, 1)
-        table(1, 2, factors[0][:])
+        table(0, 0)
         grouped_batch2 = round_batch("grouped_batch2", raw_batch2)
         look_up(1, 0)
+        fetch(0, 0, U)
         quantize(grouped_batch2, [(2, 0), (2, 1)])
-        grouped_batch3 = round_batch("grouped_batch3", raw_batch3)
         look_up(1, 1)
-        quantize(grouped_batch3, [(3, 0), (3, 1)])
-
-        exp_gather(0)
-        table(2, 0, factors[1][:], behind=(0, 0))
-        exp_gather(1)
-        table(1, 3, behind=(0, 1))
-        table(3, 0, behind=(1, 0))
-        table(2, 1, behind=(1, 1))
-        table(3, 1, behind=(1, 2))
-        table(3, 2)
-        table(3, 3, factors[2][:])
-        exp_gather(2)
-        table(2, 2, behind=(1, 3))
-        table(2, 3, behind=(2, 0))
-
+        table(0, 1)
+        table(1, 2)
+        fetch(0, 1, U)
+        grouped_batch3 = round_batch("grouped_batch3", raw_batch3)
         look_up(1, 2)
-        look_up(2, 0)
+        quantize(grouped_batch3, [(3, 0), (3, 1)])
+        table(0, 2)
+        table(1, 3)
+        fetch(0, 2, U)
         look_up(1, 3)
-        for d in range(BOOKS - 1):
-            look_up(3, d)
-            look_up(2, d + 1)
-
-        runs = [slice(c * P, (c + 1) * P) for c in range(U // P)]
-        turned = [named.tile([P, P], F32, name="turned", tag="bank%d" % c) for c in range(len(runs))]
-        terms = [fetched[LOG_BOOKS], norm_sb] + [fetched[d] for d in range(LOG_BOOKS)]
-        for i, term in enumerate(terms):
-            for c, run in enumerate(runs):
-                nc.tensor.matmul(
-                    turned[c][:],
-                    term[:, run],
-                    identity[:],
-                    start=(i == 0),
-                    stop=(i == len(terms) - 1),
-                    is_transpose=True,
-                )
-        turned_sb = keep.tile([P, U], F32, name="turned_sb", align_bytes=64)
-        shifted_total = rotating.tile([P, U], F32, name="acc")
-        for c, run in enumerate(runs):
-            nc.scalar.copy(out=turned_sb[:, run], in_=turned[c][:])
-            nc.tensor.transpose(shifted_total[:, run], turned_sb[:, run], identity[:])
-
+        table(2, 0)
+        table(0, 3)
+        table(3, 0)
+        fetch(0, 3, U)
+        for d in range(1, BOOKS):
+            table(2, d)
+            table(3, d)
         last = BOOKS - 1
-        finish(0, shifted_total, "result0", bias=shift_sum[:])
-        finish(1, sums[(1, last, 0)], "shift_sum")
-        finish(2, sums[(2, last, 0)], "sum1_%d_0" % last)
-        result3 = keep.tile([P, U], F32, name="result3", tag="sum2_%d_0" % last, align_bytes=64)
-        cuts = (0, U // 2, U - LAST_PIECE, U)
-        for c0, c1 in zip(cuts, cuts[1:]):
-            look_up(3, last, c0, c1)
-            nc.scalar.activation(result3[:, c0:c1], sums[(3, last, c0)][:], ACT.Sigmoid, scale=-1.0)
-            queue = nc.scalar if c1 == U else nc.sync
-            queue.dma_start(out=out[3 * P : 4 * P, c0:c1], in_=result3[:, c0:c1])
+        for d in range(last):
+            look_up(2, d)
+            look_up(3, d, SHARE, U)
+        turned0 = add_turned(0, U, "bank0")
+        finish(1, sums[(1, last, 0)][:], "fetched0_0")
+        total0 = turn_back(0, turned0, U)
+        for d in range(BOOKS):
+            fetch(3, d, SHARE)
+        turned3 = add_turned(3, SHARE, "bank0")
+        finish(0, total0[:], "result0")
+        total3 = turn_back(3, turned3, SHARE)
+        finish(3, total3[:], "result3", 0, SHARE)
+        look_up(2, last)
+        finish(2, sums[(2, last, 0)][:], "turned_sb3")
+        cut = U - LAST_PIECE
+        look_up(3, last, SHARE, cut)
+        finish(3, sums[(3, last, SHARE)][:], "sum2_%d_0" % last, SHARE, cut)
+        look_up(3, last, cut, U)
+        finish(3, sums[(3, last, cut)][:], "sum3_%d_%d" % (last, SHARE), cut, U, nc.scalar)

@@ -8,10 +8,11 @@ P = 128
 PACK = 4
 PASSES = K // (P * PACK)
 BOOKS = S // R
-SHARE = 128
+SHARE = 256
 WINDOW = U + 16
 FIRST_WORDS = 512
 LAST_PIECE = 64
+TURN_BANKS = 5
 FLOPS = 2 * K * V * S
 
 F32 = mybir.dt.float32
@@ -31,7 +32,6 @@ def tile_picked_yadc_prob_p_kernel(
     nc = tc.nc
     with ExitStack() as ctx:
         keep = ctx.enter_context(tc.tile_pool(name="keep", bufs=1))
-        rotating = ctx.enter_context(tc.psum_pool(name="rotating", bufs=4))
         named = ctx.enter_context(tc.psum_pool(name="named", bufs=1))
 
         store_scales = keep.tile([P, T], U8, name="store_scales", align_bytes=64)
@@ -124,11 +124,12 @@ def tile_picked_yadc_prob_p_kernel(
             for i, part in enumerate(parts):
                 quantized[part] = (q_words[:, i * P : (i + 1) * P], q_scales[:, i * P : (i + 1) * P])
 
+        tables = {}
+
         def product(b, d):
-            if b in (0, 3):
-                acc = named.tile([P, R], F32, name="named_acc", tag="bank%d" % d)
-            else:
-                acc = rotating.tile([P, R], F32, name="acc")
+            n = len(tables)
+            bank = n % TURN_BANKS if n < 14 else n - 14 + TURN_BANKS
+            acc = named.tile([P, R], F32, name="acc", tag="bank%d" % bank)
             for o in range(PASSES):
                 q_words, q_scales = quantized[(b, o)]
                 nc.tensor.matmul_mx(
@@ -142,18 +143,19 @@ def tile_picked_yadc_prob_p_kernel(
                 )
             return acc
 
-        tables = {}
-
-        def table(b, d, scale=-0.5):
+        def table(b, d, scale=-0.5, on_vector=False):
             acc = product(b, d)
             tab = keep.tile([P, WINDOW], F32, name="table%d_%d" % (b, d), align_bytes=64)
-            nc.scalar.activation(tab[:, :R], acc[:], ACT.Copy, scale=scale)
+            if on_vector:
+                nc.vector.tensor_scalar(tab[:, :R], acc[:], scale, None, mybir.AluOpType.mult)
+            else:
+                nc.scalar.activation(tab[:, :R], acc[:], ACT.Copy, scale=scale)
             tables[(b, d)] = tab
 
         fetched = {}
 
-        def fetch(b, d, width):
-            fetched[(b, d)] = keep.tile([P, width], F32, name="fetched%d_%d" % (b, d), align_bytes=64)
+        def fetch(b, d, width, tag=None):
+            fetched[(b, d)] = keep.tile([P, width], F32, name="fetched", tag=tag or "fetched%d_%d" % (b, d), align_bytes=64)
             piece = codes[d][:, : width // 16]
             nc.scalar.activation(fetched[(b, d)][:], tables[(b, d)][:].indirect(piece), ACT.Copy)
 
@@ -173,9 +175,8 @@ def tile_picked_yadc_prob_p_kernel(
             nc.scalar.activation(result[:], total, ACT.Sigmoid, scale=-1.0)
             queue.dma_start(out=out[b * P : (b + 1) * P, c0:c1], in_=result[:])
 
-        def add_turned(b, width, tag):
+        def add_turned(b, width, tag, terms):
             turned = named.tile([P, width], F32, name="turned", tag=tag)
-            terms = [norm_sb] + [fetched[(b, d)] for d in range(BOOKS)]
             for i, term in enumerate(terms):
                 for c in range(0, width, P):
                     nc.tensor.matmul(
@@ -191,7 +192,7 @@ def tile_picked_yadc_prob_p_kernel(
         def turn_back(b, turned, width):
             turned_sb = keep.tile([P, width], F32, name="turned_sb%d" % b, align_bytes=64)
             nc.scalar.copy(out=turned_sb[:], in_=turned[:])
-            total = rotating.tile([P, width], F32, name="acc")
+            total = named.tile([P, width], F32, name="total", tag="bank%d" % (7 if b == 0 else 0))
             for c in range(0, width, P):
                 nc.tensor.transpose(total[:, c : c + P], turned_sb[:, c : c + P], identity[:])
             return total
@@ -227,25 +228,30 @@ def tile_picked_yadc_prob_p_kernel(
         table(3, 0)
         fetch(0, 3, U)
         for d in range(1, BOOKS):
-            table(2, d)
-            table(3, d)
+            table(2, d, on_vector=(d == BOOKS - 1))
+            table(3, d, on_vector=(d == BOOKS - 1))
         last = BOOKS - 1
         for d in range(last):
             look_up(2, d)
             look_up(3, d, SHARE, U)
-        turned0 = add_turned(0, U, "bank0")
-        finish(1, sums[(1, last, 0)][:], "fetched0_0")
+        turned0 = add_turned(0, U, "bank4", [norm_sb] + [fetched[(0, d)] for d in range(BOOKS)])
+        fetch(3, 0, SHARE)
+        fetch(3, 1, SHARE)
         total0 = turn_back(0, turned0, U)
-        for d in range(BOOKS):
-            fetch(3, d, SHARE)
-        turned3 = add_turned(3, SHARE, "bank0")
-        finish(0, total0[:], "result0")
+        fetch(3, 2, SHARE)
+        fetch(3, 3, SHARE)
+        terms3 = [fetched[(3, 2)], fetched[(3, 0)], fetched[(3, 1)], norm_sb, fetched[(3, 3)]]
+        turned3 = add_turned(3, SHARE, "bank1", terms3)
+        finish(1, sums[(1, last, 0)][:], "fetched0_3")
         total3 = turn_back(3, turned3, SHARE)
-        finish(3, total3[:], "result3", 0, SHARE)
+        finish(0, total0[:], "fetched3_3")
         look_up(2, last)
+        finish(3, total3[:], "result3", 0, SHARE)
         finish(2, sums[(2, last, 0)][:], "turned_sb3")
-        cut = U - LAST_PIECE
-        look_up(3, last, SHARE, cut)
-        finish(3, sums[(3, last, SHARE)][:], "sum2_%d_0" % last, SHARE, cut)
-        look_up(3, last, cut, U)
-        finish(3, sums[(3, last, cut)][:], "sum3_%d_%d" % (last, SHARE), cut, U, nc.scalar)
+        cuts = (SHARE, U - LAST_PIECE, U)
+        result3 = keep.tile([P, U], F32, name="result3b", tag="sum2_%d_0" % last, align_bytes=64)
+        for c0, c1 in zip(cuts, cuts[1:]):
+            look_up(3, last, c0, c1)
+            nc.scalar.activation(result3[:, c0:c1], sums[(3, last, c0)][:], ACT.Sigmoid, scale=-1.0)
+            queue = nc.scalar if c1 == U else nc.sync
+            queue.dma_start(out=out[3 * P : 4 * P, c0:c1], in_=result3[:, c0:c1])

@@ -8,7 +8,7 @@ P = 128
 PACK = 4
 PASSES = K // (P * PACK)
 BOOKS = S // R
-SHARE = 256
+SHARE = 160
 WINDOW = U + 16
 FIRST_WORDS = 512
 LAST_PIECE = 64
@@ -35,13 +35,17 @@ def tile_picked_yadc_prob_p_kernel(
         named = ctx.enter_context(tc.psum_pool(name="named", bufs=1))
 
         store_scales = keep.tile([P, T], U8, name="store_scales", align_bytes=64)
-        nc.vector.memset(store_scales[:].bitcast(I32), 0)
+        nc.gpsimd.memset(store_scales[:].bitcast(I32), 0)
         zero = keep.tile([P, 1], F32, name="zero")
         nc.vector.memset(zero[:], 0.0)
         half = keep.tile([P, 1], F32, name="half")
         nc.scalar.activation(half[:], zero[:], ACT.Sigmoid)
         factor = keep.tile([P, 1], F32, name="factor", align_bytes=64)
         nc.scalar.activation(factor[:], half[:], ACT.Copy, scale=-1.0)
+        factor30 = keep.tile([P, 1], F32, name="factor30", tag="fetched0_3", align_bytes=64)
+        nc.gpsimd.memset(factor30[:], -0.5)
+        factor20 = keep.tile([P, 1], F32, name="factor20", tag="fetched0_2", align_bytes=64)
+        nc.gpsimd.memset(factor20[:], -0.5)
         identity = keep.tile([P, P], F32, name="identity", align_bytes=64)
         nc.vector.memset(identity[:], 0.0)
         make_identity(nc, identity[:], nomemset=True)
@@ -62,10 +66,7 @@ def tile_picked_yadc_prob_p_kernel(
             return raw
 
         def load_batch(b):
-            raw = keep.tile([P, PASSES, PACK, P], F32, name="raw_batch%d" % b, align_bytes=64)
-            for o in range(PASSES):
-                load_rows(raw[:, o, :, :], o, b, b + 1)
-            return raw
+            return [load_pass("raw%d_%d" % (b, o), o, b, b + 1) for o in range(PASSES)]
 
         def load_list(name, src, n):
             offsets = keep.tile([P, n // 16], U16, name=name)
@@ -85,11 +86,12 @@ def tile_picked_yadc_prob_p_kernel(
         raw_pass1 = {b: load_pass("raw_pass1_%d" % b, 1, b, b + 1) for b in (1, 0)}
         codes = {0: load_list("code1_sb", code1, U)}
         codes[1] = load_list("code2_sb", code2, U)
-        raw_batch2 = load_batch(2)
+        codes[2] = load_list("code3_sb", code3, U)
+        raw_batch2 = [load_pass("raw2_0", 0, 2, 3)]
         norm_sb = keep.tile([P, U], F32, name="norm_sb", align_bytes=64)
         nc.sync.dma_start(out=norm_sb[:], in_=norm)
+        raw_batch2.append(load_pass("raw2_1", 1, 2, 3))
         raw_batch3 = load_batch(3)
-        codes[2] = load_list("code3_sb", code3, U)
         codes[3] = load_list("code4_sb", code4, U)
 
         picked_scales = keep.tile([P, S], U8, name="picked_scales", align_bytes=64)
@@ -109,9 +111,17 @@ def tile_picked_yadc_prob_p_kernel(
             nc.scalar.copy(out=grouped[:], in_=raw[:].rearrange("p j w -> p w j"))
             return grouped[:].rearrange("p w j -> p (w j)")
 
+        def round_batch_aside(name, raw):
+            grouped = keep.tile([P, PASSES, P, PACK], BF16, name=name, align_bytes=64)
+            src = [raw[o][:].rearrange("p j w -> p w j") for o in range(PASSES)]
+            nc.gpsimd.tensor_scalar(grouped[:, 0], src[0], 1.0, 0.0, mybir.AluOpType.mult, ADD)
+            nc.vector.tensor_copy(out=grouped[:, 1], in_=src[1])
+            return grouped[:].rearrange("p o w j -> p (o w j)")
+
         def round_batch(name, raw):
             grouped = keep.tile([P, PASSES, P, PACK], BF16, name=name, align_bytes=64)
-            nc.vector.tensor_copy(out=grouped[:], in_=raw[:].rearrange("p o j w -> p o w j"))
+            for o in range(PASSES):
+                nc.vector.tensor_copy(out=grouped[:, o], in_=raw[o][:].rearrange("p j w -> p w j"))
             return grouped[:].rearrange("p o w j -> p (o w j)")
 
         quantized = {}
@@ -161,11 +171,12 @@ def tile_picked_yadc_prob_p_kernel(
 
         sums = {}
 
-        def look_up(b, d, c0=0, c1=U):
-            start = SHARE if b == 3 else 0
+        def look_up(b, d, c0=0, c1=U, tag=None, start=None):
+            if start is None:
+                start = SHARE if b == 3 else 0
             before = norm_sb[:, c0:c1] if d == 0 else sums[(b, d - 1, start)][:, c0 - start : c1 - start]
             name = "sum%d_%d_%d" % (b, d, c0)
-            total = keep.tile([P, c1 - c0], F32, name=name, tag=name, align_bytes=64)
+            total = keep.tile([P, c1 - c0], F32, name=name, tag=tag or name, align_bytes=64)
             piece = codes[d][:, c0 // 16 : c1 // 16]
             nc.vector.tensor_tensor(total[:], tables[(b, d)][:].indirect(piece), before, ADD)
             sums[(b, d, c0)] = total
@@ -175,26 +186,31 @@ def tile_picked_yadc_prob_p_kernel(
             nc.scalar.activation(result[:], total, ACT.Sigmoid, scale=-1.0)
             queue.dma_start(out=out[b * P : (b + 1) * P, c0:c1], in_=result[:])
 
+        def runs(width):
+            return [min(c, width - P) for c in range(0, width, P)]
+
         def add_turned(b, width, tag, terms):
-            turned = named.tile([P, width], F32, name="turned", tag=tag)
+            starts = runs(width)
+            turned = named.tile([P, len(starts) * P], F32, name="turned", tag=tag)
             for i, term in enumerate(terms):
-                for c in range(0, width, P):
+                for slot, c in enumerate(starts):
                     nc.tensor.matmul(
-                        turned[:, c : c + P],
+                        turned[:, slot * P : (slot + 1) * P],
                         term[:, c : c + P],
                         identity[:],
-                        start=(i == 0 and c == 0),
-                        stop=(i == len(terms) - 1 and c == width - P),
+                        start=(i == 0 and slot == 0),
+                        stop=(i == len(terms) - 1 and slot == len(starts) - 1),
                         is_transpose=True,
                     )
             return turned
 
         def turn_back(b, turned, width):
-            turned_sb = keep.tile([P, width], F32, name="turned_sb%d" % b, align_bytes=64)
+            starts = runs(width)
+            turned_sb = keep.tile([P, len(starts) * P], F32, name="turned_sb%d" % b, align_bytes=64)
             nc.scalar.copy(out=turned_sb[:], in_=turned[:])
             total = named.tile([P, width], F32, name="total", tag="bank%d" % (7 if b == 0 else 0))
-            for c in range(0, width, P):
-                nc.tensor.transpose(total[:, c : c + P], turned_sb[:, c : c + P], identity[:])
+            for slot, c in enumerate(starts):
+                nc.tensor.transpose(total[:, c : c + P], turned_sb[:, slot * P : (slot + 1) * P], identity[:])
             return total
 
         pick(0, 0, BOOKS)
@@ -208,32 +224,35 @@ def tile_picked_yadc_prob_p_kernel(
         table(1, 0, factor[:])
         table(1, 1)
         table(0, 0)
-        grouped_batch2 = round_batch("grouped_batch2", raw_batch2)
-        look_up(1, 0)
+        table(0, 1)
+        grouped_batch2 = round_batch_aside("grouped_batch2", raw_batch2)
+        look_up(1, 0, tag="raw2_0")
         fetch(0, 0, U)
         quantize(grouped_batch2, [(2, 0), (2, 1)])
         look_up(1, 1)
-        table(0, 1)
         table(1, 2)
         fetch(0, 1, U)
         grouped_batch3 = round_batch("grouped_batch3", raw_batch3)
-        look_up(1, 2)
+        look_up(1, 2, tag="raw3_0")
         quantize(grouped_batch3, [(3, 0), (3, 1)])
         table(0, 2)
         table(1, 3)
+        table(2, 0, factor20[:])
         fetch(0, 2, U)
+        look_up(2, 0, tag="raw3_1")
         look_up(1, 3)
-        table(2, 0)
         table(0, 3)
-        table(3, 0)
+        table(3, 0, factor30[:])
         fetch(0, 3, U)
-        for d in range(1, BOOKS):
-            table(2, d, on_vector=(d == BOOKS - 1))
-            table(3, d, on_vector=(d == BOOKS - 1))
+        table(2, 1)
+        for d in range(1, BOOKS - 1):
+            table(2, d + 1)
+            table(3, d)
+        table(3, BOOKS - 1)
         last = BOOKS - 1
-        for d in range(last):
+        for d in range(1, last):
             look_up(2, d)
-            look_up(3, d, SHARE, U)
+            look_up(3, d - 1, SHARE, U)
         turned0 = add_turned(0, U, "bank4", [norm_sb] + [fetched[(0, d)] for d in range(BOOKS)])
         fetch(3, 0, SHARE)
         fetch(3, 1, SHARE)
@@ -243,15 +262,17 @@ def tile_picked_yadc_prob_p_kernel(
         terms3 = [fetched[(3, 2)], fetched[(3, 0)], fetched[(3, 1)], norm_sb, fetched[(3, 3)]]
         turned3 = add_turned(3, SHARE, "bank1", terms3)
         finish(1, sums[(1, last, 0)][:], "fetched0_3")
+        finish(0, total0[:], "fetched3_1")
         total3 = turn_back(3, turned3, SHARE)
-        finish(0, total0[:], "fetched3_3")
         look_up(2, last)
+        finish(2, sums[(2, last, 0)][:], "fetched3_3")
         finish(3, total3[:], "result3", 0, SHARE)
-        finish(2, sums[(2, last, 0)][:], "turned_sb3")
-        cuts = (SHARE, U - LAST_PIECE, U)
+        middle = (SHARE + U) // 64 * 32
+        look_up(3, last - 1, SHARE, middle)
+        look_up(3, last - 1, middle, U)
         result3 = keep.tile([P, U], F32, name="result3b", tag="sum2_%d_0" % last, align_bytes=64)
-        for c0, c1 in zip(cuts, cuts[1:]):
-            look_up(3, last, c0, c1)
+        for c0, c1, start in ((SHARE, middle, SHARE), (middle, U - LAST_PIECE, middle), (U - LAST_PIECE, U, middle)):
+            look_up(3, last, c0, c1, start=start)
             nc.scalar.activation(result3[:, c0:c1], sums[(3, last, c0)][:], ACT.Sigmoid, scale=-1.0)
             queue = nc.scalar if c1 == U else nc.sync
             queue.dma_start(out=out[3 * P : 4 * P, c0:c1], in_=result3[:, c0:c1])

@@ -81,6 +81,8 @@ def tile_picked_yadc_prob_p_kernel(
                 in_=x_scales[:, 4 * q : 4 * q + 4, :].bitcast(I32),
             )
         load_words(0, FIRST_WORDS, T)
+        norm_quads = keep.tile([P, PACK], F32, name="norm_quads", align_bytes=64)
+        nc.sync.dma_start(out=norm_quads[:], in_=norm[0].rearrange("(p j) -> p j", j=PACK))
         raw_pass0 = load_pass("raw_pass0", 0, 0, 2)
         load_words(1, 0, T)
         raw_pass1 = {b: load_pass("raw_pass1_%d" % b, 1, b, b + 1) for b in (1, 0)}
@@ -88,11 +90,15 @@ def tile_picked_yadc_prob_p_kernel(
         codes[1] = load_list("code2_sb", code2, U)
         codes[2] = load_list("code3_sb", code3, U)
         raw_batch2 = [load_pass("raw2_0", 0, 2, 3)]
-        norm_sb = keep.tile([P, U], F32, name="norm_sb", align_bytes=64)
-        nc.sync.dma_start(out=norm_sb[:], in_=norm)
         raw_batch2.append(load_pass("raw2_1", 1, 2, 3))
         raw_batch3 = load_batch(3)
         codes[3] = load_list("code4_sb", code4, U)
+
+        spread = named.tile([P, PACK, P], F32, name="spread", tag="bank7")
+        for j in range(PACK):
+            nc.tensor.transpose(spread[:, j, :], norm_quads[:, j : j + 1].to_broadcast([P, P]), identity[:])
+        norm_sb = keep.tile([P, U], F32, name="norm_sb", align_bytes=64)
+        nc.scalar.copy(out=norm_sb[:].rearrange("p (c j) -> p c j", j=PACK), in_=spread[:].rearrange("p j c -> p c j"))
 
         picked_scales = keep.tile([P, S], U8, name="picked_scales", align_bytes=64)
         nc.vector.tensor_copy(picked_scales[:], store_scales[:].indirect(offs_sb[:]))

@@ -8,7 +8,7 @@ P = 128
 PACK = 4
 PASSES = K // (P * PACK)
 BOOKS = S // R
-SHARE = 160
+SHARE = 192
 WINDOW = U + 16
 FIRST_WORDS = 512
 LAST_PIECE = 64
@@ -221,11 +221,10 @@ def tile_picked_yadc_prob_p_kernel(
 
         pick(0, 0, BOOKS)
         quantize(round_pass("grouped_pass0", raw_pass0), [(0, 0), (1, 0)])
-        pick(1, 0, 2)
+        pick(1, 0, 3)
         quantize(round_pass("grouped_pass1_1", raw_pass1[1]), [(1, 1)])
-        pick(1, 2, 3, "raw_pass1_1")
+        pick(1, 3, 4, "raw_pass1_1")
         quantize(round_pass("grouped_pass1_0", raw_pass1[0]), [(0, 1)])
-        pick(1, 3, 4, "raw_pass1_0")
 
         table(1, 0, factor[:])
         table(1, 1)

@@ -65,9 +65,6 @@ def tile_picked_yadc_prob_p_kernel(
             load_rows(raw[:], o, b0, b1)
             return raw
 
-        def load_batch(b):
-            return [load_pass("raw%d_%d" % (b, o), o, b, b + 1) for o in range(PASSES)]
-
         def load_list(name, src, n):
             offsets = keep.tile([P, n // 16], U16, name=name)
             nc.sync.dma_start(offsets[:], src)
@@ -75,24 +72,23 @@ def tile_picked_yadc_prob_p_kernel(
 
         load_words(0, 0, FIRST_WORDS)
         offs_sb = load_list("offs_sb", offs, S)
+        norm_quads = keep.tile([P, PACK], F32, name="norm_quads", align_bytes=64)
+        nc.sync.dma_start(out=norm_quads[:], in_=norm[0].rearrange("(p j) -> p j", j=PACK))
         for q in (2, 3, 0, 1):
             nc.sync.dma_start(
                 out=store_scales[32 * q : 32 * q + 4 * PASSES, :].bitcast(I32),
                 in_=x_scales[:, 4 * q : 4 * q + 4, :].bitcast(I32),
             )
         load_words(0, FIRST_WORDS, T)
-        norm_quads = keep.tile([P, PACK], F32, name="norm_quads", align_bytes=64)
-        nc.sync.dma_start(out=norm_quads[:], in_=norm[0].rearrange("(p j) -> p j", j=PACK))
         raw_pass0 = load_pass("raw_pass0", 0, 0, 2)
         load_words(1, 0, T)
         raw_pass1 = {b: load_pass("raw_pass1_%d" % b, 1, b, b + 1) for b in (1, 0)}
-        codes = {0: load_list("code1_sb", code1, U)}
-        codes[1] = load_list("code2_sb", code2, U)
-        codes[2] = load_list("code3_sb", code3, U)
         raw_batch2 = [load_pass("raw2_0", 0, 2, 3)]
+        codes = {1: load_list("code2_sb", code2, U), 2: load_list("code3_sb", code3, U)}
         raw_batch2.append(load_pass("raw2_1", 1, 2, 3))
-        raw_batch3 = load_batch(3)
         codes[3] = load_list("code4_sb", code4, U)
+        codes[0] = load_list("code1_sb", code1, U)
+        raw_batch3 = [load_pass("raw3_%d" % o, o, 3, 4) for o in range(PASSES)]
 
         spread = named.tile([P, PACK, P], F32, name="spread", tag="bank7")
         for j in range(PACK):

@@ -8,11 +8,9 @@ P = 128
 PACK = 4
 PASSES = K // (P * PACK)
 BOOKS = S // R
-SHARE = 192
 WINDOW = U + 16
-FIRST_WORDS = 512
+ROWS0 = 96
 LAST_PIECE = 64
-TURN_BANKS = 5
 FLOPS = 2 * K * V * S
 
 F32 = mybir.dt.float32
@@ -24,6 +22,12 @@ U8 = mybir.dt.uint8
 FP8X4 = mybir.dt.float8_e4m3fn_x4
 ACT = mybir.ActivationFunctionType
 ADD = mybir.AluOpType.add
+MULT = mybir.AluOpType.mult
+FACTORS = (("f02", -0.5), ("f03", -0.5), ("f12", -0.5), ("f20", -0.5), ("f13", -0.5), ("f21", -0.5), ("f30", -0.5), ("f22", -0.5), ("f31", -0.5), ("c0", 1.0), ("f23", -0.5), ("f32", -0.5), ("f33", -0.5), ("s1", -1.0), ("s0", -1.0), ("c3", 1.0))
+SHARE = 256
+TURNED = {0: U, 3: SHARE}
+NEXT = WINDOW * 4
+WIDTH = {F32: 4, BF16: 2, I32: 4, U32: 4, U8: 1}
 
 
 def tile_picked_yadc_prob_p_kernel(
@@ -31,249 +35,307 @@ def tile_picked_yadc_prob_p_kernel(
 ):
     nc = tc.nc
     with ExitStack() as ctx:
+        lists = ctx.enter_context(tc.tile_pool(name="lists", bufs=1))
         keep = ctx.enter_context(tc.tile_pool(name="keep", bufs=1))
-        named = ctx.enter_context(tc.psum_pool(name="named", bufs=1))
+        psum = ctx.enter_context(tc.psum_pool(name="psum", bufs=1))
+        place = {"free": 0}
 
-        store_scales = keep.tile([P, T], U8, name="store_scales", align_bytes=64)
-        nc.gpsimd.memset(store_scales[:].bitcast(I32), 0)
-        zero = keep.tile([P, 1], F32, name="zero")
+        def sbuf(name, shape, dtype, over=None, shift=0):
+            if over is None:
+                size = WIDTH[dtype]
+                for n in shape[1:]:
+                    size = size * n
+                place[name] = place["free"]
+                place["free"] = place["free"] + (size + 63) // 64 * 64
+            else:
+                place[name] = place[over] + shift
+            return keep.tile(shape, dtype, name=name, align_bytes=64, offset=place[name])
+
+        def bank(name, shape, n):
+            return psum.tile(shape, F32, name=name, tag="bank%d" % n)
+
+        piece_bytes = PACK * P * 4
+        store_scales = sbuf("store_scales", [P, 4 * piece_bytes + 2 * WINDOW * 4], U8)
+        nc.gpsimd.memset(store_scales[:ROWS0, :T].bitcast(I32), 0)
+        planes = sbuf("planes", [P, PASSES * S], U8)
+        nc.gpsimd.memset(planes[:].bitcast(I32), 0)
+        zero = sbuf("zero", [P, 1], F32)
         nc.vector.memset(zero[:], 0.0)
-        half = keep.tile([P, 1], F32, name="half")
+        half = sbuf("half", [P, 1], F32)
         nc.scalar.activation(half[:], zero[:], ACT.Sigmoid)
-        factor = keep.tile([P, 1], F32, name="factor", align_bytes=64)
+        factor = sbuf("factor", [P, 1], F32)
         nc.scalar.activation(factor[:], half[:], ACT.Copy, scale=-1.0)
-        factor30 = keep.tile([P, 1], F32, name="factor30", tag="fetched0_3", align_bytes=64)
-        nc.gpsimd.memset(factor30[:], -0.5)
-        factor20 = keep.tile([P, 1], F32, name="factor20", tag="fetched0_2", align_bytes=64)
-        nc.gpsimd.memset(factor20[:], -0.5)
-        identity = keep.tile([P, P], F32, name="identity", align_bytes=64)
+        identity = sbuf("identity", [P, P], F32)
         nc.vector.memset(identity[:], 0.0)
         make_identity(nc, identity[:], nomemset=True)
-
-        store_words = [keep.tile([P, T], I32, name="store_words%d" % o, align_bytes=64) for o in range(PASSES)]
-
-        def load_words(o, c0, c1):
-            src = x_words[o].rearrange("p n t -> p (n t)").bitcast(I32)
-            nc.sync.dma_start(out=store_words[o][:, c0:c1], in_=src[:, c0:c1])
-
-        def load_rows(dst, o, b0, b1):
-            rows = hT[o * P * PACK : (o + 1) * P * PACK, b0 * P : b1 * P]
-            nc.sync.dma_start(out=dst, in_=rows.rearrange("(p j) w -> p j w", j=PACK))
-
-        def load_pass(name, o, b0, b1):
-            raw = keep.tile([P, PACK, (b1 - b0) * P], F32, name="raw", tag=name, align_bytes=64)
-            load_rows(raw[:], o, b0, b1)
-            return raw
+        factors = {}
+        for name, value in FACTORS:
+            factors[name] = sbuf(name, [P, WINDOW + 8], F32)[:, :1]
+            nc.vector.memset(factors[name], value)
+            place["free"] = place[name] + 2 * WINDOW * 4
 
         def load_list(name, src, n):
-            offsets = keep.tile([P, n // 16], U16, name=name)
+            offsets = lists.tile([P, n // 16], U16, name=name)
             nc.sync.dma_start(offsets[:], src)
             return offsets
 
-        load_words(0, 0, FIRST_WORDS)
-        offs_sb = load_list("offs_sb", offs, S)
-        norm_quads = keep.tile([P, PACK], F32, name="norm_quads", align_bytes=64)
-        nc.sync.dma_start(out=norm_quads[:], in_=norm[0].rearrange("(p j) -> p j", j=PACK))
-        for q in (2, 3, 0, 1):
-            nc.sync.dma_start(
-                out=store_scales[32 * q : 32 * q + 4 * PASSES, :].bitcast(I32),
-                in_=x_scales[:, 4 * q : 4 * q + 4, :].bitcast(I32),
-            )
-        load_words(0, FIRST_WORDS, T)
-        raw_pass0 = load_pass("raw_pass0", 0, 0, 2)
-        load_words(1, 0, T)
-        raw_pass1 = {b: load_pass("raw_pass1_%d" % b, 1, b, b + 1) for b in (1, 0)}
-        raw_batch2 = [load_pass("raw2_0", 0, 2, 3)]
-        codes = {1: load_list("code2_sb", code2, U), 2: load_list("code3_sb", code3, U)}
-        raw_batch2.append(load_pass("raw2_1", 1, 2, 3))
-        codes[3] = load_list("code4_sb", code4, U)
-        codes[0] = load_list("code1_sb", code1, U)
-        raw_batch3 = [load_pass("raw3_%d" % o, o, 3, 4) for o in range(PASSES)]
+        def load_words(o):
+            words = sbuf("store_words%d" % o, [P, T], I32)
+            nc.sync.dma_start(out=words[:], in_=x_words[o].rearrange("p n t -> p (n t)").bitcast(I32))
+            return words
 
-        spread = named.tile([P, PACK, P], F32, name="spread", tag="bank7")
+        def load_pass(name, o, b0, b1, over=None, shift=0):
+            raw = sbuf(name, [P, PACK, (b1 - b0) * P], F32, over, shift)
+            rows = hT[o * P * PACK : (o + 1) * P * PACK, b0 * P : b1 * P]
+            nc.sync.dma_start(out=raw[:], in_=rows.rearrange("(p j) w -> p j w", j=PACK))
+            return raw
+
+        nc.sync.dma_start(
+            out=store_scales[ROWS0:, :T].bitcast(I32), in_=x_scales.rearrange("o r c -> r o c").bitcast(I32)
+        )
+        offs_sb = load_list("offs_sb", offs, S)
+        store_words = [load_words(0)]
+        norm_quads = sbuf("norm_quads", [P, PACK], F32)
+        nc.sync.dma_start(out=norm_quads[:], in_=norm[0].rearrange("(p j) -> p j", j=PACK))
+        codes = [load_list("code%d_sb" % (d + 1), src, U) for d, src in enumerate((code1, code2, code3, code4))]
+        store_words.append(load_words(1))
+        early0 = load_pass("early0", 0, 0, 2)
+        raw = {(b, 0): early0[:, :, b * P : (b + 1) * P] for b in range(2)}
+        raw[(0, 1)] = load_pass("raw0_1", 1, 0, 1)[:]
+
+        picked_rows = sbuf("picked_rows", [P, S], U8)
+        nc.vector.tensor_copy(picked_rows[:], store_scales[:, :T].indirect(offs_sb[:]))
+        for q in range(4):
+            rows = picked_rows[ROWS0 + 8 * q : ROWS0 + 8 * q + 8, :]
+            nc.sync.dma_start(out=planes[32 * q : 32 * q + 4, :].bitcast(I32), in_=rows.bitcast(I32))
+
+        middle = 4 * piece_bytes + WINDOW * 4
+        raw[(1, 1)] = load_pass("raw1_1", 1, 1, 2, "store_scales", middle - piece_bytes // 2)[:]
+        for i, (b, o) in enumerate(((2, 0), (2, 1), (3, 0), (3, 1))):
+            raw[(b, o)] = load_pass("raw%d_%d" % (b, o), o, b, b + 1, "store_scales", i * piece_bytes)[:]
+
+        spread = bank("spread", [P, PACK, P], 2)
         for j in range(PACK):
             nc.tensor.transpose(spread[:, j, :], norm_quads[:, j : j + 1].to_broadcast([P, P]), identity[:])
-        norm_sb = keep.tile([P, U], F32, name="norm_sb", align_bytes=64)
+        norm_sb = sbuf("norm_sb", [P, U], F32)
         nc.scalar.copy(out=norm_sb[:].rearrange("p (c j) -> p c j", j=PACK), in_=spread[:].rearrange("p j c -> p c j"))
+        norm_turned = bank("norm_turned", [P, PACK, P], 2)
+        for j in range(PACK):
+            nc.tensor.transpose(norm_turned[:, j, :], norm_sb[:, j * P : (j + 1) * P], identity[:])
+        norm_cols = sbuf("norm_cols", [P, PACK], F32)
+        nc.scalar.copy(out=norm_cols[:], in_=norm_turned[:, :, 0])
+        totals = {}
+        for n, (b, width) in enumerate(TURNED.items()):
+            totals[b] = bank("total%d" % b, [P, width], n)
+            for j in range(width // P):
+                nc.tensor.matmul(
+                    totals[b][:, j * P : (j + 1) * P],
+                    norm_cols[:, j : j + 1].to_broadcast([P, P]),
+                    identity[:],
+                    start=(j == 0),
+                    stop=False,
+                    is_transpose=True,
+                )
 
-        picked_scales = keep.tile([P, S], U8, name="picked_scales", align_bytes=64)
-        nc.vector.tensor_copy(picked_scales[:], store_scales[:].indirect(offs_sb[:]))
-        picked_words = {}
+        picked = {}
 
-        def pick(o, d0, d1, tag=None):
-            name = "picked%d_%d" % (o, d0)
-            words = keep.tile([P, (d1 - d0) * R], U32, name=name, tag=tag or name, align_bytes=64)
+        def pick(o, d0, d1, over=None):
+            words = sbuf("picked%d_%d" % (o, d0), [P, (d1 - d0) * R], U32, over)
             piece = offs_sb[:, d0 * R // 16 : d1 * R // 16]
             nc.vector.tensor_copy(words[:], store_words[o][:].bitcast(U32).indirect(piece))
             for d in range(d0, d1):
-                picked_words[(o, d)] = words[:, (d - d0) * R : (d - d0 + 1) * R]
+                picked[(o, d)] = (words, d0)
 
-        def round_pass(name, raw):
-            grouped = keep.tile([P, raw.shape[2], PACK], BF16, name=name, align_bytes=64)
-            nc.scalar.copy(out=grouped[:], in_=raw[:].rearrange("p j w -> p w j"))
-            return grouped[:].rearrange("p w j -> p (w j)")
+        grouped = {}
 
-        def round_batch_aside(name, raw):
-            grouped = keep.tile([P, PASSES, P, PACK], BF16, name=name, align_bytes=64)
-            src = [raw[o][:].rearrange("p j w -> p w j") for o in range(PASSES)]
-            nc.gpsimd.tensor_scalar(grouped[:, 0], src[0], 1.0, 0.0, mybir.AluOpType.mult, ADD)
-            nc.vector.tensor_copy(out=grouped[:, 1], in_=src[1])
-            return grouped[:].rearrange("p o w j -> p (o w j)")
-
-        def round_batch(name, raw):
-            grouped = keep.tile([P, PASSES, P, PACK], BF16, name=name, align_bytes=64)
-            for o in range(PASSES):
-                nc.vector.tensor_copy(out=grouped[:, o], in_=raw[o][:].rearrange("p j w -> p w j"))
-            return grouped[:].rearrange("p o w j -> p (o w j)")
+        def round_pass(b, o, engine, over=None, alone=False):
+            if alone:
+                grouped[(b, o)] = (sbuf("grouped%d_%d" % (b, o), [P, 1, P, PACK], BF16, over), o)
+            elif (b, o) not in grouped:
+                both = sbuf("grouped%d" % b, [P, PASSES, P, PACK], BF16, over)
+                for i in range(PASSES):
+                    grouped[(b, i)] = (both, 0)
+            tile, first = grouped[(b, o)]
+            src = raw[(b, o)].rearrange("p j w -> p w j")
+            if engine is nc.gpsimd:
+                nc.gpsimd.tensor_scalar(tile[:, o - first], src, 1.0, 0.0, MULT, ADD)
+            elif engine is nc.vector:
+                nc.vector.tensor_copy(out=tile[:, o - first], in_=src)
+            else:
+                nc.scalar.copy(out=tile[:, o - first], in_=src)
 
         quantized = {}
 
-        def quantize(grouped, parts):
-            name = "%d_%d" % parts[0]
-            q_words = keep.tile([P, len(parts) * P], U32, name="q_words" + name, align_bytes=64)
-            q_scales = keep.tile([P, len(parts) * P], U8, name="q_scales" + name, align_bytes=64)
-            nc.vector.quantize_mx(out=q_words[:].bitcast(FP8X4), scales=q_scales[:], in_=grouped)
-            for i, part in enumerate(parts):
-                quantized[part] = (q_words[:, i * P : (i + 1) * P], q_scales[:, i * P : (i + 1) * P])
+        def quantize(b, o0=0, o1=PASSES):
+            q_words = sbuf("q_words%d_%d" % (b, o0), [P, (o1 - o0) * P], U32)
+            q_scales = sbuf("q_scales%d_%d" % (b, o0), [P, (o1 - o0) * P], U8)
+            tile, first = grouped[(b, o0)]
+            src = tile[:, o0 - first : o1 - first].rearrange("p o w j -> p (o w j)")
+            nc.vector.quantize_mx(out=q_words[:].bitcast(FP8X4), scales=q_scales[:], in_=src)
+            for o in range(o0, o1):
+                cols = slice((o - o0) * P, (o - o0 + 1) * P)
+                quantized[(b, o)] = (q_words[:, cols], q_scales[:, cols])
+
+        products = {}
+
+        def product(b, d0, d1, n, order=(0, 1)):
+            acc = bank("acc", [P, (d1 - d0) * R], n)
+            together = all(picked[(o, d0)][1] == picked[(o, d1 - 1)][1] for o in range(PASSES))
+            for e0, e1 in [(d0, d1)] if together else [(d, d + 1) for d in range(d0, d1)]:
+                for o in order:
+                    words, first = picked[(o, e0)]
+                    q_words, q_scales = quantized[(b, o)]
+                    nc.tensor.matmul_mx(
+                        out=acc[:, (e0 - d0) * R : (e1 - d0) * R],
+                        lhsT=q_words.bitcast(FP8X4),
+                        lhsT_scale=q_scales,
+                        rhs=words[:, (e0 - first) * R : (e1 - first) * R].bitcast(FP8X4),
+                        rhs_scale=planes[:, o * S + e0 * R : o * S + e1 * R],
+                        start=(o == order[0]),
+                        stop=(o == order[-1]),
+                    )
+            for d in range(d0, d1):
+                products[(b, d)] = acc[:, (d - d0) * R : (d - d0 + 1) * R]
 
         tables = {}
 
-        def product(b, d):
-            n = len(tables)
-            bank = n % TURN_BANKS if n < 14 else n - 14 + TURN_BANKS
-            acc = named.tile([P, R], F32, name="acc", tag="bank%d" % bank)
-            for o in range(PASSES):
-                q_words, q_scales = quantized[(b, o)]
-                nc.tensor.matmul_mx(
-                    out=acc[:],
-                    lhsT=q_words.bitcast(FP8X4),
-                    lhsT_scale=q_scales,
-                    rhs=picked_words[(o, d)].bitcast(FP8X4),
-                    rhs_scale=picked_scales[4 * o : P, d * R : (d + 1) * R],
-                    start=(o == 0),
-                    stop=(o == PASSES - 1),
-                )
-            return acc
-
-        def table(b, d, scale=-0.5, on_vector=False):
-            acc = product(b, d)
-            tab = keep.tile([P, WINDOW], F32, name="table%d_%d" % (b, d), align_bytes=64)
+        def table(b, d, scale=-0.5, on_vector=False, over=None, shift=0):
+            tab = sbuf("table%d_%d" % (b, d), [P, WINDOW], F32, over, shift)
             if on_vector:
-                nc.vector.tensor_scalar(tab[:, :R], acc[:], scale, None, mybir.AluOpType.mult)
+                nc.vector.tensor_scalar(tab[:, :R], products[(b, d)], scale, None, MULT)
             else:
-                nc.scalar.activation(tab[:, :R], acc[:], ACT.Copy, scale=scale)
+                nc.scalar.activation(tab[:, :R], products[(b, d)], ACT.Copy, scale=scale)
             tables[(b, d)] = tab
 
         fetched = {}
 
-        def fetch(b, d, width, tag=None):
-            fetched[(b, d)] = keep.tile([P, width], F32, name="fetched", tag=tag or "fetched%d_%d" % (b, d), align_bytes=64)
-            piece = codes[d][:, : width // 16]
-            nc.scalar.activation(fetched[(b, d)][:], tables[(b, d)][:].indirect(piece), ACT.Copy)
+        def fetch(b, d, over=None, shift=0, on_vector=False):
+            fetched[(b, d)] = sbuf("fetched%d_%d" % (b, d), [P, TURNED[b]], F32, over, shift)
+            window = tables[(b, d)][:].indirect(codes[d][:, : TURNED[b] // 16])
+            if on_vector:
+                nc.vector.tensor_copy(fetched[(b, d)][:], window)
+            else:
+                nc.scalar.activation(fetched[(b, d)][:], window, ACT.Copy)
 
         sums = {}
 
-        def look_up(b, d, c0=0, c1=U, tag=None, start=None):
-            if start is None:
-                start = SHARE if b == 3 else 0
+        def look_up(b, d, c0=0, c1=U, start=0, over=None, shift=0):
             before = norm_sb[:, c0:c1] if d == 0 else sums[(b, d - 1, start)][:, c0 - start : c1 - start]
-            name = "sum%d_%d_%d" % (b, d, c0)
-            total = keep.tile([P, c1 - c0], F32, name=name, tag=tag or name, align_bytes=64)
+            total = sbuf("sum%d_%d_%d" % (b, d, c0), [P, c1 - c0], F32, over, shift)
             piece = codes[d][:, c0 // 16 : c1 // 16]
             nc.vector.tensor_tensor(total[:], tables[(b, d)][:].indirect(piece), before, ADD)
             sums[(b, d, c0)] = total
 
-        def finish(b, total, tag, c0=0, c1=U, queue=nc.sync):
-            result = keep.tile([P, c1 - c0], F32, name="result", tag=tag, align_bytes=64)
-            nc.scalar.activation(result[:], total, ACT.Sigmoid, scale=-1.0)
+        turned = {}
+
+        def add_turned(b, d, n, first, final):
+            if first:
+                turned[b] = bank("turned%d" % b, [P, TURNED[b]], n)
+            runs = TURNED[b] // P
+            for j in range(runs):
+                nc.tensor.matmul(
+                    turned[b][:, j * P : (j + 1) * P],
+                    fetched[(b, d)][:, j * P : (j + 1) * P],
+                    identity[:],
+                    start=(first and j == 0),
+                    stop=(final and j == runs - 1),
+                    is_transpose=True,
+                )
+
+        def turn_back(b, over=None):
+            turned_sb = sbuf("turned_sb%d" % b, [P, TURNED[b]], F32, over)
+            nc.scalar.activation(turned_sb[:], turned[b][:], ACT.Copy, scale=factors["c%d" % b])
+            runs = TURNED[b] // P
+            for j in range(runs):
+                nc.tensor.matmul(
+                    totals[b][:, j * P : (j + 1) * P],
+                    turned_sb[:, j * P : (j + 1) * P],
+                    identity[:],
+                    start=False,
+                    stop=(j == runs - 1),
+                    is_transpose=True,
+                )
+
+        def finish(b, total, over=None, scale=-1.0, c0=0, c1=U, shift=0, queue=nc.sync):
+            result = sbuf("result%d_%d" % (b, c0), [P, c1 - c0], F32, over, shift)
+            nc.scalar.activation(result[:], total, ACT.Sigmoid, scale=scale)
             queue.dma_start(out=out[b * P : (b + 1) * P, c0:c1], in_=result[:])
 
-        def runs(width):
-            return [min(c, width - P) for c in range(0, width, P)]
-
-        def add_turned(b, width, tag, terms):
-            starts = runs(width)
-            turned = named.tile([P, len(starts) * P], F32, name="turned", tag=tag)
-            for i, term in enumerate(terms):
-                for slot, c in enumerate(starts):
-                    nc.tensor.matmul(
-                        turned[:, slot * P : (slot + 1) * P],
-                        term[:, c : c + P],
-                        identity[:],
-                        start=(i == 0 and slot == 0),
-                        stop=(i == len(terms) - 1 and slot == len(starts) - 1),
-                        is_transpose=True,
-                    )
-            return turned
-
-        def turn_back(b, turned, width):
-            starts = runs(width)
-            turned_sb = keep.tile([P, len(starts) * P], F32, name="turned_sb%d" % b, align_bytes=64)
-            nc.scalar.copy(out=turned_sb[:], in_=turned[:])
-            total = named.tile([P, width], F32, name="total", tag="bank%d" % (7 if b == 0 else 0))
-            for slot, c in enumerate(starts):
-                nc.tensor.transpose(total[:, c : c + P], turned_sb[:, slot * P : (slot + 1) * P], identity[:])
-            return total
-
         pick(0, 0, BOOKS)
-        quantize(round_pass("grouped_pass0", raw_pass0), [(0, 0), (1, 0)])
         pick(1, 0, 3)
-        quantize(round_pass("grouped_pass1_1", raw_pass1[1]), [(1, 1)])
-        pick(1, 3, 4, "raw_pass1_1")
-        quantize(round_pass("grouped_pass1_0", raw_pass1[0]), [(0, 1)])
-
-        table(1, 0, factor[:])
+        round_pass(0, 0, nc.scalar)
+        round_pass(0, 1, nc.scalar)
+        quantize(0, 0, 1)
+        round_pass(1, 0, nc.vector)
+        round_pass(1, 1, nc.scalar)
+        quantize(0, 1, 2)
+        pick(1, 3, 4, "raw0_1")
+        quantize(1)
+        product(0, 0, 1, 3)
+        product(0, 1, 2, 4, (1, 0))
+        product(1, 0, 1, 5)
+        product(1, 1, 2, 6)
+        table(0, 0, factor[:], over="store_scales", shift=middle - WINDOW * 4)
+        product(0, 2, 4, 3)
+        product(1, 2, 4, 7)
+        table(0, 1, over="store_scales", shift=middle)
+        fetch(0, 0)
         table(1, 1)
-        table(0, 0)
-        table(0, 1)
-        grouped_batch2 = round_batch_aside("grouped_batch2", raw_batch2)
-        look_up(1, 0, tag="raw2_0")
-        fetch(0, 0, U)
-        quantize(grouped_batch2, [(2, 0), (2, 1)])
+        round_pass(2, 0, nc.vector)
+        round_pass(2, 1, nc.vector)
+        table(1, 0, on_vector=True)
+        quantize(2)
+        look_up(1, 0)
+        product(2, 0, 1, 2)
+        product(2, 1, 2, 4)
+        table(0, 2, factors["f02"])
+        table(0, 3, factors["f03"])
+        fetch(0, 1, "f02")
+        round_pass(3, 0, nc.vector, "grouped2")
         look_up(1, 1)
-        table(1, 2)
-        fetch(0, 1, U)
-        grouped_batch3 = round_batch("grouped_batch3", raw_batch3)
-        look_up(1, 2, tag="raw3_0")
-        quantize(grouped_batch3, [(3, 0), (3, 1)])
-        table(0, 2)
-        table(1, 3)
-        table(2, 0, factor20[:])
-        fetch(0, 2, U)
-        look_up(2, 0, tag="raw3_1")
+        round_pass(3, 1, nc.vector)
+        table(1, 2, factors["f12"], over="f03")
+        look_up(1, 2)
+        quantize(3)
+        product(3, 0, 2, 5)
+        table(2, 0, factors["f20"], over="f03", shift=NEXT)
+        fetch(0, 2, "f12")
+        table(1, 3, factors["f13"], over="f20")
+        table(2, 1, factors["f21"], over="f20", shift=NEXT)
+        fetch(0, 3, "f13")
+        look_up(2, 0)
         look_up(1, 3)
-        table(0, 3)
-        table(3, 0, factor30[:])
-        fetch(0, 3, U)
-        table(2, 1)
-        for d in range(1, BOOKS - 1):
-            table(2, d + 1)
-            table(3, d)
-        table(3, BOOKS - 1)
-        last = BOOKS - 1
-        for d in range(1, last):
-            look_up(2, d)
-            look_up(3, d - 1, SHARE, U)
-        turned0 = add_turned(0, U, "bank4", [norm_sb] + [fetched[(0, d)] for d in range(BOOKS)])
-        fetch(3, 0, SHARE)
-        fetch(3, 1, SHARE)
-        total0 = turn_back(0, turned0, U)
-        fetch(3, 2, SHARE)
-        fetch(3, 3, SHARE)
-        terms3 = [fetched[(3, 2)], fetched[(3, 0)], fetched[(3, 1)], norm_sb, fetched[(3, 3)]]
-        turned3 = add_turned(3, SHARE, "bank1", terms3)
-        finish(1, sums[(1, last, 0)][:], "fetched0_3")
-        finish(0, total0[:], "fetched3_1")
-        total3 = turn_back(3, turned3, SHARE)
-        look_up(2, last)
-        finish(2, sums[(2, last, 0)][:], "fetched3_3")
-        finish(3, total3[:], "result3", 0, SHARE)
-        middle = (SHARE + U) // 64 * 32
-        look_up(3, last - 1, SHARE, middle)
-        look_up(3, last - 1, middle, U)
-        result3 = keep.tile([P, U], F32, name="result3b", tag="sum2_%d_0" % last, align_bytes=64)
-        for c0, c1, start in ((SHARE, middle, SHARE), (middle, U - LAST_PIECE, middle), (U - LAST_PIECE, U, middle)):
-            look_up(3, last, c0, c1, start=start)
-            nc.scalar.activation(result3[:, c0:c1], sums[(3, last, c0)][:], ACT.Sigmoid, scale=-1.0)
+        look_up(2, 1)
+        table(3, 0, factors["f30"], over="f21")
+        product(2, 2, 4, 6)
+        product(3, 2, 4, 2)
+        for d in range(BOOKS):
+            add_turned(0, d, 3, d == 0, d == BOOKS - 1)
+        table(2, 2, factors["f22"], over="f21", shift=NEXT)
+        fetch(3, 0, "f30")
+        table(3, 1, factors["f31"], over="f22")
+        table(2, 3, factors["f23"], over="f22", shift=NEXT)
+        fetch(3, 1, "f31")
+        table(3, 2, factors["f32"], over="f23")
+        turn_back(0)
+        fetch(3, 2, "f32")
+        table(3, 3, factors["f33"], over="f23", shift=NEXT)
+        finish(1, sums[(1, 3, 0)][:], "c0", factors["s1"])
+        fetch(3, 3, "f33")
+        look_up(3, 0, SHARE, U, SHARE)
+        look_up(2, 2)
+        look_up(3, 1, SHARE, U, SHARE)
+        look_up(2, 3, 0, U // 2)
+        look_up(3, 2, SHARE, U, SHARE)
+        look_up(2, 3, U // 2, U, over="f32", shift=NEXT)
+        for d in range(BOOKS):
+            add_turned(3, d, 7, d == 0, d == BOOKS - 1)
+        finish(0, totals[0][:], "s1", factors["s0"])
+        turn_back(3)
+        finish(2, sums[(2, 3, 0)][:], "s0", c1=U // 2)
+        finish(3, totals[3][:], c1=SHARE)
+        finish(2, sums[(2, 3, U // 2)][:], "c3", c0=U // 2)
+        for c0, c1 in ((SHARE, U - LAST_PIECE), (U - LAST_PIECE, U)):
+            look_up(3, 3, c0, c1, SHARE)
             queue = nc.scalar if c1 == U else nc.sync
-            queue.dma_start(out=out[3 * P : 4 * P, c0:c1], in_=result3[:, c0:c1])
+            finish(3, sums[(3, 3, c0)][:], "sum2_3_256", c0=c0, c1=c1, shift=4 * (c0 - SHARE), queue=queue)

@@ -23,8 +23,8 @@ FP8X4 = mybir.dt.float8_e4m3fn_x4
 ACT = mybir.ActivationFunctionType
 ADD = mybir.AluOpType.add
 MULT = mybir.AluOpType.mult
-FACTORS = (("f02", -0.5), ("f03", -0.5), ("f12", -0.5), ("f20", -0.5), ("f13", -0.5), ("f21", -0.5), ("f30", -0.5), ("f22", -0.5), ("f31", -0.5), ("c0", 1.0), ("f23", -0.5), ("f32", -0.5), ("f33", -0.5), ("s1", -1.0), ("s0", -1.0), ("c3", 1.0))
-SHARE = 256
+FACTORS = (("f02", -0.5), ("f03", -0.5), ("f12", -0.5), ("f20", -0.5), ("f13", -0.5), ("f21", -0.5), ("f30", -0.5), ("f22", -0.5), ("f31", -0.5), ("c0", 1.0), ("f23", -0.5), ("f32", -0.5), ("f33", -0.5), ("s1", -1.0), ("s3", -1.0), ("c3", 1.0))
+SHARE = 128
 TURNED = {0: U, 3: SHARE}
 NEXT = WINDOW * 4
 WIDTH = {F32: 4, BF16: 2, I32: 4, U32: 4, U8: 1}
@@ -166,8 +166,8 @@ def tile_picked_yadc_prob_p_kernel(
 
         quantized = {}
 
-        def quantize(b, o0=0, o1=PASSES):
-            q_words = sbuf("q_words%d_%d" % (b, o0), [P, (o1 - o0) * P], U32)
+        def quantize(b, o0=0, o1=PASSES, over=None):
+            q_words = sbuf("q_words%d_%d" % (b, o0), [P, (o1 - o0) * P], U32, over, NEXT)
             q_scales = sbuf("q_scales%d_%d" % (b, o0), [P, (o1 - o0) * P], U8)
             tile, first = grouped[(b, o0)]
             src = tile[:, o0 - first : o1 - first].rearrange("p o w j -> p (o w j)")
@@ -296,7 +296,7 @@ def tile_picked_yadc_prob_p_kernel(
         round_pass(3, 1, nc.vector)
         table(1, 2, factors["f12"], over="f03")
         look_up(1, 2)
-        quantize(3)
+        quantize(3, over="f12")
         product(3, 0, 2, 5)
         table(2, 0, factors["f20"], over="f03", shift=NEXT)
         fetch(0, 2, "f12")
@@ -325,17 +325,17 @@ def tile_picked_yadc_prob_p_kernel(
         look_up(3, 0, SHARE, U, SHARE)
         look_up(2, 2)
         look_up(3, 1, SHARE, U, SHARE)
-        look_up(2, 3, 0, U // 2)
-        look_up(3, 2, SHARE, U, SHARE)
-        look_up(2, 3, U // 2, U, over="f32", shift=NEXT)
+        look_up(2, 3)
+        half_way = (SHARE + U) // 64 * 32
+        look_up(3, 2, SHARE, half_way, SHARE)
+        look_up(3, 2, half_way, U, SHARE)
         for d in range(BOOKS):
             add_turned(3, d, 7, d == 0, d == BOOKS - 1)
-        finish(0, totals[0][:], "s1", factors["s0"])
+        finish(0, totals[0][:], "s1")
         turn_back(3)
-        finish(2, sums[(2, 3, 0)][:], "s0", c1=U // 2)
-        finish(3, totals[3][:], c1=SHARE)
-        finish(2, sums[(2, 3, U // 2)][:], "c3", c0=U // 2)
-        for c0, c1 in ((SHARE, U - LAST_PIECE), (U - LAST_PIECE, U)):
-            look_up(3, 3, c0, c1, SHARE)
+        finish(3, totals[3][:], scale=factors["s3"], c1=SHARE)
+        finish(2, sums[(2, 3, 0)][:], "s3")
+        for c0, c1, start in ((SHARE, half_way, SHARE), (half_way, U - LAST_PIECE, half_way), (U - LAST_PIECE, U, half_way)):
+            look_up(3, 3, c0, c1, start)
             queue = nc.scalar if c1 == U else nc.sync
-            finish(3, sums[(3, 3, c0)][:], "sum2_3_256", c0=c0, c1=c1, shift=4 * (c0 - SHARE), queue=queue)
+            finish(3, sums[(3, 3, c0)][:], "sum2_3_0", c0=c0, c1=c1, shift=4 * (c0 - SHARE), queue=queue)

@@ -24,9 +24,9 @@ ACT = mybir.ActivationFunctionType
 ADD = mybir.AluOpType.add
 MULT = mybir.AluOpType.mult
 FACTORS = (("f02", -0.5), ("f03", -0.5), ("f12", -0.5), ("f20", -0.5), ("f13", -0.5), ("f21", -0.5), ("f30", -0.5), ("f22", -0.5), ("f31", -0.5), ("c0", 1.0), ("f23", -0.5), ("f32", -0.5), ("f33", -0.5), ("s1", -1.0), ("s3", -1.0), ("c3", 1.0))
-SHARE = 128
+SHARE = 224
 TURNED = {0: U, 3: SHARE}
-NEXT = WINDOW * 4
+NEXT = 2304
 WIDTH = {F32: 4, BF16: 2, I32: 4, U32: 4, U8: 1}
 
 
@@ -46,16 +46,16 @@ def tile_picked_yadc_prob_p_kernel(
                 for n in shape[1:]:
                     size = size * n
                 place[name] = place["free"]
-                place["free"] = place["free"] + (size + 63) // 64 * 64
+                place["free"] = place["free"] + (size + 255) // 256 * 256
             else:
                 place[name] = place[over] + shift
-            return keep.tile(shape, dtype, name=name, align_bytes=64, offset=place[name])
+            return keep.tile(shape, dtype, name=name, align_bytes=256 if place[name] % 256 == 0 else 64, offset=place[name])
 
         def bank(name, shape, n):
             return psum.tile(shape, F32, name=name, tag="bank%d" % n)
 
         piece_bytes = PACK * P * 4
-        store_scales = sbuf("store_scales", [P, 4 * piece_bytes + 2 * WINDOW * 4], U8)
+        store_scales = sbuf("store_scales", [P, 4 * piece_bytes + 2 * NEXT], U8)
         nc.gpsimd.memset(store_scales[:ROWS0, :T].bitcast(I32), 0)
         planes = sbuf("planes", [P, PASSES * S], U8)
         nc.gpsimd.memset(planes[:].bitcast(I32), 0)
@@ -70,9 +70,9 @@ def tile_picked_yadc_prob_p_kernel(
         make_identity(nc, identity[:], nomemset=True)
         factors = {}
         for name, value in FACTORS:
-            factors[name] = sbuf(name, [P, WINDOW + 8], F32)[:, :1]
+            factors[name] = sbuf(name, [P, NEXT // 4 + 8], F32)[:, :1]
             nc.vector.memset(factors[name], value)
-            place["free"] = place[name] + 2 * WINDOW * 4
+            place["free"] = place[name] + 2 * NEXT
 
         def load_list(name, src, n):
             offsets = lists.tile([P, n // 16], U16, name=name)
@@ -109,7 +109,7 @@ def tile_picked_yadc_prob_p_kernel(
             rows = picked_rows[ROWS0 + 8 * q : ROWS0 + 8 * q + 8, :]
             nc.sync.dma_start(out=planes[32 * q : 32 * q + 4, :].bitcast(I32), in_=rows.bitcast(I32))
 
-        middle = 4 * piece_bytes + WINDOW * 4
+        middle = 4 * piece_bytes + NEXT
         raw[(1, 1)] = load_pass("raw1_1", 1, 1, 2, "store_scales", middle - piece_bytes // 2)[:]
         for i, (b, o) in enumerate(((2, 0), (2, 1), (3, 0), (3, 1))):
             raw[(b, o)] = load_pass("raw%d_%d" % (b, o), o, b, b + 1, "store_scales", i * piece_bytes)[:]
@@ -119,23 +119,28 @@ def tile_picked_yadc_prob_p_kernel(
             nc.tensor.transpose(spread[:, j, :], norm_quads[:, j : j + 1].to_broadcast([P, P]), identity[:])
         norm_sb = sbuf("norm_sb", [P, U], F32)
         nc.scalar.copy(out=norm_sb[:].rearrange("p (c j) -> p c j", j=PACK), in_=spread[:].rearrange("p j c -> p c j"))
-        norm_turned = bank("norm_turned", [P, PACK, P], 2)
-        for j in range(PACK):
-            nc.tensor.transpose(norm_turned[:, j, :], norm_sb[:, j * P : (j + 1) * P], identity[:])
-        norm_cols = sbuf("norm_cols", [P, PACK], F32)
-        nc.scalar.copy(out=norm_cols[:], in_=norm_turned[:, :, 0])
-        totals = {}
-        for n, (b, width) in enumerate(TURNED.items()):
-            totals[b] = bank("total%d" % b, [P, width], n)
-            for j in range(width // P):
+        turned = {}
+
+        def runs(b):
+            return [min(c, TURNED[b] - P) for c in range(0, TURNED[b], P)]
+
+        def add_turned(b, term, first=False, final=False):
+            starts = runs(b)
+            for slot, c in enumerate(starts):
                 nc.tensor.matmul(
-                    totals[b][:, j * P : (j + 1) * P],
-                    norm_cols[:, j : j + 1].to_broadcast([P, P]),
+                    turned[b][:, slot * P : (slot + 1) * P],
+                    term[:, c : c + P],
                     identity[:],
-                    start=(j == 0),
-                    stop=False,
+                    start=(first and slot == 0),
+                    stop=(final and slot == len(starts) - 1),
                     is_transpose=True,
                 )
+
+        def sum_turned(b, n):
+            turned[b] = bank("turned%d" % b, [P, len(runs(b)) * P], n)
+            add_turned(b, norm_sb, first=True)
+            for d in range(BOOKS):
+                add_turned(b, fetched[(b, d)], final=(d == BOOKS - 1))
 
         picked = {}
 
@@ -148,33 +153,30 @@ def tile_picked_yadc_prob_p_kernel(
 
         grouped = {}
 
-        def round_pass(b, o, engine, over=None, alone=False):
-            if alone:
-                grouped[(b, o)] = (sbuf("grouped%d_%d" % (b, o), [P, 1, P, PACK], BF16, over), o)
-            elif (b, o) not in grouped:
-                both = sbuf("grouped%d" % b, [P, PASSES, P, PACK], BF16, over)
-                for i in range(PASSES):
-                    grouped[(b, i)] = (both, 0)
-            tile, first = grouped[(b, o)]
+        def group(name, parts, over=None):
+            tile = sbuf(name, [P, len(parts), P, PACK], BF16, over)
+            for i, part in enumerate(parts):
+                grouped[part] = (tile, i)
+
+        def round_pass(b, o, engine):
+            tile, i = grouped[(b, o)]
             src = raw[(b, o)].rearrange("p j w -> p w j")
-            if engine is nc.gpsimd:
-                nc.gpsimd.tensor_scalar(tile[:, o - first], src, 1.0, 0.0, MULT, ADD)
-            elif engine is nc.vector:
-                nc.vector.tensor_copy(out=tile[:, o - first], in_=src)
+            if engine is nc.vector:
+                nc.vector.tensor_copy(out=tile[:, i], in_=src)
             else:
-                nc.scalar.copy(out=tile[:, o - first], in_=src)
+                nc.scalar.copy(out=tile[:, i], in_=src)
 
         quantized = {}
 
-        def quantize(b, o0=0, o1=PASSES, over=None):
-            q_words = sbuf("q_words%d_%d" % (b, o0), [P, (o1 - o0) * P], U32, over, NEXT)
-            q_scales = sbuf("q_scales%d_%d" % (b, o0), [P, (o1 - o0) * P], U8)
-            tile, first = grouped[(b, o0)]
-            src = tile[:, o0 - first : o1 - first].rearrange("p o w j -> p (o w j)")
+        def quantize(parts, over=None):
+            name = "%d_%d" % parts[0]
+            q_words = sbuf("q_words" + name, [P, len(parts) * P], U32, over, NEXT)
+            q_scales = sbuf("q_scales" + name, [P, len(parts) * P], U8)
+            tile, first = grouped[parts[0]]
+            src = tile[:, first : first + len(parts)].rearrange("p o w j -> p (o w j)")
             nc.vector.quantize_mx(out=q_words[:].bitcast(FP8X4), scales=q_scales[:], in_=src)
-            for o in range(o0, o1):
-                cols = slice((o - o0) * P, (o - o0 + 1) * P)
-                quantized[(b, o)] = (q_words[:, cols], q_scales[:, cols])
+            for i, part in enumerate(parts):
+                quantized[part] = (q_words[:, i * P : (i + 1) * P], q_scales[:, i * P : (i + 1) * P])
 
         products = {}
 
@@ -226,35 +228,15 @@ def tile_picked_yadc_prob_p_kernel(
             nc.vector.tensor_tensor(total[:], tables[(b, d)][:].indirect(piece), before, ADD)
             sums[(b, d, c0)] = total
 
-        turned = {}
+        totals = {}
 
-        def add_turned(b, d, n, first, final):
-            if first:
-                turned[b] = bank("turned%d" % b, [P, TURNED[b]], n)
-            runs = TURNED[b] // P
-            for j in range(runs):
-                nc.tensor.matmul(
-                    turned[b][:, j * P : (j + 1) * P],
-                    fetched[(b, d)][:, j * P : (j + 1) * P],
-                    identity[:],
-                    start=(first and j == 0),
-                    stop=(final and j == runs - 1),
-                    is_transpose=True,
-                )
-
-        def turn_back(b, over=None):
-            turned_sb = sbuf("turned_sb%d" % b, [P, TURNED[b]], F32, over)
+        def turn_back(b, n):
+            starts = runs(b)
+            turned_sb = sbuf("turned_sb%d" % b, [P, len(starts) * P], F32)
             nc.scalar.activation(turned_sb[:], turned[b][:], ACT.Copy, scale=factors["c%d" % b])
-            runs = TURNED[b] // P
-            for j in range(runs):
-                nc.tensor.matmul(
-                    totals[b][:, j * P : (j + 1) * P],
-                    turned_sb[:, j * P : (j + 1) * P],
-                    identity[:],
-                    start=False,
-                    stop=(j == runs - 1),
-                    is_transpose=True,
-                )
+            totals[b] = bank("total%d" % b, [P, TURNED[b]], n)
+            for slot, c in enumerate(starts):
+                nc.tensor.transpose(totals[b][:, c : c + P], turned_sb[:, slot * P : (slot + 1) * P], identity[:])
 
         def finish(b, total, over=None, scale=-1.0, c0=0, c1=U, shift=0, queue=nc.sync):
             result = sbuf("result%d_%d" % (b, c0), [P, c1 - c0], F32, over, shift)
@@ -263,19 +245,21 @@ def tile_picked_yadc_prob_p_kernel(
 
         pick(0, 0, BOOKS)
         pick(1, 0, 3)
+        for b in range(3):
+            group("grouped%d" % b, [(b, 0), (b, 1)])
         round_pass(0, 0, nc.scalar)
         round_pass(0, 1, nc.scalar)
-        quantize(0, 0, 1)
+        quantize([(0, 0)])
         round_pass(1, 0, nc.vector)
         round_pass(1, 1, nc.scalar)
-        quantize(0, 1, 2)
+        quantize([(0, 1)])
         pick(1, 3, 4, "raw0_1")
-        quantize(1)
+        quantize([(1, 0), (1, 1)])
         product(0, 0, 1, 3)
         product(0, 1, 2, 4, (1, 0))
         product(1, 0, 1, 5)
         product(1, 1, 2, 6)
-        table(0, 0, factor[:], over="store_scales", shift=middle - WINDOW * 4)
+        table(0, 0, factor[:], over="store_scales", shift=middle - NEXT)
         product(0, 2, 4, 3)
         product(1, 2, 4, 7)
         table(0, 1, over="store_scales", shift=middle)
@@ -284,19 +268,20 @@ def tile_picked_yadc_prob_p_kernel(
         round_pass(2, 0, nc.vector)
         round_pass(2, 1, nc.vector)
         table(1, 0, on_vector=True)
-        quantize(2)
+        quantize([(2, 0), (2, 1)])
         look_up(1, 0)
         product(2, 0, 1, 2)
         product(2, 1, 2, 4)
         table(0, 2, factors["f02"])
         table(0, 3, factors["f03"])
         fetch(0, 1, "f02")
-        round_pass(3, 0, nc.vector, "grouped2")
+        group("grouped3", [(3, 0), (3, 1)], "grouped2")
+        round_pass(3, 0, nc.vector)
         look_up(1, 1)
         round_pass(3, 1, nc.vector)
         table(1, 2, factors["f12"], over="f03")
         look_up(1, 2)
-        quantize(3, over="f12")
+        quantize([(3, 0), (3, 1)], "f12")
         product(3, 0, 2, 5)
         table(2, 0, factors["f20"], over="f03", shift=NEXT)
         fetch(0, 2, "f12")
@@ -309,15 +294,14 @@ def tile_picked_yadc_prob_p_kernel(
         table(3, 0, factors["f30"], over="f21")
         product(2, 2, 4, 6)
         product(3, 2, 4, 2)
-        for d in range(BOOKS):
-            add_turned(0, d, 3, d == 0, d == BOOKS - 1)
+        sum_turned(0, 3)
         table(2, 2, factors["f22"], over="f21", shift=NEXT)
         fetch(3, 0, "f30")
         table(3, 1, factors["f31"], over="f22")
         table(2, 3, factors["f23"], over="f22", shift=NEXT)
         fetch(3, 1, "f31")
         table(3, 2, factors["f32"], over="f23")
-        turn_back(0)
+        turn_back(0, 0)
         fetch(3, 2, "f32")
         table(3, 3, factors["f33"], over="f23", shift=NEXT)
         finish(1, sums[(1, 3, 0)][:], "c0", factors["s1"])
@@ -329,13 +313,12 @@ def tile_picked_yadc_prob_p_kernel(
         half_way = (SHARE + U) // 64 * 32
         look_up(3, 2, SHARE, half_way, SHARE)
         look_up(3, 2, half_way, U, SHARE)
-        for d in range(BOOKS):
-            add_turned(3, d, 7, d == 0, d == BOOKS - 1)
+        sum_turned(3, 7)
         finish(0, totals[0][:], "s1")
-        turn_back(3)
+        turn_back(3, 1)
+        finish(2, sums[(2, 3, 0)][:], "c3")
         finish(3, totals[3][:], scale=factors["s3"], c1=SHARE)
-        finish(2, sums[(2, 3, 0)][:], "s3")
         for c0, c1, start in ((SHARE, half_way, SHARE), (half_way, U - LAST_PIECE, half_way), (U - LAST_PIECE, U, half_way)):
             look_up(3, 3, c0, c1, start)
             queue = nc.scalar if c1 == U else nc.sync
-            finish(3, sums[(3, 3, c0)][:], "sum2_3_0", c0=c0, c1=c1, shift=4 * (c0 - SHARE), queue=queue)
+            finish(3, sums[(3, 3, c0)][:], "s3", c0=c0, c1=c1, shift=4 * (c0 - SHARE), queue=queue)

@@ -10,7 +10,9 @@ PASSES = K // (P * PACK)
 BOOKS = S // R
 WINDOW = U + 16
 ROWS0 = 96
+HALF = U // 2
 LAST_PIECE = 64
+SHARE = 256
 FLOPS = 2 * K * V * S
 
 F32 = mybir.dt.float32
@@ -23,10 +25,8 @@ FP8X4 = mybir.dt.float8_e4m3fn_x4
 ACT = mybir.ActivationFunctionType
 ADD = mybir.AluOpType.add
 MULT = mybir.AluOpType.mult
-FACTORS = (("f02", -0.5), ("f03", -0.5), ("f12", -0.5), ("f20", -0.5), ("f13", -0.5), ("f21", -0.5), ("f30", -0.5), ("f22", -0.5), ("f31", -0.5), ("c0", 1.0), ("f23", -0.5), ("f32", -0.5), ("f33", -0.5), ("s1", -1.0), ("s3", -1.0), ("c3", 1.0))
-SHARE = 224
-TURNED = {0: U, 3: SHARE}
-NEXT = 2304
+ROOM = 2304
+FACTORS = (("one1", 1.0), ("one2", 1.0))
 WIDTH = {F32: 4, BF16: 2, I32: 4, U32: 4, U8: 1}
 
 
@@ -55,7 +55,7 @@ def tile_picked_yadc_prob_p_kernel(
             return psum.tile(shape, F32, name=name, tag="bank%d" % n)
 
         piece_bytes = PACK * P * 4
-        store_scales = sbuf("store_scales", [P, 4 * piece_bytes + 2 * NEXT], U8)
+        store_scales = sbuf("store_scales", [P, 4 * piece_bytes + 2 * ROOM], U8)
         nc.gpsimd.memset(store_scales[:ROWS0, :T].bitcast(I32), 0)
         planes = sbuf("planes", [P, PASSES * S], U8)
         nc.gpsimd.memset(planes[:].bitcast(I32), 0)
@@ -64,15 +64,14 @@ def tile_picked_yadc_prob_p_kernel(
         half = sbuf("half", [P, 1], F32)
         nc.scalar.activation(half[:], zero[:], ACT.Sigmoid)
         factor = sbuf("factor", [P, 1], F32)
-        nc.scalar.activation(factor[:], half[:], ACT.Copy, scale=-1.0)
+        nc.scalar.activation(factor[:], half[:], ACT.Copy, scale=-4.0)
         identity = sbuf("identity", [P, P], F32)
         nc.vector.memset(identity[:], 0.0)
         make_identity(nc, identity[:], nomemset=True)
         factors = {}
         for name, value in FACTORS:
-            factors[name] = sbuf(name, [P, NEXT // 4 + 8], F32)[:, :1]
+            factors[name] = sbuf(name, [P, 2 * ROOM // 4], F32)[:, :1]
             nc.vector.memset(factors[name], value)
-            place["free"] = place[name] + 2 * NEXT
 
         def load_list(name, src, n):
             offsets = lists.tile([P, n // 16], U16, name=name)
@@ -109,7 +108,7 @@ def tile_picked_yadc_prob_p_kernel(
             rows = picked_rows[ROWS0 + 8 * q : ROWS0 + 8 * q + 8, :]
             nc.sync.dma_start(out=planes[32 * q : 32 * q + 4, :].bitcast(I32), in_=rows.bitcast(I32))
 
-        middle = 4 * piece_bytes + NEXT
+        middle = 4 * piece_bytes + ROOM
         raw[(1, 1)] = load_pass("raw1_1", 1, 1, 2, "store_scales", middle - piece_bytes // 2)[:]
         for i, (b, o) in enumerate(((2, 0), (2, 1), (3, 0), (3, 1))):
             raw[(b, o)] = load_pass("raw%d_%d" % (b, o), o, b, b + 1, "store_scales", i * piece_bytes)[:]
@@ -118,29 +117,9 @@ def tile_picked_yadc_prob_p_kernel(
         for j in range(PACK):
             nc.tensor.transpose(spread[:, j, :], norm_quads[:, j : j + 1].to_broadcast([P, P]), identity[:])
         norm_sb = sbuf("norm_sb", [P, U], F32)
-        nc.scalar.copy(out=norm_sb[:].rearrange("p (c j) -> p c j", j=PACK), in_=spread[:].rearrange("p j c -> p c j"))
-        turned = {}
-
-        def runs(b):
-            return [min(c, TURNED[b] - P) for c in range(0, TURNED[b], P)]
-
-        def add_turned(b, term, first=False, final=False):
-            starts = runs(b)
-            for slot, c in enumerate(starts):
-                nc.tensor.matmul(
-                    turned[b][:, slot * P : (slot + 1) * P],
-                    term[:, c : c + P],
-                    identity[:],
-                    start=(first and slot == 0),
-                    stop=(final and slot == len(starts) - 1),
-                    is_transpose=True,
-                )
-
-        def sum_turned(b, n):
-            turned[b] = bank("turned%d" % b, [P, len(runs(b)) * P], n)
-            add_turned(b, norm_sb, first=True)
-            for d in range(BOOKS):
-                add_turned(b, fetched[(b, d)], final=(d == BOOKS - 1))
+        nc.scalar.activation(
+            norm_sb[:].rearrange("p (c j) -> p c j", j=PACK), spread[:].rearrange("p j c -> p c j"), ACT.Copy, scale=factor[:]
+        )
 
         picked = {}
 
@@ -153,30 +132,30 @@ def tile_picked_yadc_prob_p_kernel(
 
         grouped = {}
 
-        def group(name, parts, over=None):
-            tile = sbuf(name, [P, len(parts), P, PACK], BF16, over)
-            for i, part in enumerate(parts):
-                grouped[part] = (tile, i)
+        def group(b, over=None, shift=0, spare=0):
+            tile = sbuf("grouped%d" % b, [P, PASSES * P * PACK + spare // 2], BF16, over, shift)
+            grouped[b] = tile[:, : PASSES * P * PACK].rearrange("p (o w j) -> p o w j", o=PASSES, j=PACK)
 
-        def round_pass(b, o, engine):
-            tile, i = grouped[(b, o)]
-            src = raw[(b, o)].rearrange("p j w -> p w j")
+        def round_pass(b, o, engine, w0=0, w1=P):
+            src = raw[(b, o)][:, :, w0:w1].rearrange("p j w -> p w j")
+            dst = grouped[b][:, o, w0:w1, :]
             if engine is nc.vector:
-                nc.vector.tensor_copy(out=tile[:, i], in_=src)
+                nc.vector.tensor_copy(out=dst, in_=src)
+            elif engine is nc.scalar:
+                nc.scalar.copy(out=dst, in_=src)
             else:
-                nc.scalar.copy(out=tile[:, i], in_=src)
+                nc.gpsimd.tensor_scalar(dst, src, 1.0, 0.0, MULT, ADD)
 
         quantized = {}
 
-        def quantize(parts, over=None):
-            name = "%d_%d" % parts[0]
-            q_words = sbuf("q_words" + name, [P, len(parts) * P], U32, over, NEXT)
-            q_scales = sbuf("q_scales" + name, [P, len(parts) * P], U8)
-            tile, first = grouped[parts[0]]
-            src = tile[:, first : first + len(parts)].rearrange("p o w j -> p (o w j)")
-            nc.vector.quantize_mx(out=q_words[:].bitcast(FP8X4), scales=q_scales[:], in_=src)
-            for i, part in enumerate(parts):
-                quantized[part] = (q_words[:, i * P : (i + 1) * P], q_scales[:, i * P : (i + 1) * P])
+        def quantize(b, o0=0, o1=PASSES, over=None, spare=0):
+            q_words = sbuf("q_words%d_%d" % (b, o0), [P, (o1 - o0) * P + spare // 4], U32, over)
+            q_scales = sbuf("q_scales%d_%d" % (b, o0), [P, (o1 - o0) * P], U8)
+            src = grouped[b][:, o0:o1].rearrange("p o w j -> p (o w j)")
+            nc.vector.quantize_mx(out=q_words[:, : (o1 - o0) * P].bitcast(FP8X4), scales=q_scales[:], in_=src)
+            for o in range(o0, o1):
+                cols = slice((o - o0) * P, (o - o0 + 1) * P)
+                quantized[(b, o)] = (q_words[:, cols], q_scales[:, cols])
 
         products = {}
 
@@ -201,124 +180,167 @@ def tile_picked_yadc_prob_p_kernel(
 
         tables = {}
 
-        def table(b, d, scale=-0.5, on_vector=False, over=None, shift=0):
-            tab = sbuf("table%d_%d" % (b, d), [P, WINDOW], F32, over, shift)
-            if on_vector:
-                nc.vector.tensor_scalar(tab[:, :R], products[(b, d)], scale, None, MULT)
+        def table(b, d, engine, over=None, shift=0, spare=0):
+            tab = sbuf("table%d_%d" % (b, d), [P, WINDOW + spare // 4], F32, over, shift)
+            if engine is nc.vector:
+                nc.vector.tensor_copy(tab[:, :R], products[(b, d)])
             else:
-                nc.scalar.activation(tab[:, :R], products[(b, d)], ACT.Copy, scale=scale)
+                nc.scalar.copy(tab[:, :R], products[(b, d)])
             tables[(b, d)] = tab
 
-        fetched = {}
+        looked = {}
 
-        def fetch(b, d, over=None, shift=0, on_vector=False):
-            fetched[(b, d)] = sbuf("fetched%d_%d" % (b, d), [P, TURNED[b]], F32, over, shift)
-            window = tables[(b, d)][:].indirect(codes[d][:, : TURNED[b] // 16])
-            if on_vector:
-                nc.vector.tensor_copy(fetched[(b, d)][:], window)
-            else:
-                nc.scalar.activation(fetched[(b, d)][:], window, ACT.Copy)
+        def target(b, d, c0=0, c1=U, over=None, shift=0):
+            tile = sbuf("looked%d_%d_%d" % (b, d, c0), [P, c1 - c0], F32, over, shift)
+            looked.setdefault((b, d), []).append((c0, c1, tile))
 
-        sums = {}
+        def part(b, d, c0, c1):
+            if d < 0:
+                return norm_sb[:, c0:c1]
+            first, tile = [(e0, t) for e0, e1, t in looked[(b, d)] if e0 <= c0 and c1 <= e1][0]
+            return tile[:, c0 - first : c1 - first]
 
-        def look_up(b, d, c0=0, c1=U, start=0, over=None, shift=0):
-            before = norm_sb[:, c0:c1] if d == 0 else sums[(b, d - 1, start)][:, c0 - start : c1 - start]
-            total = sbuf("sum%d_%d_%d" % (b, d, c0), [P, c1 - c0], F32, over, shift)
-            piece = codes[d][:, c0 // 16 : c1 // 16]
-            nc.vector.tensor_tensor(total[:], tables[(b, d)][:].indirect(piece), before, ADD)
-            sums[(b, d, c0)] = total
+        def ensure(b, d, over, shift):
+            if (b, d) not in looked:
+                target(b, d, 0, U, over, shift)
+
+        def fetch(b, d, c0=0, c1=U, over=None, shift=0, scale=1.0):
+            ensure(b, d, over, shift)
+            window = tables[(b, d)][:].indirect(codes[d][:, c0 // 16 : c1 // 16])
+            nc.scalar.activation(part(b, d, c0, c1), window, ACT.Copy, scale=scale)
+
+        def link(b, d, c0=0, c1=U, over=None, shift=0):
+            ensure(b, d, over, shift)
+            window = tables[(b, d)][:].indirect(codes[d][:, c0 // 16 : c1 // 16])
+            nc.vector.tensor_tensor(part(b, d, c0, c1), window, part(b, d - 1, c0, c1), ADD)
+
+        turned = {}
+
+        def runs(c0, c1):
+            return [min(c, c1 - P) for c in range(c0, c1, P)]
+
+        def open_turned(b, c0, c1, n):
+            turned[(b, c0)] = bank("turned", [P, len(runs(c0, c1)) * P], n)
+            add_turned(b, -1, c0, c1)
+
+        def add_turned(b, d, c0, c1):
+            starts = runs(c0, c1)
+            for slot, c in enumerate(starts):
+                nc.tensor.matmul(
+                    turned[(b, c0)][:, slot * P : (slot + 1) * P],
+                    part(b, d, c, c + P),
+                    identity[:],
+                    start=(d < 0 and slot == 0),
+                    stop=(d == BOOKS - 1 and slot == len(starts) - 1),
+                    is_transpose=True,
+                )
 
         totals = {}
+        copies = {}
 
-        def turn_back(b, n):
-            starts = runs(b)
-            turned_sb = sbuf("turned_sb%d" % b, [P, len(starts) * P], F32)
-            nc.scalar.activation(turned_sb[:], turned[b][:], ACT.Copy, scale=factors["c%d" % b])
-            totals[b] = bank("total%d" % b, [P, TURNED[b]], n)
+        def turn_back(b, c0, c1, n, over=None):
+            starts = runs(c0, c1)
+            turned_sb = sbuf("turned_sb%d_%d" % (b, c0), [P, U], F32, over)[:, : len(starts) * P]
+            nc.scalar.copy(turned_sb, turned[(b, c0)][:])
+            copies[(b, c0)] = turned_sb
+            total = bank("total", [P, c1 - c0], n)
             for slot, c in enumerate(starts):
-                nc.tensor.transpose(totals[b][:, c : c + P], turned_sb[:, slot * P : (slot + 1) * P], identity[:])
+                nc.tensor.transpose(total[:, c - c0 : c - c0 + P], turned_sb[:, slot * P : (slot + 1) * P], identity[:])
+            totals[(b, c0)] = total
 
-        def finish(b, total, over=None, scale=-1.0, c0=0, c1=U, shift=0, queue=nc.sync):
+        results = {}
+
+        def finish(b, total, c0=0, c1=U, over=None, shift=0, scale=0.5, queue=nc.sync):
             result = sbuf("result%d_%d" % (b, c0), [P, c1 - c0], F32, over, shift)
             nc.scalar.activation(result[:], total, ACT.Sigmoid, scale=scale)
             queue.dma_start(out=out[b * P : (b + 1) * P, c0:c1], in_=result[:])
+            results[(b, c0)] = result
 
+        vec, sca = nc.vector, nc.scalar
+        open_turned(0, 0, U, 2)
         pick(0, 0, BOOKS)
         pick(1, 0, 3)
         for b in range(3):
-            group("grouped%d" % b, [(b, 0), (b, 1)])
-        round_pass(0, 0, nc.scalar)
-        round_pass(0, 1, nc.scalar)
-        quantize([(0, 0)])
-        round_pass(1, 0, nc.vector)
-        round_pass(1, 1, nc.scalar)
-        quantize([(0, 1)])
+            group(b)
+        round_pass(0, 0, sca)
+        round_pass(0, 1, sca)
+        quantize(0, 0, 1)
+        round_pass(1, 0, vec)
+        round_pass(1, 1, sca)
+        quantize(0, 1, 2)
         pick(1, 3, 4, "raw0_1")
-        quantize([(1, 0), (1, 1)])
+        quantize(1, spare=1024)
         product(0, 0, 1, 3)
         product(0, 1, 2, 4, (1, 0))
         product(1, 0, 1, 5)
         product(1, 1, 2, 6)
-        table(0, 0, factor[:], over="store_scales", shift=middle - NEXT)
+        table(0, 0, sca, "store_scales", middle - ROOM)
         product(0, 2, 4, 3)
         product(1, 2, 4, 7)
-        table(0, 1, over="store_scales", shift=middle)
+        table(0, 1, sca, "store_scales", middle)
         fetch(0, 0)
-        table(1, 1)
-        round_pass(2, 0, nc.vector)
-        round_pass(2, 1, nc.vector)
-        table(1, 0, on_vector=True)
-        quantize([(2, 0), (2, 1)])
-        look_up(1, 0)
-        product(2, 0, 1, 2)
-        product(2, 1, 2, 4)
-        table(0, 2, factors["f02"])
-        table(0, 3, factors["f03"])
-        fetch(0, 1, "f02")
-        group("grouped3", [(3, 0), (3, 1)], "grouped2")
-        round_pass(3, 0, nc.vector)
-        look_up(1, 1)
-        round_pass(3, 1, nc.vector)
-        table(1, 2, factors["f12"], over="f03")
-        look_up(1, 2)
-        quantize([(3, 0), (3, 1)], "f12")
-        product(3, 0, 2, 5)
-        table(2, 0, factors["f20"], over="f03", shift=NEXT)
-        fetch(0, 2, "f12")
-        table(1, 3, factors["f13"], over="f20")
-        table(2, 1, factors["f21"], over="f20", shift=NEXT)
-        fetch(0, 3, "f13")
-        look_up(2, 0)
-        look_up(1, 3)
-        look_up(2, 1)
-        table(3, 0, factors["f30"], over="f21")
+        round_pass(2, 0, vec)
+        round_pass(2, 1, vec)
+        table(1, 0, vec)
+        quantize(2)
+        product(2, 0, 1, 0)
+        product(2, 1, 2, 1)
+        for b, d in ((1, 1), (0, 2), (0, 3), (1, 2)):
+            table(b, d, sca)
+        fetch(0, 1, over="q_words1_0")
+        link(1, 0)
+        group(3, "grouped2")
+        round_pass(3, 0, vec)
+        link(1, 1)
+        round_pass(3, 1, vec)
+        link(1, 2)
+        quantize(3)
+        product(3, 0, 1, 5)
+        product(3, 1, 2, 4)
+        table(2, 0, sca)
+        table(1, 3, sca, "table0_1")
+        table(2, 1, sca)
+        fetch(0, 2)
         product(2, 2, 4, 6)
-        product(3, 2, 4, 2)
-        sum_turned(0, 3)
-        table(2, 2, factors["f22"], over="f21", shift=NEXT)
-        fetch(3, 0, "f30")
-        table(3, 1, factors["f31"], over="f22")
-        table(2, 3, factors["f23"], over="f22", shift=NEXT)
-        fetch(3, 1, "f31")
-        table(3, 2, factors["f32"], over="f23")
-        turn_back(0, 0)
-        fetch(3, 2, "f32")
-        table(3, 3, factors["f33"], over="f23", shift=NEXT)
-        finish(1, sums[(1, 3, 0)][:], "c0", factors["s1"])
-        fetch(3, 3, "f33")
-        look_up(3, 0, SHARE, U, SHARE)
-        look_up(2, 2)
-        look_up(3, 1, SHARE, U, SHARE)
-        look_up(2, 3)
+        product(3, 2, 4, 0)
+        fetch(0, 3, over="grouped3")
+        for d in range(BOOKS):
+            add_turned(0, d, 0, U)
+        link(2, 0)
+        link(1, 3)
+        link(2, 1)
+        for d in range(2):
+            target(3, d, 0, SHARE)
+        table(3, 0, sca)
+        table(2, 2, sca, "table0_2")
+        fetch(3, 0, 0, SHARE)
+        table(3, 1, sca)
+        table(2, 3, sca, "table0_3")
+        fetch(3, 1, 0, SHARE, scale=factors["one1"])
+        table(3, 2, sca)
+        turn_back(0, 0, U, 1)
+        target(3, 2, 0, SHARE)
+        target(3, 3, 0, SHARE)
+        place["free"] = place["free"] + 1024
+        fetch(3, 2, 0, SHARE, scale=factors["one2"])
+        table(3, 3, sca)
+        finish(1, part(1, 3, 0, U), over="one1")
+        fetch(3, 3, 0, SHARE)
+        open_turned(3, 0, SHARE, 3)
+        for d in range(BOOKS):
+            add_turned(3, d, 0, SHARE)
+            target(3, d, SHARE, U)
         half_way = (SHARE + U) // 64 * 32
-        look_up(3, 2, SHARE, half_way, SHARE)
-        look_up(3, 2, half_way, U, SHARE)
-        sum_turned(3, 7)
-        finish(0, totals[0][:], "s1")
-        turn_back(3, 1)
-        finish(2, sums[(2, 3, 0)][:], "c3")
-        finish(3, totals[3][:], scale=factors["s3"], c1=SHARE)
-        for c0, c1, start in ((SHARE, half_way, SHARE), (half_way, U - LAST_PIECE, half_way), (U - LAST_PIECE, U, half_way)):
-            look_up(3, 3, c0, c1, start)
-            queue = nc.scalar if c1 == U else nc.sync
-            finish(3, sums[(3, 3, c0)][:], "s3", c0=c0, c1=c1, shift=4 * (c0 - SHARE), queue=queue)
+        link(3, 0, SHARE, U)
+        link(2, 2)
+        link(3, 1, SHARE, U)
+        link(2, 3)
+        link(3, 2, SHARE, half_way)
+        link(3, 2, half_way, U)
+        finish(0, totals[(0, 0)][:], over="one2")
+        turn_back(3, 0, SHARE, 7)
+        finish(2, part(2, 3, 0, U), over="looked3_3_0")
+        finish(3, totals[(3, 0)][:], 0, SHARE)
+        for c0, c1 in ((SHARE, half_way), (half_way, U - LAST_PIECE), (U - LAST_PIECE, U)):
+            link(3, 3, c0, c1)
+            finish(3, part(3, 3, c0, c1), c0, c1, "turned_sb3_0", 4 * (c0 - SHARE))

from contextlib import ExitStack

import concourse.mybir as mybir
from concourse.masks import make_identity

K, T, S, V, U, R = 1024, 2048, 1024, 512, 512, 256
P = 128
PACK = 4
PASSES = K // (P * PACK)
BOOKS = S // R
WINDOW = U + 16
ROWS0 = 96
HALF = U // 2
LAST_PIECE = 64
SHARE = 256
FLOPS = 2 * K * V * S

F32 = mybir.dt.float32
BF16 = mybir.dt.bfloat16
I32 = mybir.dt.int32
U32 = mybir.dt.uint32
U16 = mybir.dt.uint16
U8 = mybir.dt.uint8
FP8X4 = mybir.dt.float8_e4m3fn_x4
ACT = mybir.ActivationFunctionType
ADD = mybir.AluOpType.add
MULT = mybir.AluOpType.mult
ROOM = 2304
FACTORS = (("one1", 1.0), ("one2", 1.0))
WIDTH = {F32: 4, BF16: 2, I32: 4, U32: 4, U8: 1}


def tile_picked_yadc_prob_p_kernel(
    tc, x_words, x_scales, hT, norm, offs, code1, code2, code3, code4, out
):
    nc = tc.nc
    with ExitStack() as ctx:
        lists = ctx.enter_context(tc.tile_pool(name="lists", bufs=1))
        keep = ctx.enter_context(tc.tile_pool(name="keep", bufs=1))
        psum = ctx.enter_context(tc.psum_pool(name="psum", bufs=1))
        place = {"free": 0}

        def sbuf(name, shape, dtype, over=None, shift=0):
            if over is None:
                size = WIDTH[dtype]
                for n in shape[1:]:
                    size = size * n
                place[name] = place["free"]
                place["free"] = place["free"] + (size + 255) // 256 * 256
            else:
                place[name] = place[over] + shift
            return keep.tile(shape, dtype, name=name, align_bytes=256 if place[name] % 256 == 0 else 64, offset=place[name])

        def bank(name, shape, n):
            return psum.tile(shape, F32, name=name, tag="bank%d" % n)

        piece_bytes = PACK * P * 4
        store_scales = sbuf("store_scales", [P, 4 * piece_bytes + 2 * ROOM], U8)
        nc.gpsimd.memset(store_scales[:ROWS0, :T].bitcast(I32), 0)
        planes = sbuf("planes", [P, PASSES * S], U8)
        nc.gpsimd.memset(planes[:].bitcast(I32), 0)
        zero = sbuf("zero", [P, 1], F32)
        nc.vector.memset(zero[:], 0.0)
        half = sbuf("half", [P, 1], F32)
        nc.scalar.activation(half[:], zero[:], ACT.Sigmoid)
        factor = sbuf("factor", [P, 1], F32)
        nc.scalar.activation(factor[:], half[:], ACT.Copy, scale=-4.0)
        identity = sbuf("identity", [P, P], F32)
        nc.vector.memset(identity[:], 0.0)
        make_identity(nc, identity[:], nomemset=True)
        factors = {}
        for name, value in FACTORS:
            factors[name] = sbuf(name, [P, 2 * ROOM // 4], F32)[:, :1]
            nc.vector.memset(factors[name], value)

        def load_list(name, src, n):
            offsets = lists.tile([P, n // 16], U16, name=name)
            nc.sync.dma_start(offsets[:], src)
            return offsets

        def load_words(o):
            words = sbuf("store_words%d" % o, [P, T], I32)
            nc.sync.dma_start(out=words[:], in_=x_words[o].rearrange("p n t -> p (n t)").bitcast(I32))
            return words

        def load_pass(name, o, b0, b1, over=None, shift=0):
            raw = sbuf(name, [P, PACK, (b1 - b0) * P], F32, over, shift)
            rows = hT[o * P * PACK : (o + 1) * P * PACK, b0 * P : b1 * P]
            nc.sync.dma_start(out=raw[:], in_=rows.rearrange("(p j) w -> p j w", j=PACK))
            return raw

        nc.sync.dma_start(
            out=store_scales[ROWS0:, :T].bitcast(I32), in_=x_scales.rearrange("o r c -> r o c").bitcast(I32)
        )
        offs_sb = load_list("offs_sb", offs, S)
        store_words = [load_words(0)]
        norm_quads = sbuf("norm_quads", [P, PACK], F32)
        nc.sync.dma_start(out=norm_quads[:], in_=norm[0].rearrange("(p j) -> p j", j=PACK))
        codes = [load_list("code%d_sb" % (d + 1), src, U) for d, src in enumerate((code1, code2, code3, code4))]
        store_words.append(load_words(1))
        early0 = load_pass("early0", 0, 0, 2)
        raw = {(b, 0): early0[:, :, b * P : (b + 1) * P] for b in range(2)}
        raw[(0, 1)] = load_pass("raw0_1", 1, 0, 1)[:]

        picked_rows = sbuf("picked_rows", [P, S], U8)
        nc.vector.tensor_copy(picked_rows[:], store_scales[:, :T].indirect(offs_sb[:]))
        for q in range(4):
            rows = picked_rows[ROWS0 + 8 * q : ROWS0 + 8 * q + 8, :]
            nc.sync.dma_start(out=planes[32 * q : 32 * q + 4, :].bitcast(I32), in_=rows.bitcast(I32))

        middle = 4 * piece_bytes + ROOM
        raw[(1, 1)] = load_pass("raw1_1", 1, 1, 2, "store_scales", middle - piece_bytes // 2)[:]
        for i, (b, o) in enumerate(((2, 0), (2, 1), (3, 0), (3, 1))):
            raw[(b, o)] = load_pass("raw%d_%d" % (b, o), o, b, b + 1, "store_scales", i * piece_bytes)[:]

        spread = bank("spread", [P, PACK, P], 2)
        for j in range(PACK):
            nc.tensor.transpose(spread[:, j, :], norm_quads[:, j : j + 1].to_broadcast([P, P]), identity[:])
        norm_sb = sbuf("norm_sb", [P, U], F32)
        nc.scalar.activation(
            norm_sb[:].rearrange("p (c j) -> p c j", j=PACK), spread[:].rearrange("p j c -> p c j"), ACT.Copy, scale=factor[:]
        )

        picked = {}

        def pick(o, d0, d1, over=None):
            words = sbuf("picked%d_%d" % (o, d0), [P, (d1 - d0) * R], U32, over)
            piece = offs_sb[:, d0 * R // 16 : d1 * R // 16]
            nc.vector.tensor_copy(words[:], store_words[o][:].bitcast(U32).indirect(piece))
            for d in range(d0, d1):
                picked[(o, d)] = (words, d0)

        grouped = {}

        def group(b, over=None, shift=0, spare=0):
            tile = sbuf("grouped%d" % b, [P, PASSES * P * PACK + spare // 2], BF16, over, shift)
            grouped[b] = tile[:, : PASSES * P * PACK].rearrange("p (o w j) -> p o w j", o=PASSES, j=PACK)

        def round_pass(b, o, engine, w0=0, w1=P):
            src = raw[(b, o)][:, :, w0:w1].rearrange("p j w -> p w j")
            dst = grouped[b][:, o, w0:w1, :]
            if engine is nc.vector:
                nc.vector.tensor_copy(out=dst, in_=src)
            elif engine is nc.scalar:
                nc.scalar.copy(out=dst, in_=src)
            else:
                nc.gpsimd.tensor_scalar(dst, src, 1.0, 0.0, MULT, ADD)

        quantized = {}

        def quantize(b, o0=0, o1=PASSES, over=None, spare=0):
            q_words = sbuf("q_words%d_%d" % (b, o0), [P, (o1 - o0) * P + spare // 4], U32, over)
            q_scales = sbuf("q_scales%d_%d" % (b, o0), [P, (o1 - o0) * P], U8)
            src = grouped[b][:, o0:o1].rearrange("p o w j -> p (o w j)")
            nc.vector.quantize_mx(out=q_words[:, : (o1 - o0) * P].bitcast(FP8X4), scales=q_scales[:], in_=src)
            for o in range(o0, o1):
                cols = slice((o - o0) * P, (o - o0 + 1) * P)
                quantized[(b, o)] = (q_words[:, cols], q_scales[:, cols])

        products = {}

        def product(b, d0, d1, n, order=(0, 1)):
            acc = bank("acc", [P, (d1 - d0) * R], n)
            together = all(picked[(o, d0)][1] == picked[(o, d1 - 1)][1] for o in range(PASSES))
            for e0, e1 in [(d0, d1)] if together else [(d, d + 1) for d in range(d0, d1)]:
                for o in order:
                    words, first = picked[(o, e0)]
                    q_words, q_scales = quantized[(b, o)]
                    nc.tensor.matmul_mx(
                        out=acc[:, (e0 - d0) * R : (e1 - d0) * R],
                        lhsT=q_words.bitcast(FP8X4),
                        lhsT_scale=q_scales,
                        rhs=words[:, (e0 - first) * R : (e1 - first) * R].bitcast(FP8X4),
                        rhs_scale=planes[:, o * S + e0 * R : o * S + e1 * R],
                        start=(o == order[0]),
                        stop=(o == order[-1]),
                    )
            for d in range(d0, d1):
                products[(b, d)] = acc[:, (d - d0) * R : (d - d0 + 1) * R]

        tables = {}

        def table(b, d, engine, over=None, shift=0, spare=0):
            tab = sbuf("table%d_%d" % (b, d), [P, WINDOW + spare // 4], F32, over, shift)
            if engine is nc.vector:
                nc.vector.tensor_copy(tab[:, :R], products[(b, d)])
            else:
                nc.scalar.copy(tab[:, :R], products[(b, d)])
            tables[(b, d)] = tab

        looked = {}

        def target(b, d, c0=0, c1=U, over=None, shift=0):
            tile = sbuf("looked%d_%d_%d" % (b, d, c0), [P, c1 - c0], F32, over, shift)
            looked.setdefault((b, d), []).append((c0, c1, tile))

        def part(b, d, c0, c1):
            if d < 0:
                return norm_sb[:, c0:c1]
            first, tile = [(e0, t) for e0, e1, t in looked[(b, d)] if e0 <= c0 and c1 <= e1][0]
            return tile[:, c0 - first : c1 - first]

        def ensure(b, d, over, shift):
            if (b, d) not in looked:
                target(b, d, 0, U, over, shift)

        def fetch(b, d, c0=0, c1=U, over=None, shift=0, scale=1.0):
            ensure(b, d, over, shift)
            window = tables[(b, d)][:].indirect(codes[d][:, c0 // 16 : c1 // 16])
            nc.scalar.activation(part(b, d, c0, c1), window, ACT.Copy, scale=scale)

        def link(b, d, c0=0, c1=U, over=None, shift=0):
            ensure(b, d, over, shift)
            window = tables[(b, d)][:].indirect(codes[d][:, c0 // 16 : c1 // 16])
            nc.vector.tensor_tensor(part(b, d, c0, c1), window, part(b, d - 1, c0, c1), ADD)

        turned = {}

        def runs(c0, c1):
            return [min(c, c1 - P) for c in range(c0, c1, P)]

        def open_turned(b, c0, c1, n):
            turned[(b, c0)] = bank("turned", [P, len(runs(c0, c1)) * P], n)
            add_turned(b, -1, c0, c1)

        def add_turned(b, d, c0, c1):
            starts = runs(c0, c1)
            for slot, c in enumerate(starts):
                nc.tensor.matmul(
                    turned[(b, c0)][:, slot * P : (slot + 1) * P],
                    part(b, d, c, c + P),
                    identity[:],
                    start=(d < 0 and slot == 0),
                    stop=(d == BOOKS - 1 and slot == len(starts) - 1),
                    is_transpose=True,
                )

        totals = {}
        copies = {}

        def turn_back(b, c0, c1, n, over=None):
            starts = runs(c0, c1)
            turned_sb = sbuf("turned_sb%d_%d" % (b, c0), [P, U], F32, over)[:, : len(starts) * P]
            nc.scalar.copy(turned_sb, turned[(b, c0)][:])
            copies[(b, c0)] = turned_sb
            total = bank("total", [P, c1 - c0], n)
            for slot, c in enumerate(starts):
                nc.tensor.transpose(total[:, c - c0 : c - c0 + P], turned_sb[:, slot * P : (slot + 1) * P], identity[:])
            totals[(b, c0)] = total

        results = {}

        def finish(b, total, c0=0, c1=U, over=None, shift=0, scale=0.5, queue=nc.sync):
            result = sbuf("result%d_%d" % (b, c0), [P, c1 - c0], F32, over, shift)
            nc.scalar.activation(result[:], total, ACT.Sigmoid, scale=scale)
            queue.dma_start(out=out[b * P : (b + 1) * P, c0:c1], in_=result[:])
            results[(b, c0)] = result

        vec, sca = nc.vector, nc.scalar
        open_turned(0, 0, U, 2)
        pick(0, 0, BOOKS)
        pick(1, 0, 3)
        for b in range(3):
            group(b)
        round_pass(0, 0, sca)
        round_pass(0, 1, sca)
        quantize(0, 0, 1)
        round_pass(1, 0, vec)
        round_pass(1, 1, sca)
        quantize(0, 1, 2)
        pick(1, 3, 4, "raw0_1")
        quantize(1, spare=1024)
        product(0, 0, 1, 3)
        product(0, 1, 2, 4, (1, 0))
        product(1, 0, 1, 5)
        product(1, 1, 2, 6)
        table(0, 0, sca, "store_scales", middle - ROOM)
        product(0, 2, 4, 3)
        product(1, 2, 4, 7)
        table(0, 1, sca, "store_scales", middle)
        fetch(0, 0)
        round_pass(2, 0, vec)
        round_pass(2, 1, vec)
        table(1, 0, vec)
        quantize(2)
        product(2, 0, 1, 0)
        product(2, 1, 2, 1)
        for b, d in ((1, 1), (0, 2), (0, 3), (1, 2)):
            table(b, d, sca)
        fetch(0, 1, over="q_words1_0")
        link(1, 0)
        group(3, "grouped2")
        round_pass(3, 0, vec)
        link(1, 1)
        round_pass(3, 1, vec)
        link(1, 2)
        quantize(3)
        product(3, 0, 1, 5)
        product(3, 1, 2, 4)
        table(2, 0, sca)
        table(1, 3, sca, "table0_1")
        table(2, 1, sca)
        fetch(0, 2)
        product(2, 2, 4, 6)
        product(3, 2, 4, 0)
        fetch(0, 3, over="grouped3")
        for d in range(BOOKS):
            add_turned(0, d, 0, U)
        link(2, 0)
        link(1, 3)
        link(2, 1)
        for d in range(2):
            target(3, d, 0, SHARE)
        table(3, 0, sca)
        table(2, 2, sca, "table0_2")
        fetch(3, 0, 0, SHARE)
        table(3, 1, sca)
        table(2, 3, sca, "table0_3")
        fetch(3, 1, 0, SHARE, scale=factors["one1"])
        table(3, 2, sca)
        turn_back(0, 0, U, 1)
        target(3, 2, 0, SHARE)
        target(3, 3, 0, SHARE)
        place["free"] = place["free"] + 1024
        fetch(3, 2, 0, SHARE, scale=factors["one2"])
        table(3, 3, sca)
        finish(1, part(1, 3, 0, U), over="one1")
        fetch(3, 3, 0, SHARE)
        open_turned(3, 0, SHARE, 3)
        for d in range(BOOKS):
            add_turned(3, d, 0, SHARE)
            target(3, d, SHARE, U)
        half_way = (SHARE + U) // 64 * 32
        link(3, 0, SHARE, U)
        link(2, 2)
        link(3, 1, SHARE, U)
        link(2, 3)
        link(3, 2, SHARE, half_way)
        link(3, 2, half_way, U)
        finish(0, totals[(0, 0)][:], over="one2")
        turn_back(3, 0, SHARE, 7)
        finish(2, part(2, 3, 0, U), over="looked3_3_0")
        finish(3, totals[(3, 0)][:], 0, SHARE)
        for c0, c1 in ((SHARE, half_way), (half_way, U - LAST_PIECE), (U - LAST_PIECE, U)):
            link(3, 3, c0, c1)
            finish(3, part(3, 3, c0, c1), c0, c1, "turned_sb3_0", 4 * (c0 - SHARE))
